import numpy as np, ml_dtypes
CORES = [35,38,43,46]
N = 4
BF = ml_dtypes.bfloat16
def gentries(a):
    return np.ascontiguousarray(a.reshape(8, 16, -1).transpose(0, 2, 1)).reshape(8, -1)
def gtable(e):
    e = np.asarray(e); return np.ascontiguousarray(e.reshape(8, -1, 16).transpose(0, 2, 1)).reshape(128, -1).astype(np.int32)
V, L, RO, LAM, MU, STEP = 2048, 4, 2, 8, 4, 4
def perms(rng):
    return np.argsort(rng.random((N, 8, V)), axis=-1)
def parts(rng):
    sh = (N, 8, 16, V)
    return rng.integers(0, 32, sh, dtype=np.int32), rng.integers(2, 62, sh, dtype=np.int32), rng.integers(0, 100, sh, dtype=np.int32), perms(rng), perms(rng)
def pick(t, ix):
    return np.stack([np.stack([np.take(t[q, g], ix[q, g], axis=-1) for g in range(8)]) for q in range(N)])
def edges(h, a, b):
    hp = np.roll(h, 1, axis=0)
    return np.abs(h - pick(hp, a)), np.abs(h - pick(hp, b))
def forest(f, p, a, b, da, db):
    won = []
    for t in range(L):
        if t: p = np.roll(p, 1, axis=0)
        c0 = pick(p, a) + da; c1 = pick(p, b) + db
        w = np.add.reduce(c1 < c0, axis=2, dtype=np.int32) >= 9
        p = np.where(w[:, :, None, :], c1, c0) + f
        won.append(w)
    return p, won
def entered(wrong, won, a, b):
    m = wrong; u = np.zeros_like(m)
    for t in range(L - 1, 0, -1):
        x = np.zeros_like(m); y = np.zeros_like(m)
        np.put_along_axis(x, a, m & ~won[t], 2); np.put_along_axis(y, b, m & won[t], 2)
        m = np.roll(x | y, -1, axis=0); u = u | m
    return u
def bar(h, e, p, a, b):
    da, db = edges(h, a, b); c, won = forest(e, p, a, b, da, db)
    return np.ascontiguousarray(np.sort(c, axis=2)[:, :, 7, :]).astype(np.int64)
def pack(h, e, p, z, a, b):
    w = lambda x: np.ascontiguousarray(x.reshape(N, 128, V)).astype(np.float32).astype(BF)
    return {"hf": w(h), "toll": w(e), "p0": w(p), "lim": np.clip(z, 0, 1023).astype(np.int32), "sa": np.stack([gtable(x) for x in a]), "sb": np.stack([gtable(x) for x in b])}
def near(rng, q, share, under, over):
    return np.where(rng.random(q.shape) < share, q - 1 - rng.integers(0, under, q.shape), q + rng.integers(0, over, q.shape))
def classes(rng, to):
    x = np.zeros(V, np.int64)
    for c in range(8): x[c::8] = 8 * rng.permutation(V >> 3) + to[c]
    return x
def setup_inputs(rng):
    h, e, p, a, b = parts(rng)
    return pack(h, e, p, near(rng, bar(h, e, p, a, b), 0.2, 12, 24), a, b)
def setup_inputs_spread(rng):
    h, e, p, a, b = parts(rng); col = (N, 8, 1, V)
    h = np.minimum(np.exp2(2 + 3 * rng.random(col)) * rng.random(h.shape), 31).astype(np.int32)
    e = np.minimum(64 * rng.random(col) ** 2 * rng.random(e.shape) + rng.integers(0, 8, e.shape), 63).astype(np.int32)
    p = np.minimum(np.exp2(3 + 5 * rng.random(col)) * rng.random(p.shape), 255).astype(np.int32)
    h[:, :, :, ::5] = rng.integers(0, 32, h[:, :, :, ::5].shape); e[:, :, :, ::3] = rng.integers(0, 64, e[:, :, :, ::3].shape); p[:, :, :, ::7] = rng.integers(0, 256, p[:, :, :, ::7].shape)
    return pack(h, e, p, near(rng, bar(h, e, p, a, b), 0.3, 60, 90), a, b)
def setup_inputs_ends(rng):
    sh = (N, 8, 16, V)
    h = 31 * rng.integers(0, 2, sh, dtype=np.int32); e = 63 * rng.integers(0, 2, sh, dtype=np.int32); p = 255 * rng.integers(0, 2, sh, dtype=np.int32)
    z = 1023 * (rng.random((N, 8, V)) >= 0.25).astype(np.int64)
    a = np.zeros((N, 8, V), np.int64); b = np.zeros((N, 8, V), np.int64)
    hi = np.concatenate([np.arange(16), np.arange(V - 16, V)]); lo = np.arange(16, 48); mid = np.arange(48, V - 16)
    for q in range(N):
        for g in range(8):
            for s in (a, b):
                for x in (hi, lo, mid): s[q, g, x] = x[rng.permutation(len(x))]
            if g % 2: a[q, g, hi] = hi[::-1]; b[q, g, hi] = hi
            if g == 5: a[q, g, lo] = lo[::-1]; b[q, g, lo] = lo
    h[:, :, :, hi] = 31 * (np.arange(N) % 2)[:, None, None, None]; e[:, :, :, hi] = 63; p[:, :, :, hi] = 255
    h[:, :, :, lo] = 0; e[:, :, :, lo] = 0; p[:, :, :, lo] = 0
    z[:, :, V - 1] = 0
    p[:, 5, :, lo] = 1
    z[:, 5, lo] = 1023; z[:, 7, hi[1:31]] = 1023
    for i in range(16):
        x, y = rng.integers(0, 2, 2)
        z[i % N, 5, lo[31 - i if x else i]] = 0
        if i: z[i % N, 7, hi[31 - i if y else i]] = 254 + 94 * L
    return pack(h, e, p, z, a, b)
def setup_inputs_corners(rng):
    h, e, p, a, b = parts(rng); w = rng.permutation(8); k = np.arange(V)
    b[:, w[2]] = a[:, w[2]]
    b[:, w[3]] = a[:, w[3]] ^ 1; e[:, w[3]] = 63 * (k % 2)
    a[:, w[4]] = k; b[:, w[4]] = V - 1 - k
    p[:, w[5]] = rng.integers(0, 256, (N, 1, 1)); e[:, w[5]] = rng.integers(0, 64, (N, 1, 1)); h[:, w[5]] = rng.integers(0, 32, (N, 16, 1))
    lev = rng.integers(0, 2, (N, 1, V)); cut = 7 + rng.integers(0, 3, (N, 1, V))
    p[:, w[6]] = np.where(np.arange(16)[None, :, None] < cut, 10 * lev, 10 - 10 * lev); e[:, w[6]] = 20; h[:, w[6]] = rng.integers(0, 32, (N, 16, 1))
    e[:, w[7]] = 63 * rng.integers(0, 2, (N, 16, V))
    q = bar(h, e, p, a, b); z = q + rng.integers(-1, 2, q.shape)
    odd = (np.arange(N) % 2)[:, None]
    z[:, w[0]] = np.where(odd == 0, 1023, 0); z[:, w[1]] = np.where(odd == 0, 0, 1023)
    return pack(h, e, p, z, a, b)
def setup_inputs_calm(rng):
    h, e, p, a, b = parts(rng); sh = h.shape
    low = (rng.random(sh) < 0.25).astype(np.int64); low[:, 6, ::2] = rng.integers(0, 5, low[:, 6, ::2].shape)
    i = rng.permutation(16)
    for j, (x, y) in enumerate(((3, 0), (5, 5), (5, 4))): low[::2, 3, i[j]] = x; low[1::2, 3, i[j]] = y
    h = np.where((np.arange(N) % 2 == 1)[:, None, None, None], 31 - low, low).astype(np.int32); p = rng.integers(0, 4, sh, dtype=np.int32)
    base = 60 * ((np.arange(N)[:, None] + np.arange(8)[None, :]) % 2)
    base[:, 5] = 60; base[:, 7] = 60; p[:, 5] += 252; p[:, 7] += 128
    e = (base[:, :, None, None] + rng.integers(0, 4, sh)).astype(np.int32)
    z = bar(h, e, p, a, b)
    for q in range(N):
        for g in range(4): z[q, g, rng.permutation(V)[:g]] -= 1
    z[:, 4:] -= (rng.random((N, 4, V)) < 0.15)
    return pack(h, e, p, z, a, b)
def setup_inputs_crowd(rng):
    h, e, p, a, b = parts(rng); k = np.arange(V); first = k[(k & 2) == 0]; k8 = k & 7
    gap = np.array([3, LAM + MU, LAM + MU + 1, 30, 60, 60, 60, 60])[None, :, None, None]; odd = (k % 2)[None, None, None, :]
    h[:, :4] = rng.integers(0, 32, (N, 4, 16, 1)); h[:, 4:] = rng.integers(0, 11, (N, 4, 16, V))
    e = (rng.integers(0, 4, (N, 8, 16, 1)) + gap * odd).astype(np.int32); p = (rng.integers(20, 100, (N, 8, 16, 1)) + gap * odd).astype(np.int32)
    z = np.zeros((N, 8, V), np.int64)
    for q in range(N):
        for g in range(6):
            c = 2 * rng.permutation(V // 2); o = rng.integers(0, 2, V // 2)
            a[q, g, first] = c + o; a[q, g, first + 2] = c + 1 - o
            if g % 2:
                i = 2 * int(rng.integers(0, V // 2)); x = e[q, g]; x[:, [i, i + 1]] = x[:, [i + 1, i]]
                z[q, g, int(rng.integers(0, V))] = 1023
    b[:, :6] = a[:, :6] ^ 1
    step = np.array([0, 0, 0, 25, 25, 25, 25, 55])[k8]
    h[:, 6] = rng.integers(0, 30, (1, 16, 1)) + 2 * (k8 == 4)
    e[:, 6] = rng.integers(0, 4, (N, 16, 1)) + step; p[:, 6] = rng.integers(20, 100, (N, 16, 1)) + step
    h[:, 7] = rng.integers(0, 28, (1, 16, 1)) + (k8 >> 1)
    e[:, 7] = rng.integers(10, 51, (N, 16, 1)); p[:, 7] = rng.integers(20, 100, (N, 16, 1))
    h[:, 4] = rng.integers(0, 11, (N, 16, 1)); p[:, 4] = rng.integers(20, 100, (N, 16, 1))
    e[:, 4] = rng.integers(20, 41, (N, 16, 1)) + np.where(k8 < 6, k8 & 1, 0)
    for q in range(N):
        a[q, 4] = classes(rng, (2, 4, 6, 1, 3, 5, 0, 7)); b[q, 4] = classes(rng, (3, 5, 1, 7, 0, 2, 4, 6))
        a[q, 6] = classes(rng, (2, 0, 4, 1, 6, 7, 5, 3)); b[q, 6] = classes(rng, (7, 3, 0, 5, 1, 2, 6, 4))
        a[q, 7] = classes(rng, (0, 1, 2, 3, 4, 5, 6, 7)); b[q, 7] = classes(rng, (2, 3, 4, 5, 6, 7, 0, 1))
    z[:, 4] = np.where(k8 < 6, bar(h, e, p, a, b)[:, 4] - 1, 1023)
    return pack(h, e, p, z, a, b)
def check_ranges(d):
    bad = []
    for k, lo, hi in (("hf", 0, 31), ("toll", 0, 63), ("p0", 0, 255), ("lim", 0, 1023), ("sa", 0, V - 1), ("sb", 0, V - 1)):
        x = np.asarray(d[k]).astype(np.float64)
        if not np.all((x >= lo) & (x <= hi) & (x == np.floor(x))): bad.append("range of " + k)
    for k in ("sa", "sb"):
        if any(np.any(np.sort(gentries(np.asarray(d[k])[q]), axis=1) != np.arange(V)) for q in range(N)): bad.append("numbers of " + k + " not each once")
    return bad
def reference(hf, toll, p0, lim, sa, sb):
    whole_ = lambda x: x.astype(np.float32).astype(np.int32).reshape(N, 8, 16, V)
    h = whole_(hf); e = whole_(toll); p = whole_(p0); z = lim.astype(np.int32)[:, :, None, :]
    a = np.stack([gentries(x) for x in sa]).astype(np.int64); b = np.stack([gentries(x) for x in sb]).astype(np.int64)
    da, db = edges(h, a, b); tab = np.exp(-0.125 * np.arange(32)); gain = np.zeros((N, 8, 16, V))
    ident = np.broadcast_to(np.arange(V), (N, 8, V))
    for rnd in range(RO):
        last, w1 = forest(e, p, a, b, da, db)
        wrong = np.add.reduce(last > z, axis=2, dtype=np.int32) >= 9
        m1 = entered(wrong, w1, a, b).astype(np.int32)
        f = e + (LAM * m1 + MU * np.roll(m1, -1, axis=1))[:, :, None, :]
        unused, w2 = forest(f, p, a, b, da, db)
        m2 = entered(wrong, w2, a, b).astype(np.int32)
        na = ident; nb = ident; fa = h; fb = h; acc = np.zeros((N, 8, 16, V))
        for t in range(L - 1, 0, -1):
            na = np.roll(pick(np.where(w1[t], b, a), na), -1, axis=0); nb = np.roll(pick(np.where(w2[t], b, a), nb), -1, axis=0)
            oa = np.roll(fa, -1, axis=0); ob = np.roll(fb, -1, axis=0)
            fa = pick(h, na); fb = pick(h, nb)
            acc = np.roll(acc, -1, axis=0) + tab[np.abs(fa - ob)] + 0.5 * tab[np.abs(fb - oa)]
        gain = gain + acc
        e = np.clip(e + STEP * (m1 - m2)[:, :, None, :], 0, 63)
    return {"gain": gain.reshape(N, 128, V).astype(np.float32), "tollout": e.reshape(N, 128, V).astype(np.float32)}

def check_inputs(d):
    bad = list(check_ranges(d))
    if not bad:
        for name, y in reference(**d).items():
            for q in range(N):
                v = np.abs(np.asarray(y[q], np.float64)); s = np.sqrt(np.mean(v * v))
                if v.max() > 4 * s or s < 2.0 ** -4: bad.append('%s of rank %d is uneven or too small' % (name, q))
    return bad

@@ -1,0 +1,842 @@
+import math
+from concourse.bass import DstId, RemoteDMATransfer
+from concourse.mybir import AluOpType, ActivationFunctionType
+
+V = 2048
+BIG = 8192.0
+CUT = 8.5 * BIG
+HI = 6144.0
+BF, F32, F16, I32, U16 = "bfloat16", "float32", "float16", "int32", "uint16"
+
+
+def _sb(n, d):
+    return ("sbuf", [128, n], d)
+
+
+SCRATCH = {
+    "W0": _sb(4096, F32), "W1": _sb(4096, F32), "G0": _sb(V, F32), "CM0": _sb(V, BF), "CM1": _sb(V, BF),
+    "PN": _sb(V, F16), "DA": _sb(V, BF), "DB": _sb(V, BF), "S0": _sb(V, F16), "S1": _sb(V, F32),
+    "E": _sb(V, BF), "F": _sb(V, BF), "ZF": _sb(V, F32), "H": _sb(V, BF), "H32": _sb(V, BF), "HP": _sb(4096, BF),
+    "X": _sb(V, F32), "XR": _sb(4096, F32), "T1A": _sb(V, F16), "T1B": _sb(V, F16), "T2A": _sb(V, BF),
+    "T2B": _sb(V, BF), "T3A": _sb(V, BF), "T3B": _sb(V, BF), "AB": _sb(V, BF), "EX": _sb(5120, F32),
+    "CW": _sb(V, BF), "YA": _sb(V, BF), "YB": _sb(V, BF), "SEL": _sb(2560, BF), "UNW": _sb(V, BF),
+    "EN": _sb(V, BF), "DLT": _sb(256, BF), "DL": _sb(1024, BF), "DN": _sb(128, BF), "IH": _sb(512, F32),
+    "COL": _sb(8, F32), "IT": _sb(512, BF),
+    "LI": _sb(256, I32), "ZI": _sb(128, I32), "ZC": _sb(128, F16), "AB16": _sb(256, U16), "INV": _sb(256, U16),
+    "AP": _sb(128, F32), "BP": _sb(128, F32), "LX": _sb(128, F32), "LY": _sb(128, F32), "LS": _sb(13 * 128, U16),
+    "SG": _sb(4 * 128, BF), "MW": _sb(128, BF), "CC": _sb(128, BF), "UB": _sb(256, BF), "UW": _sb(512, BF),
+    "RU": _sb(256, BF), "ADW": _sb(128, BF),
+    "DJ": _sb(128, F32), "GJ": _sb(256, F32), "J16": _sb(16, F32), "PI": _sb(4, I32), "PF": _sb(8, F32),
+    "MK": _sb(16, F32), "BLK": _sb(160, BF), "II": _sb(256, BF), "NII": _sb(256, BF), "I32M": _sb(128, BF),
+    "N32M": _sb(128, BF), "N2M": _sb(128, BF), "GD": _sb(V, F32), "DD": _sb(V, BF), "WIN": _sb(256, BF), "M1": _sb(128, BF), "M2": _sb(128, BF),
+    "stL": ("dram", [4, 128, 64], I32), "lnL": ("dram", [4, 128, 64], I32),
+    "stZ": ("dram", [4, 128, 32], I32), "lnZ": ("dram", [4, 128, 32], I32),
+    "stH": ("dram", [4, 128, 512], BF), "lnH": ("dram", [4, 128, 512], BF),
+    "stP": ("dram", [4, 128, 512], BF), "lnP": ("dram", [4, 128, 512], BF),
+    "stE": ("dram", [4, 128, 512], BF), "lnE": ("dram", [4, 128, 512], BF),
+    "stG": ("dram", [16, 128, 128], F32), "lnG": ("dram", [16, 128, 128], F32),
+}
+PSUM = ["P0", "P1", "P2", "P3", "Q0", "Q1", "R0", "R1"]
+for _n in PSUM:
+    SCRATCH[_n] = ("psum", [128, 512], F32)
+
+N_DMA_SEMS = 110
+SEMAPHORES = ["eV", "eS", "eT", "eG", "sent"] + ["rx%d" % k for k in range(13)] + ["d%d" % k for k in range(N_DMA_SEMS)]
+
+CY, PCY, GA, LAT = 0.00104, 0.00052, 1.55, 0.10
+ALL, NONE = (0, 1, 2, 3), ()
+ORDER = {}
+N_EX = 10
+TUNE = {"wide": 512, "cut_y": [(0, 512), (512, 1024), (1024, 1536), (1536, 2048)], "cut_cm": [1, 1, 1, 1], "cut_pn": [1, 1, 1, 1], "sg": 0.0, "list": [0.0, 0.0],
+        "ya": ["****"] * 4, "yb": ["****"] * 4, "cw": ["****"] * 4, "skew": 1.25, "x1": "VVVV",
+        "x2": "****", "t3": "****", "zf": "*", "v_w0": 1, "tol": 0.3, "urgent": 1.0, "hops": 2, "later": [0.0, 0.0, 0.0, 0.0], "acc": 3.0,
+        "v_abs": [[NONE], [NONE] * 4, [NONE], [NONE, ALL, NONE, NONE]], "early": 0.0,
+        "passes": 6, "seed_greedy": True, "lean": 0.0, "seed": 2, "turns": 40, "shake": 2.0, "span": 100.0}
+CASES = [{"g": 1.0, "c": 1.0, "p": 1.0, "d": 1.0, "w": 1.0, "weight": 1.0},
+         {"g": 0.72, "c": 1.0, "p": 1.0, "d": 1.2, "w": 1.5, "weight": 0.6},
+         {"g": 1.3, "c": 1.0, "p": 0.9, "d": 1.0, "w": 1.0, "weight": 0.4},
+         {"g": 1.0, "c": 1.0, "p": 1.5, "d": 1.3, "w": 2.0, "weight": 0.4}]
+
+
+def split_engines(topo, src, dsts):
+    far = [d for d in dsts if topo.chip(d) != topo.chip(src)]
+    near = [d for d in dsts if topo.chip(d) == topo.chip(src)]
+    out, used = {}, []
+    for group in (far, near):
+        if not group:
+            continue
+        pool = [e for e in topo.engines(src, group[0]) if e not in used]
+        n = 1
+        while 2 * n * len(group) <= len(pool):
+            n *= 2
+        for k, d in enumerate(group):
+            mine = pool[k * n:(k + 1) * n]
+            used.extend(mine)
+            out[d] = (sum(1 << e for e in mine), n)
+    return out
+
+
+def build(g, core, T, topo):
+    q = T.rank_of(core)
+    cores = list(T.cores)
+    others = [r for r in range(4) if r != q]
+    A, F = AluOpType, ActivationFunctionType
+    ops = []
+    bias = [0.0]
+
+    def add(eng, fn, rd, wr, dur, kind="c", issue=None, after=None, acc=False, sem=None, count=0):
+        listed = any(x[0] in ("AB16", "INV", "LS") for x in rd)
+        cls = "p" if eng == "T" else "d" if kind != "c" else "g" if listed else "c"
+        ops.append({"cls": cls, "eng": eng, "fn": fn, "rd": rd, "wr": wr, "dur": dur, "kind": kind, "acc": acc, "bias": bias[0],
+                    "issue": dur if issue is None else issue, "after": after, "sem": sem, "count": count})
+        return len(ops) - 1
+
+    def ap(x):
+        return T[x[0]][:, x[1]:x[2]:x[3]] if len(x) > 3 else T[x[0]][:, x[1]:x[2]]
+
+    def width(x):
+        return (x[2] - x[1] + (x[3] - 1 if len(x) > 3 else 0)) // (x[3] if len(x) > 3 else 1)
+
+    def two(x):
+        return SCRATCH[x[0]][2] in (BF, F16, U16)
+
+    def src(x, lst):
+        return ap(x).indirect(ap(lst)) if lst else ap(x)
+
+    def cols(*xs):
+        return [x for x in xs if isinstance(x, tuple)]
+
+    def val(x):
+        return ap(x) if isinstance(x, tuple) else x
+
+    def v_tt(o, a, b, op, lst=None):
+        n = width(o)
+        f = GA if lst else (1.0 if a[0] in PSUM or b[0] in PSUM else 2.0)
+        add("V", lambda: [g.vector.tensor_tensor(ap(o), src(a, lst), ap(b), op)], cols(a, b, lst), [o], 0.06 + max(64, n * f) * CY)
+
+    def v_ts(o, a, s1, op0, s2=None, op1=None, lst=None):
+        n = width(o)
+        f = GA if lst else (0.5 if two(o) and two(a) else 1.0)
+
+        def fn():
+            if op1 is None:
+                return [g.vector.tensor_scalar(ap(o), src(a, lst), val(s1), None, op0)]
+            return [g.vector.tensor_scalar(ap(o), src(a, lst), val(s1), val(s2), op0, op1)]
+        add("V", fn, cols(a, s1, s2, lst), [o], 0.06 + max(64, n * f) * CY)
+
+    def v_cp(o, a, lst=None):
+        n = width(o)
+        f = GA if lst else (0.5 if two(o) and two(a) else 1.0)
+        add("V", lambda: [g.vector.tensor_copy(ap(o), src(a, lst))], cols(a, lst), [o], 0.06 + max(64, n * f) * CY)
+
+    def s_act(o, a, func, bias=0.0, scale=1.0, lst=None):
+        n = width(o)
+        add("S", lambda: [g.scalar.activation(ap(o), src(a, lst), func, bias=val(bias), scale=val(scale))],
+            cols(a, bias, scale, lst), [o], 0.07 + max(64, n * (GA if lst else 1.0)) * CY)
+
+    def either(on_v, on_s):
+        on_s()
+        other = ops.pop()
+        on_v()
+        ops[-1]["alt"] = {"V": (ops[-1]["fn"], ops[-1]["dur"]), "S": (other["fn"], other["dur"])}
+
+    def cp(eng, o, a, lst=None):
+        if eng == "V":
+            v_cp(o, a, lst)
+        elif eng == "S":
+            s_act(o, a, F.Identity, lst=lst)
+        else:
+            either(lambda: v_cp(o, a, lst), lambda: s_act(o, a, F.Identity, lst=lst))
+
+    def pe(mms, acc=False):
+        def fn():
+            done = []
+            for k, (o, l, r, st, sp) in enumerate(mms):
+                ins = g.tensor.matmul(ap(o), ap(l), ap(r), st, sp)
+                if sp or k == len(mms) - 1:
+                    done.append(ins)
+            return done
+        cyc = sum(max(64, width(m[2])) * (4 if SCRATCH[m[2][0]][2] == F32 else 1) for m in mms)
+        add("T", fn, [m[1] for m in mms] + [m[2] for m in mms], [(mms[0][0][0], 0, 512)], 0.06 + cyc * PCY, acc=acc)
+
+    def group(o, pairs):
+        return [(o, l, r, k == 0, k == len(pairs) - 1) for k, (l, r) in enumerate(pairs)]
+
+    def dma(eng, pairs, rd, wr, dur, **kw):
+        queue = {"Y": g.sync, "S": g.scalar, "G": g}[eng]
+        add(eng, lambda: [queue.dma_start(o, i, **kw) for o, i in pairs], rd, wr, dur, kind="d",
+            issue=(0.9 if eng == "G" else 0.06) * len(pairs))
+
+    def send(k, plan, rd, wr, dur):
+        masks = split_engines(topo, core, [cores[r] for r, _, _ in plan])
+        sem = T.sem["rx%d" % k]
+
+        def fn():
+            tr = []
+            for r, s, d in plan:
+                rid, pid, _ = topo.addr(cores[r])
+                tr.append(RemoteDMATransfer(dst_ids=[DstId(rid=rid, pnc=pid)], dma_engine_mask=masks[cores[r]][0],
+                                            remote_sem=sem, src=s, dst=d))
+            g.remote_dma_fused(tr, local_sem=T.sem.sent)
+            return []
+        me = add("G", fn, rd, [], 0.5, kind="r", count=sum(n for _, n in masks.values()))
+        got = 0
+        for r, _, _ in plan:
+            s = (2 * q - r) % 4
+            got += split_engines(topo, cores[s], [cores[(s + x - q) % 4] for x, _, _ in plan])[core][1]
+        add("X", None, [], wr, dur + 2.3, kind="x", issue=dur, after=me, sem="rx%d" % k, count=got)
+
+    def ch(name, k, n=512, base=0):
+        return (name, base + k * n, base + (k + 1) * n)
+
+    def lst(name, base, k, n=32):
+        return (name, base + k * n, base + (k + 1) * n)
+
+    ID, ROT, NID, NROT = ("II", 0, 128), ("II", 96, 224), ("NII", 0, 128), ("NII", 96, 224)
+
+    BACK = ("II", 32, 160)
+
+    def sel(i, turn=0):
+        return ("SEL", 160 * i + 32 * turn, 160 * i + 32 * turn + 128)
+
+    def unw(i):
+        return ("UNW", 128 * i, 128 * i + 128)
+
+    rows = slice(32 * q, 32 * q + 32)
+    dma("Y", [(T.stL[:, 0:64, :], T.sa[:]), (T.stL[:, 64:128, :], T.sb[:])], [], [("stL", 0, 4)], 2.2)
+    dma("S", [(T.stH[:], T.hf[:])], [], [("stH", 0, 4)], 2.8)
+    dma("S", [(T.lnL[q, 0:64, :], T.sa[rows]), (T.lnL[q, 64:128, :], T.sb[rows])], [], [("lnL", q, q + 1)], 2.2)
+    dma("Y", [(T.stP[:], T.p0[:])], [], [("stP", 0, 4)], 2.8)
+    dma("Y", [(T.stE[:], T.toll[:])], [], [("stE", 0, 4)], 3.0)
+    dma("Y", [(T.stZ[:], T.lim[:])], [], [("stZ", 0, 4)], 2.6)
+    dma("Y", [(T.lnH[q], T.hf[rows]), (T.lnP[q], T.p0[rows]), (T.lnE[q], T.toll[rows]), (T.lnZ[q], T.lim[2 * q:2 * q + 2])],
+        [], [("lnH", q, q + 1), ("lnP", q, q + 1), ("lnE", q, q + 1), ("lnZ", q, q + 1)], 3.0)
+
+    def iota(o, pat, base, cm):
+        small = SCRATCH[o[0]][2] != I32
+        add("G", lambda: [g.iota(ap(o), pat, base, cm, allow_small_or_imprecise_dtypes=small)], [], [o], 0.13 + 2 * width(o) * CY)
+
+    def send_input(k, nm, dur):
+        send(k, [(r, T["st" + nm][r], T["ln" + nm][q]) for r in others], [("st" + nm, 0, 4)],
+             [("ln" + nm, r, r + 1) for r in others], dur)
+
+    first_g = len(ops)
+    iota(("PI", 0, 1), [[0, 1]], 0, 1)
+    iota(("J16", 0, 16), [[1, 16]], 0, 0)
+    iota(("GJ", 0, 256), [[0, 2], [1, 8], [0, 16]], 0, 0)
+    iota(("IH", 0, 256), [[1, 32], [0, 8]], 0, 0)
+    iota(("IH", 256, 512), [[0, 32], [1, 8]], 0, 0)
+    send_input(0, "L", 1.1)
+    send_input(1, "H", 4.4)
+    iota(("DJ", 0, 128), [[1, 128]], 0, -1)
+    send_input(2, "P", 4.4)
+    send_input(3, "E", 4.4)
+    send_input(4, "Z", 3.0)
+    line = [k for k in range(first_g, len(ops)) if ops[k]["eng"] == "G"]
+    for a, b in zip(line, line[1:]):
+        ops[b]["after"] = a
+    dma("Y", [(T.EN[:], T.toll[:])], [("lnZ", 0, 4)], [("EN", 0, V)], 3.0)
+    dma("Y", [(T.LI[:, 0:128], T.lnL[:, 0:64, :]), (T.LI[:, 128:256], T.lnL[:, 64:128, :])], [("lnL", 0, 4)], [("LI", 0, 256)], 2.2)
+    dma("Y", [(T.H[:], T.lnH[:]), (T.HP[32:128, 0:V], T.lnH[0:3]), (T.HP[0:32, 0:V], T.lnH[3])], [("lnH", 0, 4)],
+        [("H", 0, V), ("HP", 0, V)], 3.5)
+    dma("Y", [(T.F[:], T.lnP[:])], [("lnP", 0, 4)], [("F", 0, V)], 2.8)
+    dma("Y", [(T.E[:], T.lnE[:])], [("lnE", 0, 4)], [("E", 0, V)], 2.8)
+    dma("Y", [(T.ZI[:], T.lnZ[:])], [("lnZ", 0, 4)], [("ZI", 0, 128)], 2.2)
+    dma("Y", [(T.HP[32:128, V:2 * V], T.lnH[0:3]), (T.HP[0:32, V:2 * V], T.lnH[3])], [("lnH", 0, 4)], [("HP", V, 2 * V)], 3.0)
+
+    add("V", lambda: [g.vector.memset(T.SEL[:], 0.0)], [], [("SEL", 0, 2560)], 0.06 + 1280 * CY)
+    v_ts(("PI", 1, 2), ("PI", 0, 1), 4, A.arith_shift_right)
+    v_ts(("PI", 2, 3), ("PI", 0, 1), 15, A.bitwise_and)
+    v_ts(("PI", 3, 4), ("PI", 0, 1), 4, A.arith_shift_right, 1, A.bitwise_and)
+    v_cp(("PF", 0, 4), ("PI", 0, 4))
+    v_ts(("BLK", 0, 160), ("GJ", 0, 160), ("PF", 1, 2), A.is_equal)
+    for i in range(16):
+        v_ts(("SEL", 160 * i + i, 160 * i + 160, 16), ("BLK", i, 160, 16), BIG, A.mult)
+    v_ts(("II", 0, 128), ("DJ", 0, 128), 0.0, A.is_equal)
+    v_ts(("II", 128, 256), ("DJ", 0, 128), 0.0, A.is_equal)
+    v_ts(("MK", 0, 16), ("J16", 0, 16), ("PF", 2, 3), A.is_equal)
+    v_ts(("PF", 5, 6), ("PF", 2, 3), 8.0, A.is_lt)
+    v_ts(("COL", 0, 4), ("J16", 0, 4), ("PF", 5, 6), A.mult, 64.0, A.mult)
+    v_ts(("COL", 4, 8), ("COL", 0, 4), 32.0, A.add)
+    v_ts(("PF", 6, 7), ("PF", 5, 6), 32.0, A.mult)
+    v_ts(("IT", 0, 256), ("IH", 0, 256), ("PF", 5, 6), A.mult)
+    v_ts(("IT", 256, 512), ("IH", 256, 512), ("MK", 8, 9), A.mult)
+    v_tt(("CM0", 0, 256), ("IT", 0, 256), ("IT", 256, 512), A.add)
+    v_ts(("CM0", 256, 512), ("CM0", 0, 256), ("PF", 6, 7), A.add)
+    for k in range(4):
+        if k:
+            v_ts(ch("CM0", k), ch("CM0", 0), ("COL", k, k + 1), A.add)
+        s_act(ch("G0", k), ch("CM0", 0), F.Identity, bias=("COL", 4 + k, 5 + k))
+
+    v_cp(("AB16", 0, 256), ("LI", 0, 256))
+    add("V", lambda: [g.vector.tensor_copy(T.CW[:].indirect(T.AB16[:, 0:128]), T.CM0[:])],
+        [("CM0", 0, V), ("AB16", 0, 128)], [("CW", 0, V)], 3.5 * V * CY)
+    add("S", lambda: [g.scalar.activation(T.W1[:, V:2 * V].indirect(T.AB16[:, 128:256]), T.G0[:], F.Silu)],
+        [("G0", 0, V), ("AB16", 128, 256)], [("W1", V, 2 * V)], 1.3 + 3.5 * V * CY)
+    for s, R in enumerate(("CW", "CM1")):
+        for hf in range(2):
+            bank = "Q%d" % hf
+            if s:
+                s_act(ch(R, hf, 1024), ch("W1", hf, 1024, V), F.Identity, bias=-32.0)
+            pe(group((bank, 0, 64), [(sel(i), (R, 1024 * hf + i, 1024 * hf + 1024, 16)) for i in range(16)]))
+            v_ts(("INV", 128 * s + 64 * hf, 128 * s + 64 * hf + 64), (bank, 0, 64), 1.0 / BIG, A.mult, 0.25, A.add)
+    v_ts(("AP", 0, 128), ("LI", 0, 128), CUT, A.add)
+    v_ts(("BP", 0, 128), ("LI", 128, 256), CUT + V, A.add)
+    v_ts(("NII", 0, 256), ("II", 0, 256), -1.0, A.mult)
+    for i in range(16):
+        either(lambda: v_ts(unw(i), ("BLK", 0, 128), ("MK", i, i + 1), A.mult),
+               lambda: s_act(unw(i), ("BLK", 0, 128), F.Identity, scale=("MK", i, i + 1)))
+    v_ts(("PF", 4, 5), ("PF", 3, 4), -1.0, A.mult, 1.0, A.add)
+    v_ts(("M1", 0, 128), ("DJ", 0, 128), -16.0, A.is_equal, ("PF", 3, 4), A.mult)
+    v_tt(("M1", 0, 128), ("M1", 0, 128), ID, A.add)
+    v_tt(("M1", 0, 128), ("M1", 0, 128), ID, A.add)
+    v_ts(("M2", 0, 128), ("DJ", 0, 128), 16.0, A.is_equal, ("PF", 4, 5), A.mult)
+    v_ts(("I32M", 0, 128), ID, 1.0 / 32, A.mult)
+    v_ts(("N32M", 0, 128), ID, -1.0 / 32, A.mult)
+    v_ts(("N2M", 0, 128), ID, -2.0, A.mult)
+    v_cp(("ZC", 0, 128), ("ZI", 0, 128))
+
+    for s, (D, Y) in enumerate((("DA", "YA"), ("DB", "YB"))):
+        for k in range(4):
+            v_tt(ch(Y, k), ("H", 0, V), ch("HP", k), A.subtract, lst=lst("INV", 128 * s, k))
+            s_act(ch(D, k), ch(Y, k), F.Abs)
+            bank = "P%d" % (2 * s + k % 2)
+            pe(group((bank, 0, 512), [(ID, ch("F", k)), (ID, ch(D, k))]))
+            cp("*", ch("W0", k, base=s * V), (bank, 0, 512))
+    for k in range(2):
+        v_ts(ch("H32", k, 1024), ch("H", k, 1024), 32.0, A.mult)
+
+    cur = [0]
+    steps = [0]
+
+    def compare(want_list, lbase, cc):
+        W = "W%d" % cur[0]
+        CM = "CM%d" % (steps[0] % 2)
+        steps[0] += 1
+        for k in range(4):
+            n = TUNE["cut_cm"][k]
+            for j in range(n * k, n * k + n):
+                cp("S", ch("G0", j, 512 // n), (W, 0, V), lst=lst("AB16", 0, j, 32 // n))
+                v_tt(ch(CM, j, 512 // n), (W, V, 2 * V), ch("G0", j, 512 // n), A.is_lt, lst=lst("AB16", 128, j, 32 // n))
+            if want_list and k % 2 == 1:
+                make_list(CM, lbase, k // 2, "Q%d" % (k // 2))
+            if not want_list:
+                compact(CM, k, "Q0", 0)
+        return CM
+
+    def make_list(CM, lbase, hf, bank):
+        bias[0] = TUNE["list"][hf]
+        pe(group((bank, 0, 64), [(sel(i), (CM, 1024 * hf + i, 1024 * hf + 1024, 16)) for i in range(16)]))
+        v_tt(ch("LX", hf, 64), (bank, 0, 64), ch("AP", hf, 64), A.max)
+        v_tt(ch("LY", hf, 64), ch("LX", hf, 64), ch("BP", hf, 64), A.min)
+        v_ts(ch("LS", hf, 64, lbase), ch("LY", hf, 64), -CUT, A.add)
+        bias[0] = 0.0
+
+    def compact(src_name, k, bank, turn, first=True, last=True):
+        mm = [((bank, 0, 128), sel(i, turn), (src_name, 128 * i, 128 * i + 128), first and i == 0, last and i == 15)
+              for i in range(4 * k, 4 * k + 4)]
+        pe(mm, acc=not (first and k == 0))
+
+    def signed(bank, col, eng):
+        if eng == "S":
+            s_act(("SG", 128 * col, 128 * col + 128), (bank, 0, 128), F.Identity, bias=8.5, scale=-1.0 / BIG)
+        else:
+            v_ts(("SG", 128 * col, 128 * col + 128), (bank, 0, 128), -1.0 / BIG, A.mult, 8.5, A.add)
+
+    def advance(f, lbase, Fname, PN="PN"):
+        W, Wn = "W%d" % cur[0], "W%d" % (1 - cur[0])
+        bare = Fname == "E"
+        pieces = [(j, 512 // n) for k, n in enumerate(TUNE["cut_pn"]) for j in range(n * k, n * k + n)]
+        for m, (j, n) in enumerate(pieces):
+            v_tt(ch(PN, j, n), (W, 0, 2 * V), ch(Fname, j, n), A.add, lst=lst("LS", lbase, j, n // 16))
+            a, b = ("P%d" % (2 * (m % 2)), 0, n), ("P%d" % (2 * (m % 2) + 1), 0, n)
+            pe(group(a, [(ROT, ch(PN, j, n))] + ([(ID, ch("DA", j, n))] if bare else [])))
+            cp("*", ch(Wn, j, n), a)
+            pe(group(b, [(ROT, ch(PN, j, n)), (ID, ch("DB" if bare else "DD", j, n))]))
+            cp("*", ch(Wn, j, n, V), b)
+        cur[0] = 1 - cur[0]
+
+    def spread(bank, k, small, plus=()):
+        mm = []
+        for j in range(4):
+            mm += group((bank, 128 * j, 128 * j + 128),
+                        [(l, ch(r, 4 * k + j, 128)) for l, r in plus] + [(unw(4 * k + j), small)])
+        pe(mm)
+
+    def bounds():
+        for k in range(4):
+            bank = "P%d" % k
+            spread(bank, k, ("ZC", 0, 128), [(NID, "E")])
+            cp(TUNE["zf"], ch("ZF", k), (bank, 0, 512))
+
+    def turn_x():
+        dma("Y", [(T.XR[32:128, c:c + V], T.X[0:96, :]) for c in (0, V)] + [(T.XR[0:32, c:c + V], T.X[96:128, :]) for c in (0, V)],
+            [("X", 0, V)], [("XR", 0, 2 * V)], 9.0)
+
+    terms, slots = [0], [0]
+
+    def next_ex():
+        slots[0] += 1
+        return ch("EX", slots[0] % N_EX)
+
+    def stage(e, k, first=False):
+        pair, wr = [(T.stG[4 * k:4 * k + 4], ap(e))], [("stG", 4 * k, 4 * k + 4)]
+        if first:
+            dma("Y", pair, [e], wr, 2.6)
+        else:
+            dma("G", pair, [e], wr, TUNE["acc"], accum_op=A.add, max_dma_last_dim=2048)
+
+    def term(k, pairs, off, half, v_abs):
+        n = terms[0]
+        terms[0] += 1
+        lnw = math.log(0.5) if half else 0.0
+        o = ("R%d" % (n % 2), 0, 512)
+        e, ab = next_ex(), ch("AB", n % 4)
+        pe(group(o, [(l, ch(r, k)) for l, r in pairs]))
+        if k in v_abs:
+            v_ts(ab, o, -off, A.add, 0.0, A.max)
+            pe(group(o, [(l, ch(r, k)) for l, r in pairs] + [(("N2M", 0, 128), ab)]))
+            s_act(e, o, F.Exp, bias=lnw - off / 8, scale=0.125)
+        else:
+            s_act(ab, o, F.Abs, bias=-off)
+            s_act(e, ab, F.Exp, bias=lnw, scale=-0.125)
+        stage(e, k)
+
+    def walk_back(f):
+        for t in (3, 2, 1):
+            for k in range(4):
+                bank = "P%d" % k
+                spread(bank, k, ("CC", 0, 128))
+                cp(TUNE["cw"][f][k], ch("CW", k), (bank, 0, 512))
+            bank = "Q%d" % (t % 2)
+            if t == 1:
+                pe([((bank, 0, 128), ID, ("UB", 128, 256), True, False)])
+            for k in range(4):
+                for Y, base, sign in (("YA", 0, 1.0), ("YB", 128, -1.0)):
+                    for lo, hi in TUNE["cut_y"]:
+                        if lo // 512 == k:
+                            o, l = (Y, lo, hi), ("INV", base + lo // 16, base + hi // 16)
+                            either(lambda: v_ts(o, ("CW", 0, V), sign, A.mult, 0.0, A.max, lst=l),
+                                   lambda: s_act(o, ("CW", 0, V), F.Relu, scale=sign, lst=l))
+                compact("YA", k, bank, 1, first=t > 1, last=False)
+                compact("YB", k, bank, 1, first=False, last=True)
+            if t > 1:
+                v_tt(("CC", 0, 128), (bank, 0, 128), ("SG", 128 * (t - 1), 128 * t), A.mult)
+            if t == 3:
+                v_cp(("UB", 0, 128), (bank, 0, 128))
+            if t == 2:
+                v_tt(("UB", 128, 256), (bank, 0, 128), ("UB", 0, 128), A.add)
+            if t == 1:
+                v_ts(ch("UW", f, 128), (bank, 0, 128), 0.0, A.is_gt, 4.0, A.mult)
+
+    def forest(f):
+        first, last = f % 2 == 0, f == 3
+        P = "A" if first else "B"
+        Fname = "E" if first else "F"
+        L = [128 * (3 * f + t) for t in range(4)]
+        for t in (1, 2):
+            CM = compare(True, L[t], t)
+            advance(f, L[t], Fname)
+            bias[0] = TUNE["sg"]
+            for k in range(4):
+                compact(CM, k, "Q1", 0)
+            signed("Q1", t, "S")
+            bias[0] = 0.0
+            n = TUNE["wide"]
+            for k in range(V // n):
+                if t == 1:
+                    v_tt(ch("X", k, n), ("HP", 0, 2 * V), ch("H32", k, n), A.add, lst=lst("LS", L[1], k, n // 16))
+                else:
+                    cp("*", ch("X", k, n), ("XR", 0, 2 * V), lst=lst("LS", L[2], k, n // 16))
+            turn_x()
+        CM = compare(first, L[3], 3)
+        if first:
+            W, CZ = "W%d" % cur[0], "CM%d" % (steps[0] % 2)
+            steps[0] += 1
+            for k in range(4):
+                compact(CM, k, "Q0", 0)
+            signed("Q0", 3, "S")
+            for k in range(4):
+                v_tt(ch(CZ, k), (W, 0, 2 * V), ch("ZF", k), A.is_gt, lst=lst("LS", L[3], k))
+                compact(CZ, k, "Q1", 0)
+            v_ts(("MW", 0, 128), ("Q1", 0, 128), CUT, A.is_ge)
+        else:
+            signed("Q0", 3, "V")
+        v_tt(("CC", 0, 128), ("MW", 0, 128), ("SG", 384, 512), A.mult)
+        if not first:
+            for hf in range(2):
+                make_list(CM, L[3], hf, "R%d" % hf)
+        walk_back(f)
+        bias[0] = -TUNE["later"][f]
+        n = 512 if last else TUNE["wide"]
+        for k in range(V // n):
+            cp("*", ch("T3" + P, k, n), ("HP", 0, 2 * V), lst=lst("LS", L[3], k, n // 16))
+            v_cp(ch("T1" + P, k, n), ("XR", 0, 2 * V), lst=lst("LS", L[3], k, n // 16))
+            v_ts(ch("T2" + P, k, n), ch("T1" + P, k, n), HI - 15.5, A.add)
+        v_ts(ch("WIN", min(f, 1), 128), ("SG", 384, 512), 0.0, A.is_lt, 1.0 if first else 0.5, A.mult)
+        if f:
+            v_tt(ch("WIN", 0, 128), ch("WIN", 0, 128), ch("WIN", 1, 128), A.add)
+        if last:
+            for k in range(4):
+                bank, e = "R%d" % (k % 2), next_ex()
+                spread(bank, k, ch("WIN", 0, 128))
+                v_tt(e, (bank, 0, 512), ch("GD", k), A.mult)
+                stage(e, k)
+        todo = []
+        if not first:
+            todo += [([(("I32M", 0, 128), "T2A"), (NID, "T3B")], HI / 32, False),
+                     ([(("I32M", 0, 128), "T2B"), (NID, "T3A")], HI / 32, True),
+                     ([(ID, "T1A"), (NID, "T2A"), (("N32M", 0, 128), "T2B")], -HI - HI / 32, False),
+                     ([(ID, "T1B"), (NID, "T2B"), (("N32M", 0, 128), "T2A")], -HI - HI / 32, True)]
+        skew = TUNE["skew"] if last else 0.1
+        for _, j, k in sorted((j + skew * k, j, k) for j in range(len(todo)) for k in range(4)):
+            term(k, todo[j][0], todo[j][1], todo[j][2], TUNE["v_abs"][f][j])
+        bias[0] = 0.0
+
+    def new_tolls(bank, k, small, old, new):
+        spread(bank, k, small, [(ID, old)])
+        v_ts(ch(new, k), (bank, 0, 512), 0.0, A.max, 63.0, A.min)
+
+    def tolls_home(rnd, banks, new):
+        mine = ch("DLT", rnd, 128)
+        land = lambda r: ch("DL", 4 * rnd + r, 128)
+        send(7 + rnd, [(r, ap(mine), ap(land(q))) for r in others], [mine], [land(r) for r in others], 1.1)
+        tiles = [mine if r == q else land(r) for r in range(4)]
+        bank = banks[0]
+
+        def fn():
+            return [g.tensor.matmul(T[bank][32 * r:32 * r + 32, 0:128], T.II[:, 32 * q:32 * q + 32], ap(tiles[r]), True, True)
+                    for r in range(4)]
+        add("T", fn, tiles + [ID], [(bank, 0, 512)], 0.06 + 512 * PCY)
+        v_cp(("DN", 0, 128), (bank, 0, 128))
+        for k in range(4):
+            new_tolls(banks[(k + 1) % len(banks)], k, ("DN", 0, 128), "EN", new)
+
+    compare(True, 0, 0)
+    advance(0, 0, "E", "T1B")
+    for k in range(4):
+        bank = ("R%d" % (k % 2), 0, 512)
+        pe(group(bank, [(ID, ch("DB", k)), (NID, ch("DA", k))]))
+        cp("S", ch("DD", k), bank)
+    for k in range(4):
+        pe(group(("R0", 0, 512), [(ROT, ch("T1B", k)), (NROT, ch("E", k))]))
+        v_cp(ch("S0", k), ("R0", 0, 512))
+        pe(group(("R1", 0, 512), [(ROT, ch("T1B", k)), (NROT, ch("E", k)), (ID, ch("DD", k))]))
+        cp("S", ch("S1", k), ("R1", 0, 512))
+    bias[0] = -TUNE["early"]
+    for s, D in enumerate(("DA", "DB")):
+        for k in range(4):
+            s_act(ch("XR", k, base=s * V), ch(D, k), F.Exp, scale=-0.125)
+    for k in range(4):
+        e = next_ex()
+        s_act(e, ("XR", 0, V), F.Identity, scale=3.0, lst=lst("AB16", 0, k))
+        stage(e, k, True)
+        s_act(ch("GD", k), ("XR", V, 2 * V), F.Identity, lst=lst("AB16", 128, k))
+        e = next_ex()
+        s_act(e, ("XR", 0, V), F.Identity, scale=-1.0, lst=lst("AB16", 0, k))
+        dma("G", [(ap(ch("GD", k)), ap(e))], [e], [ch("GD", k)], TUNE["acc"], accum_op=A.add, max_dma_last_dim=2048)
+    bias[0] = 0.0
+    for rnd in range(2):
+        f = 2 * rnd
+        W = "W%d" % cur[0]
+        if rnd:
+            v_tt(ch("DLT", 0, 128), ch("UW", 0, 128), ch("UW", 1, 128), A.subtract)
+            tolls_home(0, ["R0", "R1"], "EN")
+            for k in range(4):
+                bank = "P%d" % k
+                new_tolls(bank, k, ch("DLT", 0, 128), "E", "E")
+                pe(group((bank, 0, 512), [(ROT, ch("E", k)), (ID, ch("DA", k))]))
+                v_tt(ch(W, k, base=V), (bank, 0, 512), ch("S1", k), A.add)
+                bank = "Q%d" % (k % 2)
+                pe(group((bank, 0, 512), [(ROT, ch("E", k)), (ID, ch("DA", k)), (ID, ch("S0", k))]))
+                s_act(ch(W, k), (bank, 0, 512), F.Identity)
+        bounds()
+        forest(f)
+        W = "W%d" % cur[0]
+        send(5 + rnd, [((q - 1) % 4, ap(ch("UW", f, 128)), ap(ch("RU", rnd, 128)))], [ch("UW", f, 128)], [ch("RU", rnd, 128)], 0.6)
+        pe(group(("Q0", 0, 128), [(("M1", 0, 128), ch("UW", f, 128)), (("M2", 0, 128), ch("RU", rnd, 128))]))
+        v_cp(("ADW", 0, 128), ("Q0", 0, 128))
+        for k in range(4):
+            bank = "P%d" % k
+            spread(bank, k, ("ADW", 0, 128), [(ID, "E"), (BACK, "DA")])
+            s_act(ch("F", k), (bank, 0, 512), F.Identity)
+            pe(group((bank, 0, 512), [(ROT, ch("F", k))]))
+            v_tt(ch(W, k, base=V), (bank, 0, 512), ch("S1", k), A.add)
+            if k < TUNE["v_w0"]:
+                v_tt(ch(W, k), (bank, 0, 512), ch("S0", k), A.add)
+            else:
+                bank = "Q%d" % (k % 2)
+                pe(group((bank, 0, 512), [(ROT, ch("F", k)), (ID, ch("S0", k))]))
+                cp("*", ch(W, k), (bank, 0, 512))
+        forest(f + 1)
+
+    v_tt(ch("DLT", 1, 128), ch("UW", 2, 128), ch("UW", 3, 128), A.subtract)
+    tolls_home(1, ["P0", "P1", "P2", "P3"], "G0")
+    for k in range(4):
+        part = slice(512 * k, 512 * k + 512)
+        dma("Y", [(T.tollout[:, part], ap(ch("G0", k)))], [ch("G0", k)], [], 2.5)
+    for k in range(4):
+        part = slice(512 * k, 512 * k + 512)
+        st = [("stG", 4 * k, 4 * k + 4)]
+        send(9 + k, [(r, T.stG[4 * k + (r + 3) % 4], T.lnG[4 * k + q]) for r in others], st,
+             [("lnG", 4 * k + r, 4 * k + r + 1) for r in others], 2.2)
+        dma("Y", [(T.lnG[4 * k + q], T.stG[4 * k + (q + 3) % 4])], st, [("lnG", 4 * k + q, 4 * k + q + 1)], 2.4)
+        dma("Y", [(T.gain[:, part], T.lnG[4 * k:4 * k + 4])], [("lnG", 4 * k, 4 * k + 4)], [], 2.8)
+    return ops
+
+
+def dependencies(ops):
+    log = {}
+    for n, o in enumerate(ops):
+        deps, order = set(), set()
+        touched = [(x, x[0] in PSUM) for x in o["rd"]] + [(x, True) for x in o["wr"]]
+        for x, w in touched:
+            lo, hi = (0, 512) if x[0] in PSUM else (x[1], x[2])
+            for (a, b, m, mw) in log.get(x[0], []):
+                if a < hi and lo < b and (w or mw) and m != n:
+                    if o["acc"] and x[0] in PSUM and ops[m]["eng"] == "T":
+                        order.add(m)
+                    else:
+                        deps.add(m)
+        for x, w in touched:
+            lo, hi = (0, 512) if x[0] in PSUM else (x[1], x[2])
+            old = log.get(x[0], [])
+            if w:
+                old = [e for e in old if not (lo <= e[0] and e[1] <= hi)]
+            log[x[0]] = old + [(lo, hi, n, w)]
+        if o["after"] is not None:
+            order.add(o["after"])
+        o["deps"], o["order"] = deps, order - deps
+
+
+def schedule(ops):
+    n = len(ops)
+    users = [[] for _ in range(n)]
+    for k, o in enumerate(ops):
+        for d in o["deps"] | o["order"]:
+            users[d].append(k)
+    level = [0.0] * n
+    for k in range(n - 1, -1, -1):
+        level[k] = ops[k]["dur"] + max([level[u] + LAT for u in users[k]] or [0.0])
+    level = [level[k] + ops[k]["bias"] for k in range(n)]
+    missing = [len(o["deps"] | o["order"]) for o in ops]
+    ready = [0.0] * n
+    pool = {e: [] for e in "VSTGYX"}
+    free = {e: 0.0 for e in pool}
+    placed = [False] * n
+    hold = {e: 0.0 for e in pool}
+    tol, urgent = TUNE["tol"], TUNE["urgent"]
+
+    def engines(k):
+        return "VS" if "alt" in ops[k] else ops[k]["eng"]
+
+    def enter(k):
+        for e in engines(k):
+            pool[e].append(k)
+
+    def soonest(k, depth):
+        t = ready[k]
+        if missing[k]:
+            if depth == 0:
+                return 1e9
+            for d in ops[k]["deps"] | ops[k]["order"]:
+                if not placed[d]:
+                    t = max(t, max(soonest(d, depth - 1), min(free[x] for x in engines(d))) + ops[d]["dur"] + LAT)
+        return t
+
+    for k in range(n):
+        if not missing[k]:
+            enter(k)
+    out = []
+    while len(out) < n:
+        best = None
+        for e in pool:
+            if pool[e]:
+                t = max(free[e], hold[e], min(ready[k] for k in pool[e]))
+                if best is None or t < best[0]:
+                    best = (t, e)
+        t, e = best
+        now = [k for k in pool[e] if ready[k] <= t]
+        k = max(now, key=lambda j: (level[j], -j))
+        if e in "VST":
+            near = set(pool[e])
+            rim = set(j for x in pool for j in pool[x] if level[j] > level[k] + urgent)
+            for _ in range(TUNE["hops"]):
+                rim = set(u for j in rim for u in users[j] if level[u] > level[k] + urgent)
+                near |= rim
+            due = [soonest(j, TUNE["hops"]) for j in near if ops[j]["eng"] == e and "alt" not in ops[j] and level[j] > level[k] + urgent]
+            due = [x for x in due if x > t]
+            if due and min(due) < t + ops[k]["issue"] - tol:
+                fit = [j for j in now if t + ops[j]["issue"] - tol <= min(due)]
+                if not fit:
+                    hold[e] = min(min(due), t + 0.1)
+                    continue
+                k = max(fit, key=lambda j: (level[j], -j))
+        for x in engines(k):
+            pool[x].remove(k)
+        placed[k] = True
+        free[e] = t + ops[k]["issue"]
+        out.append((k, e))
+        for u in users[k]:
+            ready[u] = max(ready[u], t + ops[k]["dur"] + (LAT if k in ops[u]["deps"] else 0.0))
+            missing[u] -= 1
+            if not missing[u]:
+                enter(u)
+    return out
+
+
+def pack(ops, before, rank, fixed, backward):
+    n = len(ops)
+    after = [[] for _ in range(n)]
+    for k in range(n):
+        for d in before[k]:
+            after[d].append(k)
+    missing = [len(b) for b in before]
+    ready, start, where = [0.0] * n, [0.0] * n, [None] * n
+    busy = {e: [] for e in "VSTGYX"}
+    line_up = sorted((rank[k], k) for k in range(n) if not missing[k])
+    while line_up:
+        k = line_up.pop(0)[1]
+        o = ops[k]
+        lead = o["dur"] - o["issue"] if backward else 0.0
+        best = None
+        for e in (fixed[k] if fixed else "SV" if "alt" in o else o["eng"]):
+            t, line = ready[k] + lead, busy[e]
+            lo, hi = 0, len(line)
+            while lo < hi:
+                mid = (lo + hi) // 2
+                if line[mid][1] <= t:
+                    lo = mid + 1
+                else:
+                    hi = mid
+            while lo < len(line) and line[lo][0] < t + o["issue"] - 1e-9:
+                t = max(t, line[lo][1])
+                lo += 1
+            t += TUNE["lean"] if e == "V" and "alt" in o else 0.0
+            if best is None or t < best[0]:
+                best = (t, e, lo)
+        t, e, lo = best
+        t -= TUNE["lean"] if e == "V" and "alt" in o else 0.0
+        busy[e].insert(lo, (t, t + o["issue"]))
+        start[k], where[k] = t - lead, e
+        for u in after[k]:
+            gap = LAT if (k in ops[u]["deps"] or u in o["deps"]) else 0.0
+            ready[u] = max(ready[u], start[k] + o["dur"] + gap)
+            missing[u] -= 1
+            if not missing[u]:
+                x, lo, hi = (rank[u], u), 0, len(line_up)
+                while lo < hi:
+                    mid = (lo + hi) // 2
+                    if line_up[mid] < x:
+                        lo = mid + 1
+                    else:
+                        hi = mid
+                line_up.insert(lo, x)
+    return start, where
+
+
+def refine(ops):
+    n = len(ops)
+    before = [o["deps"] | o["order"] for o in ops]
+    after = [set() for _ in range(n)]
+    for k in range(n):
+        for d in before[k]:
+            after[d].add(k)
+    if TUNE["seed_greedy"]:
+        rank = [0.0] * n
+        for place, (k, _) in enumerate(schedule(ops)):
+            rank[k] = place
+    else:
+        level = [0.0] * n
+        for k in range(n - 1, -1, -1):
+            level[k] = ops[k]["dur"] + max([level[u] + LAT for u in after[k]] or [0.0])
+        rank = [-level[k] - ops[k]["bias"] for k in range(n)]
+    state = [TUNE["seed"]]
+
+    def draw():
+        state[0] = (state[0] * 1103515245 + 12345) % 2147483648
+        return state[0] / 2147483648.0
+
+    best = None
+    for turn in range(TUNE["turns"]):
+        if turn:
+            start, size = best[1], TUNE["shake"] * draw()
+            lo = draw() * best[3]
+            hi = lo + TUNE["span"] * (0.3 + draw())
+            rank = [start[k] + (size * (draw() - 0.5) if lo <= start[k] < hi else 0.0) for k in range(n)]
+        for _ in range(TUNE["passes"] if turn == 0 else 2):
+            start, where = pack(ops, before, rank, None, False)
+            order = [(k, where[k]) for k in sorted(range(n), key=lambda k: (start[k], k))]
+            ends = [replay(ops, order, case) for case in CASES]
+            if best is None or sum(ends) < best[0]:
+                best = (sum(ends), start, order, ends[0])
+            back, _ = pack(ops, after, [-start[k] - ops[k]["dur"] for k in range(n)], None, True)
+            rank = [-back[k] - ops[k]["dur"] for k in range(n)]
+    return best[2]
+
+
+def replay(ops, order, case):
+    free, end, wake, last = {}, [0.0] * len(ops), LAT * case["w"], 0.0
+    for k, e in order:
+        o = ops[k]
+        t = free.get(e, 0.0)
+        for d in o["deps"]:
+            if end[d] + wake > t:
+                t = end[d] + wake
+        for d in o["order"]:
+            if end[d] > t:
+                t = end[d]
+        f = case[o["cls"]]
+        free[e] = t + o["issue"] * f
+        end[k] = t + o["dur"] * f
+        if end[k] > last:
+            last = end[k]
+    return last * case["weight"]
+
+
+def emit(g, T, ops, order):
+    queue = {"V": g.vector, "S": g.scalar, "T": g.tensor, "G": g, "Y": g.sync}
+    total, seen, dmas = {"sent": 0}, {}, [0]
+    for k, e in order:
+        o = ops[k]
+        if o["kind"] == "x":
+            o["done"] = (o["sem"], o["count"])
+            total[o["sem"]] = o["count"]
+            continue
+        if "alt" in o:
+            o["fn"] = o["alt"][e][0]
+        need = {}
+        for d in o["deps"]:
+            s, c = ops[d]["done"]
+            need[s] = max(need.get(s, 0), c)
+        for s, c in need.items():
+            if seen.get((e, s), 0) < c:
+                queue[e].wait_ge(T.sem[s], c)
+                seen[(e, s)] = c
+        made = o["fn"]()
+        if o["kind"] == "r":
+            total["sent"] += o["count"]
+            continue
+        if o["kind"] == "d":
+            s, step = "d%d" % dmas[0], 16
+            dmas[0] += 1
+        else:
+            s, step = "e" + e, 1
+        for ins in made:
+            ins.then_inc(T.sem[s], step)
+            total[s] = total.get(s, 0) + step
+        o["done"] = (s, total[s])
+    for s, c in total.items():
+        if seen.get(("G", s), 0) < c:
+            g.wait_ge(T.sem[s], c)
+
+
+def rank_program(g, core, T, topo):
+    if T.rank_of(core) is None:
+        return
+    ops = build(g, core, T, topo)
+    dependencies(ops)
+    key = str(TUNE)
+    if key not in ORDER:
+        ORDER[key] = refine(ops) if TUNE["passes"] else schedule(ops)
+    emit(g, T, ops, ORDER[key])

@@ -6,7 +6,11 @@ V = 2048
 BIG = 8192.0
 CUT = 8.5 * BIG
 HI = 6144.0
+FAR = 1.0e6
+LN2 = math.log(2.0)
 BF, F32, F16, I32, U16 = "bfloat16", "float32", "float16", "int32", "uint16"
+TW = 512
+NG = V // TW
 
 
 def _sb(n, d):
@@ -14,48 +18,50 @@ def _sb(n, d):
 
 
 SCRATCH = {
-    "W0": _sb(4096, F32), "W1": _sb(4096, F32), "G0": _sb(V, F32), "CM0": _sb(V, BF), "CM1": _sb(V, BF),
-    "PN": _sb(V, F16), "DA": _sb(V, BF), "DB": _sb(V, BF), "S0": _sb(V, F16), "S1": _sb(V, F32),
-    "E": _sb(V, BF), "F": _sb(V, BF), "ZF": _sb(V, F32), "H": _sb(V, BF), "H32": _sb(V, BF), "HP": _sb(4096, BF),
-    "X": _sb(V, F32), "XR": _sb(4096, F32), "T1A": _sb(V, F16), "T1B": _sb(V, F16), "T2A": _sb(V, BF),
+    "W0": _sb(2 * V, F32), "W1": _sb(2 * V, F32), "CM0": _sb(V, BF), "CM1": _sb(V, BF), "PN": _sb(V, F16),
+    "PN0": _sb(V, F16), "TM": _sb(V, F16), "DA": _sb(V, BF), "DB": _sb(V, BF), "DL": _sb(V, BF), "E": _sb(V, BF),
+    "H": _sb(V, BF), "HW": _sb(2 * V, BF), "dH": ("dram", [128, V], F32),
+    "X": _sb(V, F32), "XR": _sb(V, F32), "XS": _sb(V, F32), "T1A": _sb(V, F16), "T1B": _sb(V, F16), "T2A": _sb(V, BF),
     "T2B": _sb(V, BF), "T3A": _sb(V, BF), "T3B": _sb(V, BF), "AB": _sb(V, BF), "EX": _sb(5120, F32),
-    "CW": _sb(V, BF), "YA": _sb(V, BF), "YB": _sb(V, BF), "SEL": _sb(2560, BF), "UNW": _sb(V, BF),
-    "EN": _sb(V, BF), "DLT": _sb(256, BF), "DL": _sb(1024, BF), "DN": _sb(128, BF), "IH": _sb(512, F32),
-    "COL": _sb(8, F32), "IT": _sb(512, BF),
+    "YA": _sb(V, BF), "YB": _sb(V, BF), "THR": _sb(V, BF), "SEL": _sb(2560, BF), "SELW": _sb(2560, BF),
+    "UNW": _sb(V, BF), "EN": _sb(V, BF), "GD": _sb(V, F32), "DLT": _sb(256, BF), "DH": _sb(512, BF), "DN": _sb(128, BF),
+    "IH": _sb(512, F32), "COL": _sb(8, F32), "IT": _sb(512, BF),
     "LI": _sb(256, I32), "ZI": _sb(128, I32), "ZC": _sb(128, F16), "AB16": _sb(256, U16), "INV": _sb(256, U16),
-    "AP": _sb(128, F32), "BP": _sb(128, F32), "LX": _sb(128, F32), "LY": _sb(128, F32), "LS": _sb(13 * 128, U16),
-    "SG": _sb(4 * 128, BF), "MW": _sb(128, BF), "CC": _sb(128, BF), "UB": _sb(256, BF), "UW": _sb(512, BF),
-    "RU": _sb(256, BF), "ADW": _sb(128, BF),
+    "AP": _sb(128, F32), "BP": _sb(128, F32), "VP": _sb(128, F32), "LX": _sb(384, F32), "LY": _sb(128, F32),
+    "LZ": _sb(256, I32), "LS": _sb(13 * 128, U16), "LP": _sb(13 * 128, U16),
+    "SG": _sb(4 * 128, BF), "MW": _sb(128, BF), "CC": _sb(128, BF), "MM": _sb(384, BF), "UW": _sb(512, BF),
+    "RU": _sb(256, BF), "ADW": _sb(128, BF), "TI": _sb(512, I32), "TJ": _sb(512, I32), "IA": _sb(128, BF),
+    "IB": _sb(128, F32), "SC": _sb(128, BF), "PW": _sb(128, BF), "C16": _sb(128, BF), "POW": _sb(2, BF),
     "DJ": _sb(128, F32), "GJ": _sb(256, F32), "J16": _sb(16, F32), "PI": _sb(4, I32), "PF": _sb(8, F32),
-    "MK": _sb(16, F32), "BLK": _sb(160, BF), "II": _sb(256, BF), "NII": _sb(256, BF), "I32M": _sb(128, BF),
-    "N32M": _sb(128, BF), "N2M": _sb(128, BF), "GD": _sb(V, F32), "DD": _sb(V, BF), "WIN": _sb(256, BF), "M1": _sb(128, BF), "M2": _sb(128, BF),
+    "MK": _sb(16, F32), "MK4": _sb(16, F32), "BLK": _sb(160, BF), "II": _sb(256, BF), "NID": _sb(128, BF),
+    "N32M": _sb(128, BF), "N2M": _sb(128, BF), "WIN": _sb(256, BF), "M1": _sb(256, BF),
+    "M2": _sb(256, BF),
     "stL": ("dram", [4, 128, 64], I32), "lnL": ("dram", [4, 128, 64], I32),
     "stZ": ("dram", [4, 128, 32], I32), "lnZ": ("dram", [4, 128, 32], I32),
     "stH": ("dram", [4, 128, 512], BF), "lnH": ("dram", [4, 128, 512], BF),
     "stP": ("dram", [4, 128, 512], BF), "lnP": ("dram", [4, 128, 512], BF),
     "stE": ("dram", [4, 128, 512], BF), "lnE": ("dram", [4, 128, 512], BF),
-    "stG": ("dram", [16, 128, 128], F32), "lnG": ("dram", [16, 128, 128], F32),
+    "stN": ("dram", [4, 128, 512], BF), "lnN": ("dram", [4, 128, 512], BF),
+    "stG": ("dram", [4 * NG, 128, TW // 4], F32), "lnG": ("dram", [4 * NG, 128, TW // 4], F32),
 }
-PSUM = ["P0", "P1", "P2", "P3", "Q0", "Q1", "R0", "R1"]
+PSUM = {"P": 2048, "Q": 1024, "R": 1024}
 for _n in PSUM:
-    SCRATCH[_n] = ("psum", [128, 512], F32)
+    SCRATCH[_n] = ("psum", [128, PSUM[_n]], F32)
 
 N_DMA_SEMS = 110
 SEMAPHORES = ["eV", "eS", "eT", "eG", "sent"] + ["rx%d" % k for k in range(13)] + ["d%d" % k for k in range(N_DMA_SEMS)]
 
-CY, PCY, GA, LAT = 0.00104, 0.00052, 1.55, 0.10
-ALL, NONE = (0, 1, 2, 3), ()
+CY, PCY, GA, LAT = 0.00083, 0.00042, 1.56, 0.10
 ORDER = {}
-N_EX = 10
-TUNE = {"wide": 512, "cut_y": [(0, 512), (512, 1024), (1024, 1536), (1536, 2048)], "cut_cm": [1, 1, 1, 1], "cut_pn": [1, 1, 1, 1], "sg": 0.0, "list": [0.0, 0.0],
-        "ya": ["****"] * 4, "yb": ["****"] * 4, "cw": ["****"] * 4, "skew": 1.25, "x1": "VVVV",
-        "x2": "****", "t3": "****", "zf": "*", "v_w0": 1, "tol": 0.3, "urgent": 1.0, "hops": 2, "later": [0.0, 0.0, 0.0, 0.0], "acc": 3.0,
-        "v_abs": [[NONE], [NONE] * 4, [NONE], [NONE, ALL, NONE, NONE]], "early": 0.0,
-        "passes": 6, "seed_greedy": True, "lean": 0.0, "seed": 2, "turns": 40, "shake": 2.0, "span": 100.0}
+SIDE = ("X", "XR", "XS", "T1A", "T1B", "T2A", "T2B", "T3A", "T3B", "AB", "EX", "GD", "WIN", "LZ", "LP", "stG", "H32")
+N_EX = 5120 // TW
+TUNE = {"pieces": [(1024, 2048), (512, 1024), (0, 512)], "cmp": 512, "last": 256, "help": [[1, 0], [1, 0], [1, 0], [1, 0]],
+        "lean": 0.3, "early": 0.5, "side": 0.0, "walk": 512, "wide": 1024, "zf": 1024, "v_abs": [[], [], [], [1]], "skew": 1.25, "acc": 3.0,
+        "passes": 4, "seed": 2, "turns": 8, "shake": 2.0, "span": 100.0}
 CASES = [{"g": 1.0, "c": 1.0, "p": 1.0, "d": 1.0, "w": 1.0, "weight": 1.0},
-         {"g": 0.72, "c": 1.0, "p": 1.0, "d": 1.2, "w": 1.5, "weight": 0.6},
-         {"g": 1.3, "c": 1.0, "p": 0.9, "d": 1.0, "w": 1.0, "weight": 0.4},
-         {"g": 1.0, "c": 1.0, "p": 1.5, "d": 1.3, "w": 2.0, "weight": 0.4}]
+         {"g": 0.9, "c": 1.2, "p": 1.2, "d": 1.2, "w": 1.5, "weight": 0.5},
+         {"g": 1.7, "c": 1.3, "p": 1.3, "d": 1.0, "w": 1.0, "weight": 0.4},
+         {"g": 1.25, "c": 1.25, "p": 1.6, "d": 1.3, "w": 2.0, "weight": 0.4}]
 
 
 def split_engines(topo, src, dsts):
@@ -85,9 +91,10 @@ def build(g, core, T, topo):
     bias = [0.0]
 
     def add(eng, fn, rd, wr, dur, kind="c", issue=None, after=None, acc=False, sem=None, count=0):
-        listed = any(x[0] in ("AB16", "INV", "LS") for x in rd)
+        listed = any(x[0] in ("AB16", "INV", "LS", "LP") for x in rd)
         cls = "p" if eng == "T" else "d" if kind != "c" else "g" if listed else "c"
-        ops.append({"cls": cls, "eng": eng, "fn": fn, "rd": rd, "wr": wr, "dur": dur, "kind": kind, "acc": acc, "bias": bias[0],
+        ops.append({"cls": cls, "eng": eng, "fn": fn, "rd": rd, "wr": wr, "dur": dur, "kind": kind, "acc": acc,
+                    "bias": bias[0] - (TUNE["side"] if any(x[0] in SIDE for x in wr + rd) else 0.0),
                     "issue": dur if issue is None else issue, "after": after, "sem": sem, "count": count})
         return len(ops) - 1
 
@@ -129,10 +136,10 @@ def build(g, core, T, topo):
         f = GA if lst else (0.5 if two(o) and two(a) else 1.0)
         add("V", lambda: [g.vector.tensor_copy(ap(o), src(a, lst))], cols(a, lst), [o], 0.06 + max(64, n * f) * CY)
 
-    def s_act(o, a, func, bias=0.0, scale=1.0, lst=None):
+    def s_act(o, a, func, bias=0.0, scale=1.0, lst=None, after=None):
         n = width(o)
         add("S", lambda: [g.scalar.activation(ap(o), src(a, lst), func, bias=val(bias), scale=val(scale))],
-            cols(a, bias, scale, lst), [o], 0.07 + max(64, n * (GA if lst else 1.0)) * CY)
+            cols(a, bias, scale, lst), [o], 0.075 + max(64, n * (GA if lst else 1.0)) * CY, after=after)
 
     def either(on_v, on_s):
         on_s()
@@ -153,19 +160,19 @@ def build(g, core, T, topo):
             done = []
             for k, (o, l, r, st, sp) in enumerate(mms):
                 ins = g.tensor.matmul(ap(o), ap(l), ap(r), st, sp)
-                if sp or k == len(mms) - 1:
+                if k == len(mms) - 1:
                     done.append(ins)
             return done
-        cyc = sum(max(64, width(m[2])) * (4 if SCRATCH[m[2][0]][2] == F32 else 1) for m in mms)
-        add("T", fn, [m[1] for m in mms] + [m[2] for m in mms], [(mms[0][0][0], 0, 512)], 0.06 + cyc * PCY, acc=acc)
+        cyc = sum(max(64, width(m[2])) for m in mms)
+        add("T", fn, [m[1] for m in mms] + [m[2] for m in mms], [mms[0][0]], 0.06 + cyc * PCY, acc=acc)
 
-    def group(o, pairs):
-        return [(o, l, r, k == 0, k == len(pairs) - 1) for k, (l, r) in enumerate(pairs)]
+    def group(o, pairs, first=True, last=True):
+        return [(o, l, r, first and k == 0, last and k == len(pairs) - 1) for k, (l, r) in enumerate(pairs)]
 
     def dma(eng, pairs, rd, wr, dur, **kw):
         queue = {"Y": g.sync, "S": g.scalar, "G": g}[eng]
-        add(eng, lambda: [queue.dma_start(o, i, **kw) for o, i in pairs], rd, wr, dur, kind="d",
-            issue=(0.9 if eng == "G" else 0.06) * len(pairs))
+        return add(eng, lambda: [queue.dma_start(o, i, **kw) for o, i in pairs], rd, wr, dur, kind="d",
+                   issue=(0.9 if eng == "G" else 0.06) * len(pairs))
 
     def send(k, plan, rd, wr, dur):
         masks = split_engines(topo, core, [cores[r] for r, _, _ in plan])
@@ -189,15 +196,19 @@ def build(g, core, T, topo):
     def ch(name, k, n=512, base=0):
         return (name, base + k * n, base + (k + 1) * n)
 
-    def lst(name, base, k, n=32):
-        return (name, base + k * n, base + (k + 1) * n)
+    def part(name, lo, hi, base=0):
+        return (name, base + lo, base + hi)
 
-    ID, ROT, NID, NROT = ("II", 0, 128), ("II", 96, 224), ("NII", 0, 128), ("NII", 96, 224)
+    def lst(name, base, lo, hi):
+        return (name, base + lo // 16, base + hi // 16)
 
-    BACK = ("II", 32, 160)
+    def cut(lo, hi, n):
+        return [(a, min(a + n, hi)) for a in range(lo, hi, n)][::-1]
 
-    def sel(i, turn=0):
-        return ("SEL", 160 * i + 32 * turn, 160 * i + 32 * turn + 128)
+    ID, ROT, NID, N2 = ("II", 0, 128), ("II", 96, 224), ("NID", 0, 128), ("N2M", 0, 128)
+
+    def sel(i, turn=0, name="SEL"):
+        return (name, 160 * i + 32 * turn, 160 * i + 32 * turn + 128)
 
     def unw(i):
         return ("UNW", 128 * i, 128 * i + 128)
@@ -216,7 +227,7 @@ def build(g, core, T, topo):
         small = SCRATCH[o[0]][2] != I32
         add("G", lambda: [g.iota(ap(o), pat, base, cm, allow_small_or_imprecise_dtypes=small)], [], [o], 0.13 + 2 * width(o) * CY)
 
-    def send_input(k, nm, dur):
+    def exchange(k, nm, dur):
         send(k, [(r, T["st" + nm][r], T["ln" + nm][q]) for r in others], [("st" + nm, 0, 4)],
              [("ln" + nm, r, r + 1) for r in others], dur)
 
@@ -226,25 +237,25 @@ def build(g, core, T, topo):
     iota(("GJ", 0, 256), [[0, 2], [1, 8], [0, 16]], 0, 0)
     iota(("IH", 0, 256), [[1, 32], [0, 8]], 0, 0)
     iota(("IH", 256, 512), [[0, 32], [1, 8]], 0, 0)
-    send_input(0, "L", 1.1)
-    send_input(1, "H", 4.4)
+    exchange(0, "L", 1.1)
+    exchange(1, "H", 4.4)
     iota(("DJ", 0, 128), [[1, 128]], 0, -1)
-    send_input(2, "P", 4.4)
-    send_input(3, "E", 4.4)
-    send_input(4, "Z", 3.0)
+    exchange(2, "P", 4.4)
+    exchange(3, "E", 4.4)
+    exchange(4, "Z", 1.0)
+    iota(("VP", 0, 128), [[16, 128]], int(CUT), 0)
+    dma("G", [(T.W0[:, V:2 * V], T.lnP[:])], [("lnP", 0, 4)], [("W0", V, 2 * V)], 4.0)
     line = [k for k in range(first_g, len(ops)) if ops[k]["eng"] == "G"]
     for a, b in zip(line, line[1:]):
         ops[b]["after"] = a
-    dma("Y", [(T.EN[:], T.toll[:])], [("lnZ", 0, 4)], [("EN", 0, V)], 3.0)
     dma("Y", [(T.LI[:, 0:128], T.lnL[:, 0:64, :]), (T.LI[:, 128:256], T.lnL[:, 64:128, :])], [("lnL", 0, 4)], [("LI", 0, 256)], 2.2)
-    dma("Y", [(T.H[:], T.lnH[:]), (T.HP[32:128, 0:V], T.lnH[0:3]), (T.HP[0:32, 0:V], T.lnH[3])], [("lnH", 0, 4)],
-        [("H", 0, V), ("HP", 0, V)], 3.5)
-    dma("Y", [(T.F[:], T.lnP[:])], [("lnP", 0, 4)], [("F", 0, V)], 2.8)
+    dma("Y", [(T.HW[32:128, V:2 * V], T.lnH[0:3]), (T.HW[0:32, V:2 * V], T.lnH[3])], [("lnH", 0, 4)], [("HW", V, 2 * V)], 3.2)
+    dma("S", [(T.H[:], T.lnH[:])], [("lnH", 0, 4)], [("H", 0, V)], 3.2)
     dma("Y", [(T.E[:], T.lnE[:])], [("lnE", 0, 4)], [("E", 0, V)], 2.8)
     dma("Y", [(T.ZI[:], T.lnZ[:])], [("lnZ", 0, 4)], [("ZI", 0, 128)], 2.2)
-    dma("Y", [(T.HP[32:128, V:2 * V], T.lnH[0:3]), (T.HP[0:32, V:2 * V], T.lnH[3])], [("lnH", 0, 4)], [("HP", V, 2 * V)], 3.0)
 
     add("V", lambda: [g.vector.memset(T.SEL[:], 0.0)], [], [("SEL", 0, 2560)], 0.06 + 1280 * CY)
+    add("V", lambda: [g.vector.memset(T.C16[:], 65536.0)], [], [("C16", 0, 128)], 0.12)
     v_ts(("PI", 1, 2), ("PI", 0, 1), 4, A.arith_shift_right)
     v_ts(("PI", 2, 3), ("PI", 0, 1), 15, A.bitwise_and)
     v_ts(("PI", 3, 4), ("PI", 0, 1), 4, A.arith_shift_right, 1, A.bitwise_and)
@@ -266,118 +277,172 @@ def build(g, core, T, topo):
     for k in range(4):
         if k:
             v_ts(ch("CM0", k), ch("CM0", 0), ("COL", k, k + 1), A.add)
-        s_act(ch("G0", k), ch("CM0", 0), F.Identity, bias=("COL", 4 + k, 5 + k))
-
-    v_cp(("AB16", 0, 256), ("LI", 0, 256))
-    add("V", lambda: [g.vector.tensor_copy(T.CW[:].indirect(T.AB16[:, 0:128]), T.CM0[:])],
-        [("CM0", 0, V), ("AB16", 0, 128)], [("CW", 0, V)], 3.5 * V * CY)
-    add("S", lambda: [g.scalar.activation(T.W1[:, V:2 * V].indirect(T.AB16[:, 128:256]), T.G0[:], F.Silu)],
-        [("G0", 0, V), ("AB16", 128, 256)], [("W1", V, 2 * V)], 1.3 + 3.5 * V * CY)
-    for s, R in enumerate(("CW", "CM1")):
-        for hf in range(2):
-            bank = "Q%d" % hf
-            if s:
-                s_act(ch(R, hf, 1024), ch("W1", hf, 1024, V), F.Identity, bias=-32.0)
-            pe(group((bank, 0, 64), [(sel(i), (R, 1024 * hf + i, 1024 * hf + 1024, 16)) for i in range(16)]))
-            v_ts(("INV", 128 * s + 64 * hf, 128 * s + 64 * hf + 64), (bank, 0, 64), 1.0 / BIG, A.mult, 0.25, A.add)
-    v_ts(("AP", 0, 128), ("LI", 0, 128), CUT, A.add)
-    v_ts(("BP", 0, 128), ("LI", 128, 256), CUT + V, A.add)
-    v_ts(("NII", 0, 256), ("II", 0, 256), -1.0, A.mult)
+        s_act(ch("X", k), ch("CM0", 0), F.Identity, bias=("COL", 4 + k, 5 + k))
+    v_ts(("NID", 0, 128), ID, -1.0, A.mult)
+    v_ts(("MK4", 0, 16), ("MK", 0, 16), 4.0, A.mult)
     for i in range(16):
-        either(lambda: v_ts(unw(i), ("BLK", 0, 128), ("MK", i, i + 1), A.mult),
-               lambda: s_act(unw(i), ("BLK", 0, 128), F.Identity, scale=("MK", i, i + 1)))
+        either(lambda: v_ts(unw(i), ("BLK", 0, 128), ("MK4", i, i + 1), A.mult),
+               lambda: s_act(unw(i), ("BLK", 0, 128), F.Identity, scale=("MK4", i, i + 1)))
     v_ts(("PF", 4, 5), ("PF", 3, 4), -1.0, A.mult, 1.0, A.add)
+    v_ts(("PF", 7, 8), ("PF", 2, 3), 4.0, A.mult)
     v_ts(("M1", 0, 128), ("DJ", 0, 128), -16.0, A.is_equal, ("PF", 3, 4), A.mult)
     v_tt(("M1", 0, 128), ("M1", 0, 128), ID, A.add)
     v_tt(("M1", 0, 128), ("M1", 0, 128), ID, A.add)
+    v_cp(("M1", 128, 256), ("M1", 0, 128))
     v_ts(("M2", 0, 128), ("DJ", 0, 128), 16.0, A.is_equal, ("PF", 4, 5), A.mult)
-    v_ts(("I32M", 0, 128), ID, 1.0 / 32, A.mult)
+    v_cp(("M2", 128, 256), ("M2", 0, 128))
     v_ts(("N32M", 0, 128), ID, -1.0 / 32, A.mult)
     v_ts(("N2M", 0, 128), ID, -2.0, A.mult)
-    v_cp(("ZC", 0, 128), ("ZI", 0, 128))
+    v_ts(("VP", 0, 128), ("VP", 0, 128), ("PF", 2, 3), A.add)
+    v_ts(("ZC", 0, 128), ("ZI", 0, 128), 0.5, A.mult, 0.25, A.add)
 
-    for s, (D, Y) in enumerate((("DA", "YA"), ("DB", "YB"))):
-        for k in range(4):
-            v_tt(ch(Y, k), ("H", 0, V), ch("HP", k), A.subtract, lst=lst("INV", 128 * s, k))
-            s_act(ch(D, k), ch(Y, k), F.Abs)
-            bank = "P%d" % (2 * s + k % 2)
-            pe(group((bank, 0, 512), [(ID, ch("F", k)), (ID, ch(D, k))]))
-            cp("*", ch("W0", k, base=s * V), (bank, 0, 512))
-    for k in range(2):
-        v_ts(ch("H32", k, 1024), ch("H", k, 1024), 32.0, A.mult)
+    def votes(o, name, lo, hi):
+        pe(group(o, [(sel(i), (name, lo + i, hi, 16)) for i in range(16)]))
 
-    cur = [0]
-    steps = [0]
+    def compact(name, lo, hi, o, turn=0, first=True, last=True, weights="SEL"):
+        pairs = [(sel(i, turn, weights), (name, 128 * i, 128 * i + 128)) for i in range(lo // 128, hi // 128)]
+        pe(group(o, pairs, first, last), acc=not first)
 
-    def compare(want_list, lbase, cc):
-        W = "W%d" % cur[0]
-        CM = "CM%d" % (steps[0] % 2)
+    def spread(o, k, small, first, last):
+        return [((o[0], o[1] + 128 * j, o[1] + 128 * j + 128), unw(4 * k + j), small, first, last and (first or j == 3))
+                for j in range(4)]
+
+    def summed(o, k, pairs, small=None, last=True):
+        mm = group(o, [(l, ch(r, k)) for l, r in pairs], True, last and small is None)
+        return mm + (spread(o, k, small, not pairs, True) if small else [])
+
+    v_cp(("AB16", 0, 256), ("LI", 0, 256))
+    add("V", lambda: [g.vector.tensor_copy(T.YA[:].indirect(T.AB16[:, 0:128]), T.CM0[:])],
+        [("CM0", 0, V), ("AB16", 0, 128)], [("YA", 0, V)], 2.4 * GA * V * CY)
+    silu = add("S", lambda: [g.scalar.activation(T.W1[:, V:2 * V].indirect(T.AB16[:, 128:256]), T.X[:], F.Silu)],
+               [("X", 0, V), ("AB16", 128, 256)], [("W1", V, 2 * V)], 1.3 + 2.4 * GA * V * CY)
+    v_ts(("AP", 0, 128), ("LI", 0, 128), CUT, A.add)
+    v_ts(("BP", 0, 128), ("LI", 128, 256), CUT + V, A.add)
+    for hf in range(2):
+        either(lambda: v_ts(ch("CM1", hf, 1024), ch("W1", hf, 1024, V), -32.0, A.add),
+               lambda: s_act(ch("CM1", hf, 1024), ch("W1", hf, 1024, V), F.Identity, bias=-32.0))
+    for s, R in enumerate(("YA", "CM1")):
+        o = ("Q", 512 * s, 512 * s + 128)
+        votes(o, R, 0, V)
+        v_ts(ch("TI", s, 128), o, 1.0 / BIG, A.mult)
+        v_ts(ch("TJ", s, 128), ch("TI", s, 128), 127, A.bitwise_and)
+        v_cp(ch("INV", s, 128), ch("TJ", s, 128))
+        compact(R, 0, V, o, turn=s)
+        v_ts(ch("TI", 2 + s, 128), o, 1.0 / BIG, A.mult)
+        v_ts(ch("TJ", 2 + s, 128), ch("TI", 2 + s, 128), 7, A.arith_shift_right)
+        v_cp(("IB" if s else "IA", 0, 128), ch("TJ", 2 + s, 128))
+    for k in range(4):
+        pe(summed(ch("R", k % 2), k, [], ("IA", 0, 128)))
+        v_ts(ch("THR", k), ch("R", k % 2), ("PF", 7, 8), A.not_equal, FAR, A.mult)
+    s_act(("SC", 0, 128), ("IB", 0, 128), F.Exp, bias=-LN2, scale=-LN2)
+    s_act(("PW", 0, 128), ("IB", 0, 128), F.Exp, scale=LN2)
+    s_act(("POW", 0, 1), ("PF", 2, 3), F.Exp, bias=-math.log(BIG), scale=LN2, after=silu)
+    for hf in range(2):
+        v_ts(ch("SELW", hf, 1280), ch("SEL", hf, 1280), ("POW", 0, 1), A.mult)
+
+    for k in (3, 2, 1, 0):
+        cp("S", ch("HW", k), ("HW", V, 2 * V), lst=lst("AB16", 0, 512 * k, 512 * k + 512))
+        v_tt(ch("YB", k), ("HW", V, 2 * V), ch("H", k), A.subtract, lst=lst("AB16", 128, 512 * k, 512 * k + 512))
+        pe(summed(ch("P", k), k, [(ID, "HW"), (NID, "H")]))
+        s_act(ch("DA", k), ch("P", k), F.Abs)
+        s_act(ch("DB", k), ch("YB", k), F.Abs)
+        pe(summed(ch("P", k), k, [(ID, "DA"), (NID, "DB")]))
+        cp("*", ch("DL", k), ch("P", k))
+    dma("G", [(T.dH[:], T.HW[:, V:2 * V])], [("HW", V, 2 * V), ("W0", V, 2 * V)], [("dH", 0, 1)], 4.0)
+
+    cur, steps = [0], [0]
+
+    def make_list(CM, n, lo, hi, o, winners):
+        o, y = (o[0], o[1], o[1] + (hi - lo) // 16), lst("LX", 128 * (n % 3), lo, hi)
+        votes(o, CM, lo, hi)
+        v_tt(y, o, lst("BP", 0, lo, hi), A.min)
+        if winners:
+            v_tt(lst("LY", 0, lo, hi), y, lst("VP", 0, lo, hi), A.max)
+            v_ts(lst("LS", 128 * n, lo, hi), lst("LY", 0, lo, hi), -CUT - lo, A.add)
+
+    def predecessors(n):
+        v_tt(("LZ", 0, 128), ch("LX", n % 3, 128), ("AP", 0, 128), A.max)
+        v_ts(("LZ", 128, 256), ("LZ", 0, 128), V - 1, A.bitwise_and)
+        v_cp(ch("LP", n, 128), ("LZ", 128, 256))
+
+    def open_window(pairs, small=None):
+        for k in (3, 2, 1, 0):
+            mm = group(ch("P", k), [(l, ch(r, k)) for l, r in pairs], True, False)
+            pe(mm + (spread(ch("P", k), k, small, False, False) if small else []))
+
+    def close_window(k, name, small=None):
+        o = ch("P", k)
+        pe(spread(o, k, small, False, True) if small else group(o, [(ROT, ch(name, k))], False, True), acc=True)
+        cp("*", ch("W%d" % (1 - cur[0]), k, base=V), o)
+
+    def step(n, t, first, marks, PN):
+        W, CM = "W%d" % cur[0], "CM%d" % (steps[0] % 2)
         steps[0] += 1
-        for k in range(4):
-            n = TUNE["cut_cm"][k]
-            for j in range(n * k, n * k + n):
-                cp("S", ch("G0", j, 512 // n), (W, 0, V), lst=lst("AB16", 0, j, 32 // n))
-                v_tt(ch(CM, j, 512 // n), (W, V, 2 * V), ch("G0", j, 512 // n), A.is_lt, lst=lst("AB16", 128, j, 32 // n))
-            if want_list and k % 2 == 1:
-                make_list(CM, lbase, k // 2, "Q%d" % (k // 2))
-            if not want_list:
-                compact(CM, k, "Q0", 0)
-        return CM
-
-    def make_list(CM, lbase, hf, bank):
-        bias[0] = TUNE["list"][hf]
-        pe(group((bank, 0, 64), [(sel(i), (CM, 1024 * hf + i, 1024 * hf + 1024, 16)) for i in range(16)]))
-        v_tt(ch("LX", hf, 64), (bank, 0, 64), ch("AP", hf, 64), A.max)
-        v_tt(ch("LY", hf, 64), ch("LX", hf, 64), ch("BP", hf, 64), A.min)
-        v_ts(ch("LS", hf, 64, lbase), ch("LY", hf, 64), -CUT, A.add)
+        if t in (1, 2):
+            open_window([(ROT, "E"), (ROT, "DB")], marks)
+        if t == 3 and first:
+            CZ = "CM%d" % (steps[0] % 2)
+            steps[0] += 1
+            for k in (3, 2, 1, 0):
+                pe(group(ch("P", k), [(N2, ch("E", k)), (N2, ch("DB", k))], True, False) + spread(ch("P", k), k, ("ZC", 0, 128), False, False))
+        pieces = TUNE["pieces"]
+        helped = TUNE["help"][t]
+        bias[0] = TUNE["early"] * 4
+        for k in helped:
+            cp("S", ch("TM", k), (W, V, 2 * V), lst=lst("AB16", 0, 512 * k, 512 * k + 512))
+            pe(summed(ch("R", k % 2), k, [(ID, "TM")] + ([(ID, "DL")] if t else [(ID, "DA"), (NID, "DB")])))
+            cp("S", ch(W, k), ch("R", k % 2))
+        for j, (lo, hi) in enumerate(pieces):
+            bias[0] = TUNE["early"] * lo / 512
+            for a, b in cut(lo, hi, TUNE["cmp"]):
+                if a // 512 not in helped:
+                    v_tt(part(W, a, b), (W, V, 2 * V), part("DL", a, b), A.add, lst=lst("AB16", 0, a, b))
+                v_tt(part(CM, a, b), (W, V, 2 * V), part(W, a, b), A.is_lt, lst=lst("AB16", 128, a, b))
+                if t == 3:
+                    compact(CM, a, b, ("Q", 512, 640), first=b == V, last=a == 0)
+            if t == 3 and not first:
+                continue
+            make_list(CM, n, lo, hi, ("Q", 512 * (j % 2 if t < 3 else 0)), True)
+            for a, b in cut(lo, hi, 512):
+                for c, d in cut(a, b, TUNE["last"] if lo == 0 else 512):
+                    cp("*", part(PN, c, d), (W, lo, 2 * V), lst=lst("LS", 128 * n, c, d))
+                if t in (1, 2):
+                    close_window(a // 512, PN)
+                if t == 3:
+                    o = part("P", a, b)
+                    pe(group(o, [(N2, part(PN, a, b))], False, True), acc=True)
+                    either(lambda: v_ts(part(CZ, a, b), o, -1.0, A.max, 1.0, A.min), lambda: s_act(part(CZ, a, b), o, F.Sign))
+                    compact(CZ, a, b, ("R", 0, 128), first=b == V, last=a == 0)
         bias[0] = 0.0
+        sg = ch("SG", t, 128)
+        if t in (1, 2):
+            compact(CM, 0, V, ("Q", 512, 640))
+            cur[0] = 1 - cur[0]
+        if t:
+            either(lambda: v_ts(sg, ("Q", 512, 640), -1.0 / BIG, A.mult, 8.5, A.add),
+                   lambda: s_act(sg, ("Q", 512, 640), F.Identity, bias=8.5, scale=-1.0 / BIG))
+        if t == 3:
+            if first:
+                v_ts(("MW", 0, 128), ("R", 0, 128), -BIG, A.is_le)
+            v_tt(("CC", 0, 128), ("MW", 0, 128), sg, A.mult)
+            if not first:
+                make_list(CM, n, 0, V, ("P", 0), False)
+        if t > 1:
+            predecessors(n)
 
-    def compact(src_name, k, bank, turn, first=True, last=True):
-        mm = [((bank, 0, 128), sel(i, turn), (src_name, 128 * i, 128 * i + 128), first and i == 0, last and i == 15)
-              for i in range(4 * k, 4 * k + 4)]
-        pe(mm, acc=not (first and k == 0))
-
-    def signed(bank, col, eng):
-        if eng == "S":
-            s_act(("SG", 128 * col, 128 * col + 128), (bank, 0, 128), F.Identity, bias=8.5, scale=-1.0 / BIG)
-        else:
-            v_ts(("SG", 128 * col, 128 * col + 128), (bank, 0, 128), -1.0 / BIG, A.mult, 8.5, A.add)
-
-    def advance(f, lbase, Fname, PN="PN"):
-        W, Wn = "W%d" % cur[0], "W%d" % (1 - cur[0])
-        bare = Fname == "E"
-        pieces = [(j, 512 // n) for k, n in enumerate(TUNE["cut_pn"]) for j in range(n * k, n * k + n)]
-        for m, (j, n) in enumerate(pieces):
-            v_tt(ch(PN, j, n), (W, 0, 2 * V), ch(Fname, j, n), A.add, lst=lst("LS", lbase, j, n // 16))
-            a, b = ("P%d" % (2 * (m % 2)), 0, n), ("P%d" % (2 * (m % 2) + 1), 0, n)
-            pe(group(a, [(ROT, ch(PN, j, n))] + ([(ID, ch("DA", j, n))] if bare else [])))
-            cp("*", ch(Wn, j, n), a)
-            pe(group(b, [(ROT, ch(PN, j, n)), (ID, ch("DB" if bare else "DD", j, n))]))
-            cp("*", ch(Wn, j, n, V), b)
-        cur[0] = 1 - cur[0]
-
-    def spread(bank, k, small, plus=()):
-        mm = []
-        for j in range(4):
-            mm += group((bank, 128 * j, 128 * j + 128),
-                        [(l, ch(r, 4 * k + j, 128)) for l, r in plus] + [(unw(4 * k + j), small)])
-        pe(mm)
-
-    def bounds():
-        for k in range(4):
-            bank = "P%d" % k
-            spread(bank, k, ("ZC", 0, 128), [(NID, "E")])
-            cp(TUNE["zf"], ch("ZF", k), (bank, 0, 512))
+    def join_x():
+        dma("Y", [(T.XR[:, 0:V], T.dH[:])], [("dH", 0, 1)], [("XR", 0, V)], 4.0)
+        dma("G", [(T.XR[32:128, 0:V], T.YA[0:96, :]), (T.XR[0:32, 0:V], T.YA[96:128, :])], [("YA", 0, V)], [("XR", 0, V)], 9.0,
+            accum_op=A.add, max_dma_last_dim=4096)
 
     def turn_x():
-        dma("Y", [(T.XR[32:128, c:c + V], T.X[0:96, :]) for c in (0, V)] + [(T.XR[0:32, c:c + V], T.X[96:128, :]) for c in (0, V)],
-            [("X", 0, V)], [("XR", 0, 2 * V)], 9.0)
+        dma("Y", [(T.XS[32:128, :], T.X[0:96, :]), (T.XS[0:32, :], T.X[96:128, :])], [("X", 0, V)], [("XS", 0, V)], 6.0)
 
     terms, slots = [0], [0]
 
     def next_ex():
         slots[0] += 1
-        return ch("EX", slots[0] % N_EX)
+        return ch("EX", slots[0] % N_EX, TW)
 
     def stage(e, k, first=False):
         pair, wr = [(T.stG[4 * k:4 * k + 4], ap(e))], [("stG", 4 * k, 4 * k + 4)]
@@ -386,16 +451,25 @@ def build(g, core, T, topo):
         else:
             dma("G", pair, [e], wr, TUNE["acc"], accum_op=A.add, max_dma_last_dim=2048)
 
+    free = [ch("R", k, TW) for k in range(1024 // TW)]
+
+    def banks(n):
+        return free[n % len(free)]
+
+    def fill(o, k, pairs, small=None, last=True):
+        for j in range(TW // 512):
+            pe(summed(ch(o[0], j, base=o[1]), k * TW // 512 + j, pairs, small, last))
+
     def term(k, pairs, off, half, v_abs):
         n = terms[0]
         terms[0] += 1
         lnw = math.log(0.5) if half else 0.0
-        o = ("R%d" % (n % 2), 0, 512)
-        e, ab = next_ex(), ch("AB", n % 4)
-        pe(group(o, [(l, ch(r, k)) for l, r in pairs]))
-        if k in v_abs:
+        o, e, ab = banks(n), next_ex(), ch("AB", n % NG, TW)
+        fill(o, k, pairs)
+        if v_abs:
             v_ts(ab, o, -off, A.add, 0.0, A.max)
-            pe(group(o, [(l, ch(r, k)) for l, r in pairs] + [(("N2M", 0, 128), ab)]))
+            for j in range(TW // 512):
+                pe(group(ch(o[0], j, base=o[1]), [(l, ch(r, k * TW // 512 + j)) for l, r in pairs] + [(N2, ch("AB", j, base=ab[1]))]))
             s_act(e, o, F.Exp, bias=lnw - off / 8, scale=0.125)
         else:
             s_act(ab, o, F.Abs, bias=-off)
@@ -403,185 +477,125 @@ def build(g, core, T, topo):
         stage(e, k)
 
     def walk_back(f):
+        qa, qb = ("Q", 0, 128), ("Q", 512, 640)
         for t in (3, 2, 1):
-            for k in range(4):
-                bank = "P%d" % k
-                spread(bank, k, ("CC", 0, 128))
-                cp(TUNE["cw"][f][k], ch("CW", k), (bank, 0, 512))
-            bank = "Q%d" % (t % 2)
             if t == 1:
-                pe([((bank, 0, 128), ID, ("UB", 128, 256), True, False)])
-            for k in range(4):
-                for Y, base, sign in (("YA", 0, 1.0), ("YB", 128, -1.0)):
-                    for lo, hi in TUNE["cut_y"]:
-                        if lo // 512 == k:
-                            o, l = (Y, lo, hi), ("INV", base + lo // 16, base + hi // 16)
-                            either(lambda: v_ts(o, ("CW", 0, V), sign, A.mult, 0.0, A.max, lst=l),
-                                   lambda: s_act(o, ("CW", 0, V), F.Relu, scale=sign, lst=l))
-                compact("YA", k, bank, 1, first=t > 1, last=False)
-                compact("YB", k, bank, 1, first=False, last=True)
+                pe(group(qa, [(ID, ch("MM", 0, 128)), (ID, ch("MM", 1, 128))], True, False))
+            pe(group(qb, [(ID, ("C16", 0, 128)), (NID, ("PW", 0, 128))], True, False))
+            for a, b in cut(0, V, TUNE["walk"]):
+                v_tt(part("YA", a, b), ("CC", 0, 128), part("THR", a, b), A.is_gt, lst=lst("INV", 0, a, b))
+                s_act(part("YB", a, b), ("CC", 0, 128), F.Sign, bias=-0.25, scale=-1.0, lst=lst("INV", 128, a, b))
+                compact("YA", a, b, qa, 1, first=t > 1 and b == V, last=a == 0)
+                compact("YB", a, b, qb, 1, first=False, last=a == 0, weights="SELW")
+            m = ch("MM", 3 - t, 128)
+            v_tt(("TI", 0, 128), qb, ("SC", 0, 128), A.mult)
+            v_ts(("TJ", 0, 128), ("TI", 0, 128), 1, A.bitwise_and)
+            v_tt(m, qa, ("TJ", 0, 128), A.add)
             if t > 1:
-                v_tt(("CC", 0, 128), (bank, 0, 128), ("SG", 128 * (t - 1), 128 * t), A.mult)
-            if t == 3:
-                v_cp(("UB", 0, 128), (bank, 0, 128))
-            if t == 2:
-                v_tt(("UB", 128, 256), (bank, 0, 128), ("UB", 0, 128), A.add)
-            if t == 1:
-                v_ts(ch("UW", f, 128), (bank, 0, 128), 0.0, A.is_gt, 4.0, A.mult)
+                v_tt(("CC", 0, 128), m, ch("SG", t - 1, 128), A.mult)
+            else:
+                v_ts(ch("UW", f, 128), m, 0.0, A.is_gt)
 
-    def forest(f):
+    def forest(f, marks):
         first, last = f % 2 == 0, f == 3
         P = "A" if first else "B"
-        Fname = "E" if first else "F"
-        L = [128 * (3 * f + t) for t in range(4)]
-        for t in (1, 2):
-            CM = compare(True, L[t], t)
-            advance(f, L[t], Fname)
-            bias[0] = TUNE["sg"]
-            for k in range(4):
-                compact(CM, k, "Q1", 0)
-            signed("Q1", t, "S")
-            bias[0] = 0.0
-            n = TUNE["wide"]
-            for k in range(V // n):
-                if t == 1:
-                    v_tt(ch("X", k, n), ("HP", 0, 2 * V), ch("H32", k, n), A.add, lst=lst("LS", L[1], k, n // 16))
-                else:
-                    cp("*", ch("X", k, n), ("XR", 0, 2 * V), lst=lst("LS", L[2], k, n // 16))
-            turn_x()
-        CM = compare(first, L[3], 3)
-        if first:
-            W, CZ = "W%d" % cur[0], "CM%d" % (steps[0] % 2)
-            steps[0] += 1
-            for k in range(4):
-                compact(CM, k, "Q0", 0)
-            signed("Q0", 3, "S")
-            for k in range(4):
-                v_tt(ch(CZ, k), (W, 0, 2 * V), ch("ZF", k), A.is_gt, lst=lst("LS", L[3], k))
-                compact(CZ, k, "Q1", 0)
-            v_ts(("MW", 0, 128), ("Q1", 0, 128), CUT, A.is_ge)
-        else:
-            signed("Q0", 3, "V")
-        v_tt(("CC", 0, 128), ("MW", 0, 128), ("SG", 384, 512), A.mult)
-        if not first:
-            for hf in range(2):
-                make_list(CM, L[3], hf, "R%d" % hf)
+        wide = TUNE["wide"]
+        step(3 * f + 1, 1, first, marks, "PN")
+        for lo, hi in TUNE["pieces"]:
+            for a, b in cut(lo, hi, wide):
+                l = lst("LS", 128 * (3 * f + 1), a, b)
+                either(lambda: v_ts(part("YA", a, b), ("HW", lo, 2 * V), 32.0, A.mult, lst=l),
+                       lambda: s_act(part("YA", a, b), ("HW", lo, 2 * V), F.Identity, scale=32.0, lst=l))
+        join_x()
+        step(3 * f + 2, 2, first, marks, "PN")
+        for a, b in cut(0, V, wide):
+            cp("*", part("X", a, b), ("XR", 0, V), lst=lst("LP", 128 * (3 * f + 2), a, b))
+        turn_x()
+        step(3 * f + 3, 3, first, marks, "PN")
         walk_back(f)
-        bias[0] = -TUNE["later"][f]
-        n = 512 if last else TUNE["wide"]
-        for k in range(V // n):
-            cp("*", ch("T3" + P, k, n), ("HP", 0, 2 * V), lst=lst("LS", L[3], k, n // 16))
-            v_cp(ch("T1" + P, k, n), ("XR", 0, 2 * V), lst=lst("LS", L[3], k, n // 16))
-            v_ts(ch("T2" + P, k, n), ch("T1" + P, k, n), HI - 15.5, A.add)
-        v_ts(ch("WIN", min(f, 1), 128), ("SG", 384, 512), 0.0, A.is_lt, 1.0 if first else 0.5, A.mult)
+        for a, b in cut(0, V, TW if last else wide)[::-1]:
+            l = lst("LP", 128 * (3 * f + 3), a, b)
+            cp("*", part("T3" + P, a, b), ("HW", V, 2 * V), lst=l)
+            cp("*", part("T1" + P, a, b), ("XS", 0, V), lst=l)
+            either(lambda: v_ts(part("T2" + P, a, b), part("T1" + P, a, b), HI - 15.5, A.add),
+                   lambda: s_act(part("T2" + P, a, b), part("T1" + P, a, b), F.Identity, bias=HI - 15.5))
+        v_ts(ch("WIN", min(f, 1), 128), ch("SG", 3, 128), 0.0, A.is_lt, 0.25 if first else 0.125, A.mult)
         if f:
             v_tt(ch("WIN", 0, 128), ch("WIN", 0, 128), ch("WIN", 1, 128), A.add)
         if last:
-            for k in range(4):
-                bank, e = "R%d" % (k % 2), next_ex()
-                spread(bank, k, ch("WIN", 0, 128))
-                v_tt(e, (bank, 0, 512), ch("GD", k), A.mult)
+            free.extend(ch("P", k, TW) for k in range(NG))
+            for k in range(NG):
+                o, e = banks(k), next_ex()
+                fill(o, k, [], ch("WIN", 0, 128))
+                v_tt(e, o, ch("GD", k, TW), A.mult)
                 stage(e, k)
-        todo = []
-        if not first:
-            todo += [([(("I32M", 0, 128), "T2A"), (NID, "T3B")], HI / 32, False),
-                     ([(("I32M", 0, 128), "T2B"), (NID, "T3A")], HI / 32, True),
-                     ([(ID, "T1A"), (NID, "T2A"), (("N32M", 0, 128), "T2B")], -HI - HI / 32, False),
-                     ([(ID, "T1B"), (NID, "T2B"), (("N32M", 0, 128), "T2A")], -HI - HI / 32, True)]
+        if first:
+            return
+        todo = [([(ID, "T1B"), (NID, "T2B"), (NID, "T3A")], -HI, True),
+                ([(ID, "T1A"), (NID, "T2A"), (NID, "T3B")], -HI, False),
+                ([(ID, "T1B"), (NID, "T2B"), (("N32M", 0, 128), "T2A")], -HI - HI / 32, False),
+                ([(ID, "T1A"), (NID, "T2A"), (("N32M", 0, 128), "T2B")], -HI - HI / 32, True)]
         skew = TUNE["skew"] if last else 0.1
-        for _, j, k in sorted((j + skew * k, j, k) for j in range(len(todo)) for k in range(4)):
-            term(k, todo[j][0], todo[j][1], todo[j][2], TUNE["v_abs"][f][j])
-        bias[0] = 0.0
+        for _, j, k in sorted((j + skew * k, j, k) for j in range(4) for k in range(NG)):
+            term(k, todo[j][0], todo[j][1], todo[j][2], j in TUNE["v_abs"][f])
 
-    def new_tolls(bank, k, small, old, new):
-        spread(bank, k, small, [(ID, old)])
-        v_ts(ch(new, k), (bank, 0, 512), 0.0, A.max, 63.0, A.min)
+    def new_tolls(o, k, small, old, new):
+        pe(summed(o, k, [(ID, old)], small))
+        v_ts(ch(new, k), o, 0.0, A.max, 63.0, A.min)
 
-    def tolls_home(rnd, banks, new):
-        mine = ch("DLT", rnd, 128)
-        land = lambda r: ch("DL", 4 * rnd + r, 128)
-        send(7 + rnd, [(r, ap(mine), ap(land(q))) for r in others], [mine], [land(r) for r in others], 1.1)
-        tiles = [mine if r == q else land(r) for r in range(4)]
-        bank = banks[0]
-
-        def fn():
-            return [g.tensor.matmul(T[bank][32 * r:32 * r + 32, 0:128], T.II[:, 32 * q:32 * q + 32], ap(tiles[r]), True, True)
-                    for r in range(4)]
-        add("T", fn, tiles + [ID], [(bank, 0, 512)], 0.06 + 512 * PCY)
-        v_cp(("DN", 0, 128), (bank, 0, 128))
-        for k in range(4):
-            new_tolls(banks[(k + 1) % len(banks)], k, ("DN", 0, 128), "EN", new)
-
-    compare(True, 0, 0)
-    advance(0, 0, "E", "T1B")
-    for k in range(4):
-        bank = ("R%d" % (k % 2), 0, 512)
-        pe(group(bank, [(ID, ch("DB", k)), (NID, ch("DA", k))]))
-        cp("S", ch("DD", k), bank)
-    for k in range(4):
-        pe(group(("R0", 0, 512), [(ROT, ch("T1B", k)), (NROT, ch("E", k))]))
-        v_cp(ch("S0", k), ("R0", 0, 512))
-        pe(group(("R1", 0, 512), [(ROT, ch("T1B", k)), (NROT, ch("E", k)), (ID, ch("DD", k))]))
-        cp("S", ch("S1", k), ("R1", 0, 512))
-    bias[0] = -TUNE["early"]
-    for s, D in enumerate(("DA", "DB")):
-        for k in range(4):
-            s_act(ch("XR", k, base=s * V), ch(D, k), F.Exp, scale=-0.125)
-    for k in range(4):
+    step(0, 0, True, None, "PN0")
+    for k in range(NG):
         e = next_ex()
-        s_act(e, ("XR", 0, V), F.Identity, scale=3.0, lst=lst("AB16", 0, k))
+        s_act(e, ch("DA", k, TW), F.Exp, bias=math.log(3.0), scale=-0.125, after=silu)
         stage(e, k, True)
-        s_act(ch("GD", k), ("XR", V, 2 * V), F.Identity, lst=lst("AB16", 128, k))
-        e = next_ex()
-        s_act(e, ("XR", 0, V), F.Identity, scale=-1.0, lst=lst("AB16", 0, k))
-        dma("G", [(ap(ch("GD", k)), ap(e))], [e], [ch("GD", k)], TUNE["acc"], accum_op=A.add, max_dma_last_dim=2048)
-    bias[0] = 0.0
+        s_act(ch("GD", k, TW), ch("DB", k, TW), F.Exp, scale=-0.125, after=silu)
+        e2 = next_ex()
+        either(lambda: v_ts(e2, e, -1.0 / 3, A.mult), lambda: s_act(e2, e, F.Identity, scale=-1.0 / 3))
+        dma("G", [(ap(ch("GD", k, TW)), ap(e2))], [e2], [ch("GD", k, TW)], TUNE["acc"], accum_op=A.add, max_dma_last_dim=2048)
     for rnd in range(2):
         f = 2 * rnd
-        W = "W%d" % cur[0]
         if rnd:
             v_tt(ch("DLT", 0, 128), ch("UW", 0, 128), ch("UW", 1, 128), A.subtract)
-            tolls_home(0, ["R0", "R1"], "EN")
-            for k in range(4):
-                bank = "P%d" % k
-                new_tolls(bank, k, ch("DLT", 0, 128), "E", "E")
-                pe(group((bank, 0, 512), [(ROT, ch("E", k)), (ID, ch("DA", k))]))
-                v_tt(ch(W, k, base=V), (bank, 0, 512), ch("S1", k), A.add)
-                bank = "Q%d" % (k % 2)
-                pe(group((bank, 0, 512), [(ROT, ch("E", k)), (ID, ch("DA", k)), (ID, ch("S0", k))]))
-                s_act(ch(W, k), (bank, 0, 512), F.Identity)
-        bounds()
-        forest(f)
-        W = "W%d" % cur[0]
+            open_window([(ROT, "PN0"), (ROT, "DB")])
+            for k in (3, 2, 1, 0):
+                new_tolls(ch("Q", k % 2), k, ch("DLT", 0, 128), "E", "E")
+                close_window(k, "E")
+            dma("Y", [(T.stN[:], T.E[:])], [("E", 0, V)], [("stN", 0, 4)], 3.0)
+            exchange(7, "N", 4.4)
+            dma("Y", [(T.lnN[q], T.stN[q])], [("stN", 0, 4)], [("lnN", q, q + 1)], 2.4)
+            dma("Y", [(T.EN[:], T.lnN[:])], [("lnN", 0, 4)], [("EN", 0, V)], 3.0)
+        else:
+            open_window([(ROT, "E"), (ROT, "DB")])
+            for k in (3, 2, 1, 0):
+                close_window(k, "PN0")
+        cur[0] = 1 - cur[0]
+        forest(f, None)
         send(5 + rnd, [((q - 1) % 4, ap(ch("UW", f, 128)), ap(ch("RU", rnd, 128)))], [ch("UW", f, 128)], [ch("RU", rnd, 128)], 0.6)
-        pe(group(("Q0", 0, 128), [(("M1", 0, 128), ch("UW", f, 128)), (("M2", 0, 128), ch("RU", rnd, 128))]))
-        v_cp(("ADW", 0, 128), ("Q0", 0, 128))
-        for k in range(4):
-            bank = "P%d" % k
-            spread(bank, k, ("ADW", 0, 128), [(ID, "E"), (BACK, "DA")])
-            s_act(ch("F", k), (bank, 0, 512), F.Identity)
-            pe(group((bank, 0, 512), [(ROT, ch("F", k))]))
-            v_tt(ch(W, k, base=V), (bank, 0, 512), ch("S1", k), A.add)
-            if k < TUNE["v_w0"]:
-                v_tt(ch(W, k), (bank, 0, 512), ch("S0", k), A.add)
-            else:
-                bank = "Q%d" % (k % 2)
-                pe(group((bank, 0, 512), [(ROT, ch("F", k)), (ID, ch("S0", k))]))
-                cp("*", ch(W, k), (bank, 0, 512))
-        forest(f + 1)
+        open_window([(ROT, "PN0"), (ROT, "DB"), (ROT, "E")])
+        pe(group(("Q", 0, 128), [(("M1", 96, 224), ch("UW", f, 128)), (("M2", 96, 224), ch("RU", rnd, 128))]))
+        cp("*", ("ADW", 0, 128), ("Q", 0, 128))
+        for k in (3, 2, 1, 0):
+            close_window(k, None, ("ADW", 0, 128))
+        cur[0] = 1 - cur[0]
+        forest(f + 1, ("ADW", 0, 128))
 
-    v_tt(ch("DLT", 1, 128), ch("UW", 2, 128), ch("UW", 3, 128), A.subtract)
-    tolls_home(1, ["P0", "P1", "P2", "P3"], "G0")
+    mine = ch("DLT", 1, 128)
+    v_tt(mine, ch("UW", 2, 128), ch("UW", 3, 128), A.subtract)
+    send(8, [(r, ap(mine), ap(ch("DH", q, 128))) for r in others], [mine], [ch("DH", r, 128) for r in others], 1.1)
+    tiles = [mine if r == q else ch("DH", r, 128) for r in range(4)]
+    add("T", lambda: [[g.tensor.matmul(T.Q[32 * r:32 * r + 32, 0:128], T.II[:, 32 * q:32 * q + 32], ap(tiles[r]), True, True)
+                       for r in range(4)][-1]], tiles + [ID], [("Q", 0, 128)], 0.06 + 512 * PCY)
+    cp("*", ("DN", 0, 128), ("Q", 0, 128))
     for k in range(4):
-        part = slice(512 * k, 512 * k + 512)
-        dma("Y", [(T.tollout[:, part], ap(ch("G0", k)))], [ch("G0", k)], [], 2.5)
-    for k in range(4):
-        part = slice(512 * k, 512 * k + 512)
+        new_tolls(ch("P", k), k, ("DN", 0, 128), "EN", "W0")
+        dma("Y", [(T.tollout[:, 512 * k:512 * k + 512], ap(ch("W0", k)))], [ch("W0", k)], [], 2.5)
+    for k in range(NG):
         st = [("stG", 4 * k, 4 * k + 4)]
         send(9 + k, [(r, T.stG[4 * k + (r + 3) % 4], T.lnG[4 * k + q]) for r in others], st,
-             [("lnG", 4 * k + r, 4 * k + r + 1) for r in others], 2.2)
-        dma("Y", [(T.lnG[4 * k + q], T.stG[4 * k + (q + 3) % 4])], st, [("lnG", 4 * k + q, 4 * k + q + 1)], 2.4)
-        dma("Y", [(T.gain[:, part], T.lnG[4 * k:4 * k + 4])], [("lnG", 4 * k, 4 * k + 4)], [], 2.8)
+             [("lnG", 4 * k + r, 4 * k + r + 1) for r in others], 2.2 * TW / 512)
+        dma("Y", [(T.gain[rows, TW * k:TW * k + TW], T.stG[4 * k + (q + 3) % 4])], st, [], 2.4)
+        dma("Y", [(T.gain[32 * r:32 * r + 32, TW * k:TW * k + TW], T.lnG[4 * k + r]) for r in others],
+            [("lnG", 4 * k + r, 4 * k + r + 1) for r in others], [], 2.6)
     return ops
 
 
@@ -589,103 +603,28 @@ def dependencies(ops):
     log = {}
     for n, o in enumerate(ops):
         deps, order = set(), set()
-        touched = [(x, x[0] in PSUM) for x in o["rd"]] + [(x, True) for x in o["wr"]]
-        for x, w in touched:
-            lo, hi = (0, 512) if x[0] in PSUM else (x[1], x[2])
-            for (a, b, m, mw) in log.get(x[0], []):
+        touched = []
+        for x, w in [(x, x[0] in PSUM) for x in o["rd"]] + [(x, True) for x in o["wr"]]:
+            lo, hi = (x[1] // 512 * 512, (x[2] + 511) // 512 * 512) if x[0] in PSUM else (x[1], x[2])
+            touched.append((x[0], lo, hi, w))
+        for name, lo, hi, w in touched:
+            for (a, b, m, mw) in log.get(name, []):
                 if a < hi and lo < b and (w or mw) and m != n:
-                    if o["acc"] and x[0] in PSUM and ops[m]["eng"] == "T":
+                    if o["acc"] and name in PSUM and ops[m]["eng"] == "T":
                         order.add(m)
                     else:
                         deps.add(m)
-        for x, w in touched:
-            lo, hi = (0, 512) if x[0] in PSUM else (x[1], x[2])
-            old = log.get(x[0], [])
+        for name, lo, hi, w in touched:
+            old = log.get(name, [])
             if w:
                 old = [e for e in old if not (lo <= e[0] and e[1] <= hi)]
-            log[x[0]] = old + [(lo, hi, n, w)]
+            log[name] = old + [(lo, hi, n, w)]
         if o["after"] is not None:
             order.add(o["after"])
         o["deps"], o["order"] = deps, order - deps
 
 
-def schedule(ops):
-    n = len(ops)
-    users = [[] for _ in range(n)]
-    for k, o in enumerate(ops):
-        for d in o["deps"] | o["order"]:
-            users[d].append(k)
-    level = [0.0] * n
-    for k in range(n - 1, -1, -1):
-        level[k] = ops[k]["dur"] + max([level[u] + LAT for u in users[k]] or [0.0])
-    level = [level[k] + ops[k]["bias"] for k in range(n)]
-    missing = [len(o["deps"] | o["order"]) for o in ops]
-    ready = [0.0] * n
-    pool = {e: [] for e in "VSTGYX"}
-    free = {e: 0.0 for e in pool}
-    placed = [False] * n
-    hold = {e: 0.0 for e in pool}
-    tol, urgent = TUNE["tol"], TUNE["urgent"]
-
-    def engines(k):
-        return "VS" if "alt" in ops[k] else ops[k]["eng"]
-
-    def enter(k):
-        for e in engines(k):
-            pool[e].append(k)
-
-    def soonest(k, depth):
-        t = ready[k]
-        if missing[k]:
-            if depth == 0:
-                return 1e9
-            for d in ops[k]["deps"] | ops[k]["order"]:
-                if not placed[d]:
-                    t = max(t, max(soonest(d, depth - 1), min(free[x] for x in engines(d))) + ops[d]["dur"] + LAT)
-        return t
-
-    for k in range(n):
-        if not missing[k]:
-            enter(k)
-    out = []
-    while len(out) < n:
-        best = None
-        for e in pool:
-            if pool[e]:
-                t = max(free[e], hold[e], min(ready[k] for k in pool[e]))
-                if best is None or t < best[0]:
-                    best = (t, e)
-        t, e = best
-        now = [k for k in pool[e] if ready[k] <= t]
-        k = max(now, key=lambda j: (level[j], -j))
-        if e in "VST":
-            near = set(pool[e])
-            rim = set(j for x in pool for j in pool[x] if level[j] > level[k] + urgent)
-            for _ in range(TUNE["hops"]):
-                rim = set(u for j in rim for u in users[j] if level[u] > level[k] + urgent)
-                near |= rim
-            due = [soonest(j, TUNE["hops"]) for j in near if ops[j]["eng"] == e and "alt" not in ops[j] and level[j] > level[k] + urgent]
-            due = [x for x in due if x > t]
-            if due and min(due) < t + ops[k]["issue"] - tol:
-                fit = [j for j in now if t + ops[j]["issue"] - tol <= min(due)]
-                if not fit:
-                    hold[e] = min(min(due), t + 0.1)
-                    continue
-                k = max(fit, key=lambda j: (level[j], -j))
-        for x in engines(k):
-            pool[x].remove(k)
-        placed[k] = True
-        free[e] = t + ops[k]["issue"]
-        out.append((k, e))
-        for u in users[k]:
-            ready[u] = max(ready[u], t + ops[k]["dur"] + (LAT if k in ops[u]["deps"] else 0.0))
-            missing[u] -= 1
-            if not missing[u]:
-                enter(u)
-    return out
-
-
-def pack(ops, before, rank, fixed, backward):
+def pack(ops, before, rank, backward):
     n = len(ops)
     after = [[] for _ in range(n)]
     for k in range(n):
@@ -700,8 +639,10 @@ def pack(ops, before, rank, fixed, backward):
         o = ops[k]
         lead = o["dur"] - o["issue"] if backward else 0.0
         best = None
-        for e in (fixed[k] if fixed else "SV" if "alt" in o else o["eng"]):
+        for e in ("SV" if "alt" in o else o["eng"]):
             t, line = ready[k] + lead, busy[e]
+            if "alt" in o:
+                o["dur"] = o["issue"] = o["alt"][e][1]
             lo, hi = 0, len(line)
             while lo < hi:
                 mid = (lo + hi) // 2
@@ -712,11 +653,12 @@ def pack(ops, before, rank, fixed, backward):
             while lo < len(line) and line[lo][0] < t + o["issue"] - 1e-9:
                 t = max(t, line[lo][1])
                 lo += 1
-            t += TUNE["lean"] if e == "V" and "alt" in o else 0.0
-            if best is None or t < best[0]:
-                best = (t, e, lo)
-        t, e, lo = best
-        t -= TUNE["lean"] if e == "V" and "alt" in o else 0.0
+            end = t + o["issue"] + (TUNE["lean"] if e == "V" else 0.0)
+            if best is None or end < best[0]:
+                best = (end, t, e, lo)
+        _, t, e, lo = best
+        if "alt" in o:
+            o["dur"] = o["issue"] = o["alt"][e][1]
         busy[e].insert(lo, (t, t + o["issue"]))
         start[k], where[k] = t - lead, e
         for u in after[k]:
@@ -742,15 +684,10 @@ def refine(ops):
     for k in range(n):
         for d in before[k]:
             after[d].add(k)
-    if TUNE["seed_greedy"]:
-        rank = [0.0] * n
-        for place, (k, _) in enumerate(schedule(ops)):
-            rank[k] = place
-    else:
-        level = [0.0] * n
-        for k in range(n - 1, -1, -1):
-            level[k] = ops[k]["dur"] + max([level[u] + LAT for u in after[k]] or [0.0])
-        rank = [-level[k] - ops[k]["bias"] for k in range(n)]
+    level = [0.0] * n
+    for k in range(n - 1, -1, -1):
+        level[k] = ops[k]["dur"] + max([level[u] + LAT for u in after[k]] or [0.0])
+    rank = [-level[k] - ops[k]["bias"] for k in range(n)]
     state = [TUNE["seed"]]
 
     def draw():
@@ -765,13 +702,14 @@ def refine(ops):
             hi = lo + TUNE["span"] * (0.3 + draw())
             rank = [start[k] + (size * (draw() - 0.5) if lo <= start[k] < hi else 0.0) for k in range(n)]
         for _ in range(TUNE["passes"] if turn == 0 else 2):
-            start, where = pack(ops, before, rank, None, False)
+            start, where = pack(ops, before, rank, False)
             order = [(k, where[k]) for k in sorted(range(n), key=lambda k: (start[k], k))]
             ends = [replay(ops, order, case) for case in CASES]
             if best is None or sum(ends) < best[0]:
                 best = (sum(ends), start, order, ends[0])
-            back, _ = pack(ops, after, [-start[k] - ops[k]["dur"] for k in range(n)], None, True)
+            back, _ = pack(ops, after, [-start[k] - ops[k]["dur"] for k in range(n)], True)
             rank = [-back[k] - ops[k]["dur"] for k in range(n)]
+    ORDER["end"] = best[3]
     return best[2]
 
 
@@ -787,8 +725,9 @@ def replay(ops, order, case):
             if end[d] > t:
                 t = end[d]
         f = case[o["cls"]]
-        free[e] = t + o["issue"] * f
-        end[k] = t + o["dur"] * f
+        issue, dur = (o["alt"][e][1],) * 2 if "alt" in o else (o["issue"], o["dur"])
+        free[e] = t + issue * f
+        end[k] = t + dur * f
         if end[k] > last:
             last = end[k]
     return last * case["weight"]
@@ -838,5 +777,5 @@ def rank_program(g, core, T, topo):
     dependencies(ops)
     key = str(TUNE)
     if key not in ORDER:
-        ORDER[key] = refine(ops) if TUNE["passes"] else schedule(ops)
+        ORDER[key] = refine(ops)
     emit(g, T, ops, ORDER[key])

@@ -9,8 +9,7 @@ HI = 6144.0
 FAR = 1.0e6
 LN2 = math.log(2.0)
 BF, F32, F16, I32, U16 = "bfloat16", "float32", "float16", "int32", "uint16"
-TW = 512
-NG = V // TW
+GAIN = [(0, 512), (512, 1024), (1024, 1536), (1536, 2048)]
 
 
 def _sb(n, d):
@@ -22,17 +21,17 @@ SCRATCH = {
     "PN0": _sb(V, F16), "TM": _sb(V, F16), "DA": _sb(V, BF), "DB": _sb(V, BF), "DL": _sb(V, BF), "E": _sb(V, BF),
     "H": _sb(V, BF), "HW": _sb(2 * V, BF), "dH": ("dram", [128, V], F32),
     "X": _sb(V, F32), "XR": _sb(V, F32), "XS": _sb(V, F32), "T1A": _sb(V, F16), "T1B": _sb(V, F16), "T2A": _sb(V, BF),
-    "T2B": _sb(V, BF), "T3A": _sb(V, BF), "T3B": _sb(V, BF), "AB": _sb(V, BF), "EX": _sb(5120, F32),
-    "YA": _sb(V, BF), "YB": _sb(V, BF), "THR": _sb(V, BF), "SEL": _sb(2560, BF), "SELW": _sb(2560, BF),
+    "T2B": _sb(V, BF), "T3A": _sb(V, BF), "T3B": _sb(V, BF), "AB": _sb(V, BF), "EX": _sb(7168, F32),
+    "YA": _sb(V, BF), "YB": _sb(V, BF), "THR": _sb(2560, BF), "SEL": _sb(2560, BF), "SELW": _sb(2560, BF),
     "UNW": _sb(V, BF), "EN": _sb(V, BF), "GD": _sb(V, F32), "DLT": _sb(256, BF), "DH": _sb(512, BF), "DN": _sb(128, BF),
-    "IH": _sb(512, F32), "COL": _sb(8, F32), "IT": _sb(512, BF),
+    "IH": _sb(256, F32),
     "LI": _sb(256, I32), "ZI": _sb(128, I32), "ZC": _sb(128, F16), "AB16": _sb(256, U16), "INV": _sb(256, U16),
     "AP": _sb(128, F32), "BP": _sb(128, F32), "VP": _sb(128, F32), "LX": _sb(384, F32), "LY": _sb(128, F32),
     "LZ": _sb(256, I32), "LS": _sb(13 * 128, U16), "LP": _sb(13 * 128, U16),
     "SG": _sb(4 * 128, BF), "MW": _sb(128, BF), "CC": _sb(128, BF), "MM": _sb(384, BF), "UW": _sb(512, BF),
     "RU": _sb(256, BF), "ADW": _sb(128, BF), "TI": _sb(512, I32), "TJ": _sb(512, I32), "IA": _sb(128, BF),
-    "IB": _sb(128, F32), "SC": _sb(128, BF), "PW": _sb(128, BF), "C16": _sb(128, BF), "POW": _sb(2, BF),
-    "DJ": _sb(128, F32), "GJ": _sb(256, F32), "J16": _sb(16, F32), "PI": _sb(4, I32), "PF": _sb(8, F32),
+    "IB": _sb(128, F32), "SP": _sb(256, BF), "C16": _sb(256, BF), "POW": _sb(2, BF),
+    "DJ": _sb(128, F32), "GJ": _sb(256, F32), "J16": _sb(16, F32), "PI": _sb(4, I32), "PF": _sb(12, F32),
     "MK": _sb(16, F32), "MK4": _sb(16, F32), "BLK": _sb(160, BF), "II": _sb(256, BF), "NID": _sb(128, BF),
     "N32M": _sb(128, BF), "N2M": _sb(128, BF), "WIN": _sb(256, BF), "M1": _sb(256, BF),
     "M2": _sb(256, BF),
@@ -41,26 +40,30 @@ SCRATCH = {
     "stH": ("dram", [4, 128, 512], BF), "lnH": ("dram", [4, 128, 512], BF),
     "stP": ("dram", [4, 128, 512], BF), "lnP": ("dram", [4, 128, 512], BF),
     "stE": ("dram", [4, 128, 512], BF), "lnE": ("dram", [4, 128, 512], BF),
+    "stT": ("dram", [4, 128, 640], BF), "lnT": ("dram", [4, 128, 640], BF),
     "stN": ("dram", [4, 128, 512], BF), "lnN": ("dram", [4, 128, 512], BF),
-    "stG": ("dram", [4 * NG, 128, TW // 4], F32), "lnG": ("dram", [4 * NG, 128, TW // 4], F32),
 }
+for _p, (_lo, _hi) in enumerate(GAIN):
+    SCRATCH["stG%d" % _p] = SCRATCH["lnG%d" % _p] = ("dram", [4, 128, (_hi - _lo) // 4], F32)
 PSUM = {"P": 2048, "Q": 1024, "R": 1024}
 for _n in PSUM:
     SCRATCH[_n] = ("psum", [128, PSUM[_n]], F32)
 
 N_DMA_SEMS = 110
-SEMAPHORES = ["eV", "eS", "eT", "eG", "sent"] + ["rx%d" % k for k in range(13)] + ["d%d" % k for k in range(N_DMA_SEMS)]
+SEMAPHORES = ["eV", "eS", "eT", "eG", "sent"] + ["rx%d" % k for k in range(14)] + ["d%d" % k for k in range(N_DMA_SEMS)]
 
-CY, PCY, GA, LAT = 0.00083, 0.00042, 1.56, 0.10
+CY, PCY, GA, LAT = 0.00083, 0.00045, 1.56, 0.09
 ORDER = {}
+QUEUES = "VSTGYXZ"
 SIDE = ("X", "XR", "XS", "T1A", "T1B", "T2A", "T2B", "T3A", "T3B", "AB", "EX", "GD", "WIN", "LZ", "LP", "stG", "H32")
-N_EX = 5120 // TW
-TUNE = {"pieces": [(1024, 2048), (512, 1024), (0, 512)], "cmp": 512, "last": 256, "help": [[1, 0], [1, 0], [1, 0], [1, 0]],
-        "lean": 0.3, "early": 0.5, "side": 0.0, "walk": 512, "wide": 1024, "zf": 1024, "v_abs": [[], [], [], [1]], "skew": 1.25, "acc": 3.0,
-        "passes": 4, "seed": 2, "turns": 8, "shake": 2.0, "span": 100.0}
+TUNE = {"pieces": [(1024, 2048), (0, 1024)], "cmp": 512, "last": 256,
+        "help": [[1, 0]] + [[1, 0], [1, 0], [0], [1, 0], [1, 0], [1, 0]] * 2,
+        "pull": 0.5, "any": 0.5, "cases": 3, "moves": 5000, "far": 12, "slack": 0.0, "lend": [], "own": 0.0, "urgent": 1.0, "hops": 1, "share": 0.6, "lean": 0.3, "early": 0.0, "side": 0.0, "walk": [(1536, 2048), (1024, 1536), (512, 1024), (0, 512)],
+        "join": 1024, "lent": 512, "with": 4, "back": True, "pace": [1, 5, 11], "t2": [0, 1, 2, 3], "v_db": [], "wide": 512, "v_abs": [[], [], [], []], "skew": 5.0, "acc": 0.9,
+        "passes": 4, "seed": 2, "turns": 1, "shake": 2.0, "span": 100.0}
 CASES = [{"g": 1.0, "c": 1.0, "p": 1.0, "d": 1.0, "w": 1.0, "weight": 1.0},
-         {"g": 0.9, "c": 1.2, "p": 1.2, "d": 1.2, "w": 1.5, "weight": 0.5},
-         {"g": 1.7, "c": 1.3, "p": 1.3, "d": 1.0, "w": 1.0, "weight": 0.4},
+         {"g": 0.9, "c": 1.1, "p": 1.2, "d": 1.5, "w": 1.5, "weight": 0.6},
+         {"g": 1.6, "c": 1.3, "p": 1.3, "d": 1.0, "w": 1.0, "weight": 0.5},
          {"g": 1.25, "c": 1.25, "p": 1.6, "d": 1.3, "w": 2.0, "weight": 0.4}]
 
 
@@ -73,7 +76,7 @@ def split_engines(topo, src, dsts):
             continue
         pool = [e for e in topo.engines(src, group[0]) if e not in used]
         n = 1
-        while 2 * n * len(group) <= len(pool):
+        while 2 * n * len(group) <= len(pool) and (not out or n < min(m for _, m in out.values())):
             n *= 2
         for k, d in enumerate(group):
             mine = pool[k * n:(k + 1) * n]
@@ -172,7 +175,7 @@ def build(g, core, T, topo):
     def dma(eng, pairs, rd, wr, dur, **kw):
         queue = {"Y": g.sync, "S": g.scalar, "G": g}[eng]
         return add(eng, lambda: [queue.dma_start(o, i, **kw) for o, i in pairs], rd, wr, dur, kind="d",
-                   issue=(0.9 if eng == "G" else 0.06) * len(pairs))
+                   issue=(1.3 if eng == "G" else 0.06) * len(pairs))
 
     def send(k, plan, rd, wr, dur):
         masks = split_engines(topo, core, [cores[r] for r, _, _ in plan])
@@ -191,7 +194,15 @@ def build(g, core, T, topo):
         for r, _, _ in plan:
             s = (2 * q - r) % 4
             got += split_engines(topo, cores[s], [cores[(s + x - q) % 4] for x, _, _ in plan])[core][1]
-        add("X", None, [], wr, dur + 2.3, kind="x", issue=dur, after=me, sem="rx%d" % k, count=got)
+        link = add("X", None, [], [("link", 0, 1)] * (k < 5), dur, kind="x", after=me, sem="rx%d" % k, count=got)
+        add("Z", None, [], wr, 2.6, kind="x", issue=0.0, after=link, sem="rx%d" % k, count=got)
+        return me
+
+    def in_line(begin, engines="VS"):
+        for e in engines:
+            line = [k for k in range(begin, len(ops)) if ops[k]["eng"] == e and "alt" not in ops[k] and ops[k]["kind"] == "c"]
+            for a, b in zip(line, line[1:]):
+                ops[b]["after"] = a
 
     def ch(name, k, n=512, base=0):
         return (name, base + k * n, base + (k + 1) * n)
@@ -215,13 +226,17 @@ def build(g, core, T, topo):
 
     rows = slice(32 * q, 32 * q + 32)
     dma("Y", [(T.stL[:, 0:64, :], T.sa[:]), (T.stL[:, 64:128, :], T.sb[:])], [], [("stL", 0, 4)], 2.2)
-    dma("S", [(T.stH[:], T.hf[:])], [], [("stH", 0, 4)], 2.8)
+    dma("S", [(T.TI[:, 0:128], T.sa[:]), (T.TI[:, 128:256], T.sb[:])], [], [("TI", 0, 256)], 2.4)
+    ops[-1]["bias"] = 50.0
+    dma("Y", [(T.stH[:], T.hf[:])], [], [("stH", 0, 4)], 2.8)
+    ops[-1]["bias"] = 50.0
     dma("S", [(T.lnL[q, 0:64, :], T.sa[rows]), (T.lnL[q, 64:128, :], T.sb[rows])], [], [("lnL", q, q + 1)], 2.2)
-    dma("Y", [(T.stP[:], T.p0[:])], [], [("stP", 0, 4)], 2.8)
-    dma("Y", [(T.stE[:], T.toll[:])], [], [("stE", 0, 4)], 3.0)
-    dma("Y", [(T.stZ[:], T.lim[:])], [], [("stZ", 0, 4)], 2.6)
+    later = [("stH", 0, 4)]
+    dma("Y", [(T.stP[:], T.p0[:])], later, [("stP", 0, 4)], 2.8)
+    dma("Y", [(T.stE[:], T.toll[:])], later, [("stE", 0, 4)], 3.0)
+    dma("Y", [(T.stZ[:], T.lim[:])], later, [("stZ", 0, 4)], 2.6)
     dma("Y", [(T.lnH[q], T.hf[rows]), (T.lnP[q], T.p0[rows]), (T.lnE[q], T.toll[rows]), (T.lnZ[q], T.lim[2 * q:2 * q + 2])],
-        [], [("lnH", q, q + 1), ("lnP", q, q + 1), ("lnE", q, q + 1), ("lnZ", q, q + 1)], 3.0)
+        later, [("lnH", q, q + 1), ("lnP", q, q + 1), ("lnE", q, q + 1), ("lnZ", q, q + 1)], 3.0)
 
     def iota(o, pat, base, cm):
         small = SCRATCH[o[0]][2] != I32
@@ -233,68 +248,62 @@ def build(g, core, T, topo):
 
     first_g = len(ops)
     iota(("PI", 0, 1), [[0, 1]], 0, 1)
+    iota(ch("X", 0), [[1, 512]], 32, 0)
     iota(("J16", 0, 16), [[1, 16]], 0, 0)
     iota(("GJ", 0, 256), [[0, 2], [1, 8], [0, 16]], 0, 0)
-    iota(("IH", 0, 256), [[1, 32], [0, 8]], 0, 0)
-    iota(("IH", 256, 512), [[0, 32], [1, 8]], 0, 0)
-    exchange(0, "L", 1.1)
-    exchange(1, "H", 4.4)
     iota(("DJ", 0, 128), [[1, 128]], 0, -1)
-    exchange(2, "P", 4.4)
-    exchange(3, "E", 4.4)
-    exchange(4, "Z", 1.0)
     iota(("VP", 0, 128), [[16, 128]], int(CUT), 0)
-    dma("G", [(T.W0[:, V:2 * V], T.lnP[:])], [("lnP", 0, 4)], [("W0", V, 2 * V)], 4.0)
+    exchange(0, "L", 1.3)
+    ops[-3]["dur"] = ops[-3]["issue"] = 5.5
+    exchange(1, "H", 5.4)
+    exchange(2, "P", 5.4)
+    exchange(3, "E", 5.4)
+    exchange(4, "Z", 1.0)
     line = [k for k in range(first_g, len(ops)) if ops[k]["eng"] == "G"]
     for a, b in zip(line, line[1:]):
         ops[b]["after"] = a
+    dma("Y", [(T.T3A[:], T.lnP[:])], [("lnP", 0, 4)], [("T3A", 0, V)], 3.2)
+    dma("G", [(T.W0[:, V:2 * V], T.T3A[:])], [("T3A", 0, V)], [("W0", V, 2 * V)], 5.0)
+    ops[-1]["after"] = line[-1]
     dma("Y", [(T.LI[:, 0:128], T.lnL[:, 0:64, :]), (T.LI[:, 128:256], T.lnL[:, 64:128, :])], [("lnL", 0, 4)], [("LI", 0, 256)], 2.2)
-    dma("Y", [(T.HW[32:128, V:2 * V], T.lnH[0:3]), (T.HW[0:32, V:2 * V], T.lnH[3])], [("lnH", 0, 4)], [("HW", V, 2 * V)], 3.2)
-    dma("S", [(T.H[:], T.lnH[:])], [("lnH", 0, 4)], [("H", 0, V)], 3.2)
+    dma("Y", [(T.HW[32:128, V:2 * V], T.lnH[0:3]), (T.HW[0:32, V:2 * V], T.lnH[3])], [("lnH", 0, 4)], [("HW", V, 2 * V)], 3.6)
+    dma("Y", [(T.H[:], T.lnH[:])], [("lnH", 0, 4)], [("H", 0, V)], 3.8)
     dma("Y", [(T.E[:], T.lnE[:])], [("lnE", 0, 4)], [("E", 0, V)], 2.8)
     dma("Y", [(T.ZI[:], T.lnZ[:])], [("lnZ", 0, 4)], [("ZI", 0, 128)], 2.2)
 
+    begin = len(ops)
     add("V", lambda: [g.vector.memset(T.SEL[:], 0.0)], [], [("SEL", 0, 2560)], 0.06 + 1280 * CY)
-    add("V", lambda: [g.vector.memset(T.C16[:], 65536.0)], [], [("C16", 0, 128)], 0.12)
     v_ts(("PI", 1, 2), ("PI", 0, 1), 4, A.arith_shift_right)
     v_ts(("PI", 2, 3), ("PI", 0, 1), 15, A.bitwise_and)
     v_ts(("PI", 3, 4), ("PI", 0, 1), 4, A.arith_shift_right, 1, A.bitwise_and)
     v_cp(("PF", 0, 4), ("PI", 0, 4))
-    v_ts(("BLK", 0, 160), ("GJ", 0, 160), ("PF", 1, 2), A.is_equal)
-    for i in range(16):
-        v_ts(("SEL", 160 * i + i, 160 * i + 160, 16), ("BLK", i, 160, 16), BIG, A.mult)
-    v_ts(("II", 0, 128), ("DJ", 0, 128), 0.0, A.is_equal)
-    v_ts(("II", 128, 256), ("DJ", 0, 128), 0.0, A.is_equal)
     v_ts(("MK", 0, 16), ("J16", 0, 16), ("PF", 2, 3), A.is_equal)
-    v_ts(("PF", 5, 6), ("PF", 2, 3), 8.0, A.is_lt)
-    v_ts(("COL", 0, 4), ("J16", 0, 4), ("PF", 5, 6), A.mult, 64.0, A.mult)
-    v_ts(("COL", 4, 8), ("COL", 0, 4), 32.0, A.add)
-    v_ts(("PF", 6, 7), ("PF", 5, 6), 32.0, A.mult)
-    v_ts(("IT", 0, 256), ("IH", 0, 256), ("PF", 5, 6), A.mult)
-    v_ts(("IT", 256, 512), ("IH", 256, 512), ("MK", 8, 9), A.mult)
-    v_tt(("CM0", 0, 256), ("IT", 0, 256), ("IT", 256, 512), A.add)
-    v_ts(("CM0", 256, 512), ("CM0", 0, 256), ("PF", 6, 7), A.add)
-    for k in range(4):
-        if k:
-            v_ts(ch("CM0", k), ch("CM0", 0), ("COL", k, k + 1), A.add)
-        s_act(ch("X", k), ch("CM0", 0), F.Identity, bias=("COL", 4 + k, 5 + k))
-    v_ts(("NID", 0, 128), ID, -1.0, A.mult)
     v_ts(("MK4", 0, 16), ("MK", 0, 16), 4.0, A.mult)
-    for i in range(16):
-        either(lambda: v_ts(unw(i), ("BLK", 0, 128), ("MK4", i, i + 1), A.mult),
-               lambda: s_act(unw(i), ("BLK", 0, 128), F.Identity, scale=("MK4", i, i + 1)))
-    v_ts(("PF", 4, 5), ("PF", 3, 4), -1.0, A.mult, 1.0, A.add)
-    v_ts(("PF", 7, 8), ("PF", 2, 3), 4.0, A.mult)
-    v_ts(("M1", 0, 128), ("DJ", 0, 128), -16.0, A.is_equal, ("PF", 3, 4), A.mult)
-    v_tt(("M1", 0, 128), ("M1", 0, 128), ID, A.add)
-    v_tt(("M1", 0, 128), ("M1", 0, 128), ID, A.add)
-    v_cp(("M1", 128, 256), ("M1", 0, 128))
-    v_ts(("M2", 0, 128), ("DJ", 0, 128), 16.0, A.is_equal, ("PF", 4, 5), A.mult)
-    v_cp(("M2", 128, 256), ("M2", 0, 128))
-    v_ts(("N32M", 0, 128), ID, -1.0 / 32, A.mult)
-    v_ts(("N2M", 0, 128), ID, -2.0, A.mult)
-    v_ts(("VP", 0, 128), ("VP", 0, 128), ("PF", 2, 3), A.add)
-    v_ts(("ZC", 0, 128), ("ZI", 0, 128), 0.5, A.mult, 0.25, A.add)
+    v_ts(("BLK", 0, 160), ("GJ", 0, 160), ("PF", 1, 2), A.is_equal)
+    for k in (1, 2, 3):
+        s_act(ch("X", k), ch("X", 0), F.Identity, bias=512.0 * k)
+
+    def matrices():
+        for i in range(16):
+            v_ts(("SEL", 160 * i + i, 160 * i + 160, 16), ("BLK", i, 160, 16), BIG, A.mult)
+        v_ts(("II", 0, 128), ("DJ", 0, 128), 0.0, A.is_equal)
+        v_ts(("II", 128, 256), ("DJ", 0, 128), 0.0, A.is_equal)
+        v_ts(("NID", 0, 128), ID, -1.0, A.mult)
+        v_ts(("PF", 7, 8), ("PF", 2, 3), 4.0, A.mult)
+        v_ts(("VP", 0, 128), ("VP", 0, 128), ("PF", 2, 3), A.add)
+        v_ts(("N2M", 0, 128), ID, -2.0, A.mult)
+
+    def more_matrices():
+        add("V", lambda: [g.vector.memset(T.C16[:, 0:128], 65536.0)], [], [("C16", 0, 128)], 0.12)
+        v_ts(("PF", 4, 5), ("PF", 3, 4), -1.0, A.mult, 1.0, A.add)
+        v_ts(("PF", 8, 9), ("PF", 2, 3), TUNE["lent"] / 128, A.is_ge)
+        v_ts(("M1", 0, 128), ("DJ", 0, 128), -16.0, A.is_equal, ("PF", 3, 4), A.mult)
+        v_ts(("M2", 0, 128), ("DJ", 0, 128), 16.0, A.is_equal, ("PF", 4, 5), A.mult)
+        v_ts(("C16", 128, 256), ("C16", 0, 128), ("PF", 8, 9), A.mult, 1.0, A.max)
+        v_tt(("M1", 0, 128), ("M1", 0, 128), N2, A.subtract)
+        v_cp(("M2", 128, 256), ("M2", 0, 128))
+        v_ts(("N32M", 0, 128), ID, -1.0 / 32, A.mult)
+        v_cp(("M1", 128, 256), ("M1", 0, 128))
 
     def votes(o, name, lo, hi):
         pe(group(o, [(sel(i), (name, lo + i, hi, 16)) for i in range(16)]))
@@ -311,44 +320,69 @@ def build(g, core, T, topo):
         mm = group(o, [(l, ch(r, k)) for l, r in pairs], True, last and small is None)
         return mm + (spread(o, k, small, not pairs, True) if small else [])
 
+    v_cp(("INV", 0, 256), ("TI", 0, 256))
+    add("V", lambda: [g.vector.tensor_copy(T.W1[:, 0:V].indirect(T.INV[:, 0:128]), T.X[:])],
+        [("X", 0, V), ("INV", 0, 128)], [("W1", 0, V)], 2.4 * GA * V * CY)
+    silu = add("S", lambda: [g.scalar.activation(T.W1[:, V:2 * V].indirect(T.INV[:, 128:256]), T.X[:], F.Silu)],
+               [("X", 0, V), ("INV", 128, 256)], [("W1", V, 2 * V)], 1.3 + 2.4 * GA * V * CY)
+    v_ts(("TM", 0, V), ("W1", 0, V), -32.0, A.add)
+    s_act(("PN", 0, V), ("W1", V, 2 * V), F.Identity, bias=-32.0)
+    matrices()
+    for i in range(16):
+        s_act(unw(i), ("BLK", 0, 128), F.Identity, scale=("MK4", i, i + 1))
+    for s, R in enumerate(("TM", "PN")):
+        o = ("Q", 512 * s, 512 * s + 256)
+        votes((o[0], o[1], o[1] + 128), R, 0, V)
+        compact(R, 0, V, (o[0], o[1] + 128, o[2]))
+    s_act(("POW", 0, 1), ("PF", 2, 3), F.Exp, bias=-math.log(BIG), scale=LN2)
+    more_matrices()
     v_cp(("AB16", 0, 256), ("LI", 0, 256))
-    add("V", lambda: [g.vector.tensor_copy(T.YA[:].indirect(T.AB16[:, 0:128]), T.CM0[:])],
-        [("CM0", 0, V), ("AB16", 0, 128)], [("YA", 0, V)], 2.4 * GA * V * CY)
-    silu = add("S", lambda: [g.scalar.activation(T.W1[:, V:2 * V].indirect(T.AB16[:, 128:256]), T.X[:], F.Silu)],
-               [("X", 0, V), ("AB16", 128, 256)], [("W1", V, 2 * V)], 1.3 + 2.4 * GA * V * CY)
-    v_ts(("AP", 0, 128), ("LI", 0, 128), CUT, A.add)
-    v_ts(("BP", 0, 128), ("LI", 128, 256), CUT + V, A.add)
-    for hf in range(2):
-        either(lambda: v_ts(ch("CM1", hf, 1024), ch("W1", hf, 1024, V), -32.0, A.add),
-               lambda: s_act(ch("CM1", hf, 1024), ch("W1", hf, 1024, V), F.Identity, bias=-32.0))
-    for s, R in enumerate(("YA", "CM1")):
-        o = ("Q", 512 * s, 512 * s + 128)
-        votes(o, R, 0, V)
-        v_ts(ch("TI", s, 128), o, 1.0 / BIG, A.mult)
-        v_ts(ch("TJ", s, 128), ch("TI", s, 128), 127, A.bitwise_and)
-        v_cp(ch("INV", s, 128), ch("TJ", s, 128))
-        compact(R, 0, V, o, turn=s)
-        v_ts(ch("TI", 2 + s, 128), o, 1.0 / BIG, A.mult)
-        v_ts(ch("TJ", 2 + s, 128), ch("TI", 2 + s, 128), 7, A.arith_shift_right)
+    for s in range(2):
+        v_ts(ch("TI", s, 256), ("Q", 512 * s, 512 * s + 256), 1.0 / (16 * BIG), A.mult)
+    for s in range(2):
+        v_ts(ch("TJ", 2 + s, 128), ch("TI", 2 * s + 1, 128), 7, A.arith_shift_right)
+    for s in range(2):
         v_cp(("IB" if s else "IA", 0, 128), ch("TJ", 2 + s, 128))
+    for s in range(2):
+        v_ts(ch("TJ", s, 128), ch("TI", 2 * s, 128), 127, A.bitwise_and)
+    s_act(ch("THR", 0, 128, V), ("IB", 0, 128), F.Exp, bias=-LN2, scale=-LN2)
+    s_act(ch("THR", 1, 128, V), ("IB", 0, 128), F.Exp, scale=LN2)
+    v_cp(("THR", V + 256, V + 512), ("TJ", 0, 256))
     for k in range(4):
         pe(summed(ch("R", k % 2), k, [], ("IA", 0, 128)))
         v_ts(ch("THR", k), ch("R", k % 2), ("PF", 7, 8), A.not_equal, FAR, A.mult)
-    s_act(("SC", 0, 128), ("IB", 0, 128), F.Exp, bias=-LN2, scale=-LN2)
-    s_act(("PW", 0, 128), ("IB", 0, 128), F.Exp, scale=LN2)
-    s_act(("POW", 0, 1), ("PF", 2, 3), F.Exp, bias=-math.log(BIG), scale=LN2, after=silu)
-    for hf in range(2):
-        v_ts(ch("SELW", hf, 1280), ch("SEL", hf, 1280), ("POW", 0, 1), A.mult)
 
     for k in (3, 2, 1, 0):
-        cp("S", ch("HW", k), ("HW", V, 2 * V), lst=lst("AB16", 0, 512 * k, 512 * k + 512))
+        cp("S" if k else "*", ch("HW", k), ("HW", V, 2 * V), lst=lst("AB16", 0, 512 * k, 512 * k + 512))
         v_tt(ch("YB", k), ("HW", V, 2 * V), ch("H", k), A.subtract, lst=lst("AB16", 128, 512 * k, 512 * k + 512))
+    in_line(begin)
+    v_ts(("AP", 0, 128), ("LI", 0, 128), CUT, A.add)
+    v_ts(("BP", 0, 128), ("LI", 128, 256), CUT + V, A.add)
+    v_ts(("ZC", 0, 128), ("ZI", 0, 128), 0.5, A.mult, 0.25, A.add)
+    for k in (3, 2, 1, 0):
         pe(summed(ch("P", k), k, [(ID, "HW"), (NID, "H")]))
         s_act(ch("DA", k), ch("P", k), F.Abs)
-        s_act(ch("DB", k), ch("YB", k), F.Abs)
+        if k in TUNE["v_db"]:
+            v_ts(ch("YA", k), ch("YB", k), -2.0, A.mult, 0.0, A.max)
+            pe(summed(ch("R", k % 2), k, [(ID, "YA"), (ID, "YB")]))
+            cp("*", ch("DB", k), ch("R", k % 2))
+        else:
+            s_act(ch("DB", k), ch("YB", k), F.Abs)
         pe(summed(ch("P", k), k, [(ID, "DA"), (NID, "DB")]))
         cp("*", ch("DL", k), ch("P", k))
     dma("G", [(T.dH[:], T.HW[:, V:2 * V])], [("HW", V, 2 * V), ("W0", V, 2 * V)], [("dH", 0, 1)], 4.0)
+
+    for hf in range(2):
+        v_ts(ch("SELW", hf, 1280), ch("SEL", hf, 1280), ("POW", 0, 1), A.mult)
+    dma("Y", [(T.stT[:], T.THR[:])], [("THR", 0, 2560)], [("stT", 0, 4)], 3.0)
+    exchange(13, "T", 5.5)
+    ops[-3]["after"] = line[-1]
+    dma("Y", [(T.lnT[q], T.stT[q])], [("stT", 0, 4)], [("lnT", q, q + 1)], 2.4)
+    dma("Y", [(T.THR[:], T.lnT[:])], [("lnT", 0, 4)], [("THR", 0, 2560)], 3.2)
+    dma("Y", [(T.SP[0:96, :], T.lnT[1:4, 3::4, 128:384]), (T.SP[96:128, :], T.lnT[0, 3::4, 128:384])], [("lnT", 0, 4)],
+        [("SP", 0, 256)], 2.6)
+    v_cp(("IH", 0, 256), ("THR", V + 256, V + 512))
+    v_cp(("INV", 0, 256), ("IH", 0, 256))
 
     cur, steps = [0], [0]
 
@@ -385,23 +419,15 @@ def build(g, core, T, topo):
             steps[0] += 1
             for k in (3, 2, 1, 0):
                 pe(group(ch("P", k), [(N2, ch("E", k)), (N2, ch("DB", k))], True, False) + spread(ch("P", k), k, ("ZC", 0, 128), False, False))
-        pieces = TUNE["pieces"]
-        helped = TUNE["help"][t]
-        bias[0] = TUNE["early"] * 4
+        costs = (W, V, 2 * V) if t else ("T3A", 0, V)
+        helped = TUNE["help"][n]
+        begin = len(ops)
         for k in helped:
-            cp("S", ch("TM", k), (W, V, 2 * V), lst=lst("AB16", 0, 512 * k, 512 * k + 512))
-            pe(summed(ch("R", k % 2), k, [(ID, "TM")] + ([(ID, "DL")] if t else [(ID, "DA"), (NID, "DB")])))
-            cp("S", ch(W, k), ch("R", k % 2))
-        for j, (lo, hi) in enumerate(pieces):
-            bias[0] = TUNE["early"] * lo / 512
-            for a, b in cut(lo, hi, TUNE["cmp"]):
-                if a // 512 not in helped:
-                    v_tt(part(W, a, b), (W, V, 2 * V), part("DL", a, b), A.add, lst=lst("AB16", 0, a, b))
-                v_tt(part(CM, a, b), (W, V, 2 * V), part(W, a, b), A.is_lt, lst=lst("AB16", 128, a, b))
-                if t == 3:
-                    compact(CM, a, b, ("Q", 512, 640), first=b == V, last=a == 0)
-            if t == 3 and not first:
-                continue
+            cp("S", ch("TM", k), costs, lst=lst("AB16", 0, 512 * k, 512 * k + 512))
+            pe(summed(ch("Q", 1 - k % 2), k, [(ID, "TM")] + ([(ID, "DL")] if t else [(ID, "DA"), (NID, "DB")])))
+            cp("S", ch(W, k), ch("Q", 1 - k % 2))
+
+        def winners(j, lo, hi):
             make_list(CM, n, lo, hi, ("Q", 512 * (j % 2 if t < 3 else 0)), True)
             for a, b in cut(lo, hi, 512):
                 for c, d in cut(a, b, TUNE["last"] if lo == 0 else 512):
@@ -412,18 +438,37 @@ def build(g, core, T, topo):
                     o = part("P", a, b)
                     pe(group(o, [(N2, part(PN, a, b))], False, True), acc=True)
                     either(lambda: v_ts(part(CZ, a, b), o, -1.0, A.max, 1.0, A.min), lambda: s_act(part(CZ, a, b), o, F.Sign))
-                    compact(CZ, a, b, ("R", 0, 128), first=b == V, last=a == 0)
-        bias[0] = 0.0
+                    compact(CZ, a, b, ("Q", 512, 640), first=b == V, last=a == 0)
+
+        waiting = []
+        for j, (lo, hi) in enumerate(TUNE["pieces"]):
+            for a, b in cut(lo, hi, TUNE["cmp"]):
+                if a // 512 not in helped:
+                    v_tt(part(W, a, b), costs, part("DL", a, b), A.add, lst=lst("AB16", 0, a, b))
+                    while waiting:
+                        winners(*waiting.pop())
+            for a, b in cut(lo, hi, TUNE["cmp"]):
+                v_tt(part(CM, a, b), costs, part(W, a, b), A.is_lt, lst=lst("AB16", 128, a, b))
+                if t == 3 and not first:
+                    compact(CM, a, b, ("Q", 512, 640), first=b == V, last=a == 0)
+                while waiting:
+                    winners(*waiting.pop())
+            if t < 3 or first:
+                waiting.append((j, lo, hi))
+        while waiting:
+            winners(*waiting.pop())
+        in_line(begin, "V")
         sg = ch("SG", t, 128)
+        o = ("Q", 0, 128) if t == 3 and first else ("Q", 512, 640)
+        if t in (1, 2) or t == 3 and first:
+            compact(CM, 0, V, o)
         if t in (1, 2):
-            compact(CM, 0, V, ("Q", 512, 640))
             cur[0] = 1 - cur[0]
         if t:
-            either(lambda: v_ts(sg, ("Q", 512, 640), -1.0 / BIG, A.mult, 8.5, A.add),
-                   lambda: s_act(sg, ("Q", 512, 640), F.Identity, bias=8.5, scale=-1.0 / BIG))
+            either(lambda: v_ts(sg, o, -1.0 / BIG, A.mult, 8.5, A.add), lambda: s_act(sg, o, F.Identity, bias=8.5, scale=-1.0 / BIG))
         if t == 3:
             if first:
-                v_ts(("MW", 0, 128), ("R", 0, 128), -BIG, A.is_le)
+                v_ts(("MW", 0, 128), ("Q", 512, 640), -BIG, A.is_le)
             v_tt(("CC", 0, 128), ("MW", 0, 128), sg, A.mult)
             if not first:
                 make_list(CM, n, 0, V, ("P", 0), False)
@@ -432,63 +477,75 @@ def build(g, core, T, topo):
 
     def join_x():
         dma("Y", [(T.XR[:, 0:V], T.dH[:])], [("dH", 0, 1)], [("XR", 0, V)], 4.0)
-        dma("G", [(T.XR[32:128, 0:V], T.YA[0:96, :]), (T.XR[0:32, 0:V], T.YA[96:128, :])], [("YA", 0, V)], [("XR", 0, V)], 9.0,
-            accum_op=A.add, max_dma_last_dim=4096)
+        for a, b in cut(0, V, TUNE["join"]):
+            dma("G", [(T.XR[32:128, a:b], T.YA[0:96, a:b]), (T.XR[0:32, a:b], T.YA[96:128, a:b])], [("YA", a, b)], [("XR", a, b)],
+                4.5 + 4.5 * (b - a) / V, accum_op=A.add, max_dma_last_dim=4096)
 
     def turn_x():
-        dma("Y", [(T.XS[32:128, :], T.X[0:96, :]), (T.XS[0:32, :], T.X[96:128, :])], [("X", 0, V)], [("XS", 0, V)], 6.0)
+        for a, b in cut(0, V, 1024):
+            dma("Y", [(T.XS[32:128, a:b], T.X[0:96, a:b]), (T.XS[0:32, a:b], T.X[96:128, a:b])], [("X", a, b)], [("XS", a, b)], 4.8)
 
     terms, slots = [0], [0]
 
-    def next_ex():
-        slots[0] += 1
-        return ch("EX", slots[0] % N_EX, TW)
+    def next_ex(n):
+        if slots[0] + n > SCRATCH["EX"][1][1]:
+            slots[0] = 0
+        slots[0] += n
+        return ("EX", slots[0] - n, slots[0])
 
-    def stage(e, k, first=False):
-        pair, wr = [(T.stG[4 * k:4 * k + 4], ap(e))], [("stG", 4 * k, 4 * k + 4)]
+    def stage(e, p, first=False):
+        pair, wr = [(T["stG%d" % p][:], ap(e))], [("stG%d" % p, 0, 4)]
         if first:
-            dma("Y", pair, [e], wr, 2.6)
+            dma("Y", pair, [e], wr, 3.2)
         else:
-            dma("G", pair, [e], wr, TUNE["acc"], accum_op=A.add, max_dma_last_dim=2048)
+            dma("G", pair, [e], wr, 3.6 + width(e) / 512 * TUNE["acc"], accum_op=A.add, max_dma_last_dim=2048)
 
-    free = [ch("R", k, TW) for k in range(1024 // TW)]
+    free = [ch("R", 0), ch("R", 1)]
 
-    def banks(n):
-        return free[n % len(free)]
-
-    def fill(o, k, pairs, small=None, last=True):
-        for j in range(TW // 512):
-            pe(summed(ch(o[0], j, base=o[1]), k * TW // 512 + j, pairs, small, last))
-
-    def term(k, pairs, off, half, v_abs):
-        n = terms[0]
+    def bank():
         terms[0] += 1
+        return free[terms[0] % len(free)]
+
+    def term(p, pairs, off, half, v_abs, plus):
+        lo, hi = GAIN[p]
         lnw = math.log(0.5) if half else 0.0
-        o, e, ab = banks(n), next_ex(), ch("AB", n % NG, TW)
-        fill(o, k, pairs)
-        if v_abs:
-            v_ts(ab, o, -off, A.add, 0.0, A.max)
-            for j in range(TW // 512):
-                pe(group(ch(o[0], j, base=o[1]), [(l, ch(r, k * TW // 512 + j)) for l, r in pairs] + [(N2, ch("AB", j, base=ab[1]))]))
-            s_act(e, o, F.Exp, bias=lnw - off / 8, scale=0.125)
-        else:
-            s_act(ab, o, F.Abs, bias=-off)
-            s_act(e, ab, F.Exp, bias=lnw, scale=-0.125)
-        stage(e, k)
+        e = ("GD", lo, hi) if plus else next_ex(hi - lo)
+        for k in range(lo // 512, hi // 512):
+            o = bank()
+            ab, out = ch("AB", terms[0] % 4), o if plus else ch("EX", k, base=e[1] - lo)
+            pe(summed(o, k, pairs))
+            if v_abs:
+                v_ts(ab, o, -off, A.add, 0.0, A.max)
+                pe(group(o, [(l, ch(r, k)) for l, r in pairs] + [(N2, ab)]))
+                s_act(out, o, F.Exp, bias=lnw - off / 8, scale=0.125)
+            else:
+                s_act(ab, o, F.Abs, bias=-off)
+                s_act(out, ab, F.Exp, bias=lnw, scale=-0.125)
+            if plus:
+                v_tt(ch("GD", k), o, ch("GD", k), A.add)
+        if plus != 1:
+            stage(e, p, plus == 2 and TUNE["back"])
+
+    walked = [None] * 3
 
     def walk_back(f):
         qa, qb = ("Q", 0, 128), ("Q", 512, 640)
         for t in (3, 2, 1):
             if t == 1:
                 pe(group(qa, [(ID, ch("MM", 0, 128)), (ID, ch("MM", 1, 128))], True, False))
-            pe(group(qb, [(ID, ("C16", 0, 128)), (NID, ("PW", 0, 128))], True, False))
-            for a, b in cut(0, V, TUNE["walk"]):
+            lend = f in TUNE["lend"]
+            pe(group(qb, [(ID, ch("C16", int(lend), 128)), (NID, ("SP", 128, 256))], True, False))
+            for a, b in TUNE["walk"]:
                 v_tt(part("YA", a, b), ("CC", 0, 128), part("THR", a, b), A.is_gt, lst=lst("INV", 0, a, b))
-                s_act(part("YB", a, b), ("CC", 0, 128), F.Sign, bias=-0.25, scale=-1.0, lst=lst("INV", 128, a, b))
+                if lend and b <= TUNE["lent"]:
+                    v_ts(part("YB", a, b), ("CC", 0, 128), -0.25, A.is_lt, 2.0, A.mult, lst=lst("INV", 128, a, b))
+                else:
+                    s_act(part("YB", a, b), ("CC", 0, 128), F.Sign, bias=-0.25, scale=-1.0, lst=lst("INV", 128, a, b))
                 compact("YA", a, b, qa, 1, first=t > 1 and b == V, last=a == 0)
                 compact("YB", a, b, qb, 1, first=False, last=a == 0, weights="SELW")
             m = ch("MM", 3 - t, 128)
-            v_tt(("TI", 0, 128), qb, ("SC", 0, 128), A.mult)
+            walked[3 - t] = len(ops) - 1
+            v_tt(("TI", 0, 128), qb, ("SP", 0, 128), A.mult)
             v_ts(("TJ", 0, 128), ("TI", 0, 128), 1, A.bitwise_and)
             v_tt(m, qa, ("TJ", 0, 128), A.add)
             if t > 1:
@@ -513,22 +570,27 @@ def build(g, core, T, topo):
         turn_x()
         step(3 * f + 3, 3, first, marks, "PN")
         walk_back(f)
-        for a, b in cut(0, V, TW if last else wide)[::-1]:
+        for a, b in cut(0, V, wide)[::-1]:
             l = lst("LP", 128 * (3 * f + 3), a, b)
             cp("*", part("T3" + P, a, b), ("HW", V, 2 * V), lst=l)
             cp("*", part("T1" + P, a, b), ("XS", 0, V), lst=l)
-            either(lambda: v_ts(part("T2" + P, a, b), part("T1" + P, a, b), HI - 15.5, A.add),
-                   lambda: s_act(part("T2" + P, a, b), part("T1" + P, a, b), F.Identity, bias=HI - 15.5))
+            if f in TUNE["t2"]:
+                v_ts(part("T2" + P, a, b), part("T1" + P, a, b), HI - 15.5, A.add)
+            else:
+                either(lambda: v_ts(part("T2" + P, a, b), part("T1" + P, a, b), HI - 15.5, A.add),
+                       lambda: s_act(part("T2" + P, a, b), part("T1" + P, a, b), F.Identity, bias=HI - 15.5))
         v_ts(ch("WIN", min(f, 1), 128), ch("SG", 3, 128), 0.0, A.is_lt, 0.25 if first else 0.125, A.mult)
         if f:
             v_tt(ch("WIN", 0, 128), ch("WIN", 0, 128), ch("WIN", 1, 128), A.add)
         if last:
-            free.extend(ch("P", k, TW) for k in range(NG))
-            for k in range(NG):
-                o, e = banks(k), next_ex()
-                fill(o, k, [], ch("WIN", 0, 128))
-                v_tt(e, o, ch("GD", k, TW), A.mult)
-                stage(e, k)
+            free.extend(ch("P", k) for k in range(4))
+            for k in range(4):
+                o = bank()
+                pe(summed(o, k, [], ch("WIN", 0, 128)))
+                v_tt(ch("GD", k), o, ch("GD", k), A.mult)
+                if TUNE["back"]:
+                    dma("G", [(ap(ch("GD", k)), T["stG%d" % k][:])], [("stG%d" % k, 0, 4)], [ch("GD", k)], 4.6,
+                        accum_op=A.add, max_dma_last_dim=2048)
         if first:
             return
         todo = [([(ID, "T1B"), (NID, "T2B"), (NID, "T3A")], -HI, True),
@@ -536,22 +598,28 @@ def build(g, core, T, topo):
                 ([(ID, "T1B"), (NID, "T2B"), (("N32M", 0, 128), "T2A")], -HI - HI / 32, False),
                 ([(ID, "T1A"), (NID, "T2A"), (("N32M", 0, 128), "T2B")], -HI - HI / 32, True)]
         skew = TUNE["skew"] if last else 0.1
-        for _, j, k in sorted((j + skew * k, j, k) for j in range(4) for k in range(NG)):
-            term(k, todo[j][0], todo[j][1], todo[j][2], j in TUNE["v_abs"][f])
+        for m, (_, j, p) in enumerate(sorted((j + skew * p, j, p) for j in range(4) for p in range(len(GAIN)))):
+            begin = len(ops)
+            term(p, todo[j][0], todo[j][1], todo[j][2], j in TUNE["v_abs"][f],
+                 0 if not last or j < 4 - TUNE["with"] else 1 + (j == 3))
+            if last and m in TUNE["pace"]:
+                ops[begin + 1]["after"] = walked[TUNE["pace"].index(m)]
 
     def new_tolls(o, k, small, old, new):
-        pe(summed(o, k, [(ID, old)], small))
+        pe(group(o, [(ID, ch(old, k))], True, False))
+        pe(spread(o, k, small, False, True), acc=True)
         v_ts(ch(new, k), o, 0.0, A.max, 63.0, A.min)
 
     step(0, 0, True, None, "PN0")
-    for k in range(NG):
-        e = next_ex()
-        s_act(e, ch("DA", k, TW), F.Exp, bias=math.log(3.0), scale=-0.125, after=silu)
-        stage(e, k, True)
-        s_act(ch("GD", k, TW), ch("DB", k, TW), F.Exp, scale=-0.125, after=silu)
-        e2 = next_ex()
-        either(lambda: v_ts(e2, e, -1.0 / 3, A.mult), lambda: s_act(e2, e, F.Identity, scale=-1.0 / 3))
-        dma("G", [(ap(ch("GD", k, TW)), ap(e2))], [e2], [ch("GD", k, TW)], TUNE["acc"], accum_op=A.add, max_dma_last_dim=2048)
+    for p, (lo, hi) in enumerate(GAIN):
+        e, e2 = next_ex(hi - lo), next_ex(hi - lo)
+        for k in range(lo // 512, hi // 512):
+            ea, less = ch("EX", k, base=e[1] - lo), ch("EX", k, base=e2[1] - lo)
+            s_act(ea, ch("DA", k), F.Exp, bias=math.log(3.0), scale=-0.125)
+            s_act(ch("GD", k), ch("DB", k), F.Exp, scale=-0.125)
+            either(lambda: v_ts(less, ea, -1.0 / 3, A.mult), lambda: s_act(less, ea, F.Identity, scale=-1.0 / 3))
+        stage(e, p, True)
+        dma("G", [(ap(("GD", lo, hi)), ap(e2))], [e2], [("GD", lo, hi)], 5.0, accum_op=A.add, max_dma_last_dim=2048)
     for rnd in range(2):
         f = 2 * rnd
         if rnd:
@@ -589,13 +657,12 @@ def build(g, core, T, topo):
     for k in range(4):
         new_tolls(ch("P", k), k, ("DN", 0, 128), "EN", "W0")
         dma("Y", [(T.tollout[:, 512 * k:512 * k + 512], ap(ch("W0", k)))], [ch("W0", k)], [], 2.5)
-    for k in range(NG):
-        st = [("stG", 4 * k, 4 * k + 4)]
-        send(9 + k, [(r, T.stG[4 * k + (r + 3) % 4], T.lnG[4 * k + q]) for r in others], st,
-             [("lnG", 4 * k + r, 4 * k + r + 1) for r in others], 2.2 * TW / 512)
-        dma("Y", [(T.gain[rows, TW * k:TW * k + TW], T.stG[4 * k + (q + 3) % 4])], st, [], 2.4)
-        dma("Y", [(T.gain[32 * r:32 * r + 32, TW * k:TW * k + TW], T.lnG[4 * k + r]) for r in others],
-            [("lnG", 4 * k + r, 4 * k + r + 1) for r in others], [], 2.6)
+    for p, (lo, hi) in enumerate(GAIN):
+        st, ln = "stG%d" % p, "lnG%d" % p
+        send(9 + p, [(r, T[st][(r + 3) % 4], T[ln][q]) for r in others], [(st, 0, 4)], [(ln, r, r + 1) for r in others],
+             2.7 * (hi - lo) / 512)
+        dma("Y", [(T.gain[rows, lo:hi], T[st][(q + 3) % 4])], [(st, 0, 4)], [], 2.8)
+        dma("Y", [(T.gain[32 * r:32 * r + 32, lo:hi], T[ln][r]) for r in others], [(ln, r, r + 1) for r in others], [], 3.0)
     return ops
 
 
@@ -610,7 +677,7 @@ def dependencies(ops):
         for name, lo, hi, w in touched:
             for (a, b, m, mw) in log.get(name, []):
                 if a < hi and lo < b and (w or mw) and m != n:
-                    if o["acc"] and name in PSUM and ops[m]["eng"] == "T":
+                    if name == "link" or o["acc"] and name in PSUM and ops[m]["eng"] == "T":
                         order.add(m)
                     else:
                         deps.add(m)
@@ -624,6 +691,71 @@ def dependencies(ops):
         o["deps"], o["order"] = deps, order - deps
 
 
+def greedy(ops, level):
+    n = len(ops)
+    users = [[] for _ in range(n)]
+    for k, o in enumerate(ops):
+        for d in o["deps"] | o["order"]:
+            users[d].append(k)
+    missing = [len(o["deps"] | o["order"]) for o in ops]
+    ready, start, where = [0.0] * n, [0.0] * n, [None] * n
+    pool = {e: [] for e in QUEUES}
+    free = {e: 0.0 for e in pool}
+
+    def engines(k):
+        return "VS" if "alt" in ops[k] else ops[k]["eng"]
+
+    def span(k, e):
+        return (ops[k]["alt"][e][1],) * 2 if "alt" in ops[k] else (ops[k]["issue"], ops[k]["dur"])
+
+    def soon(k, depth):
+        t = ready[k]
+        if missing[k]:
+            if not depth:
+                return 1e9
+            for d in ops[k]["deps"] | ops[k]["order"]:
+                if where[d] is None:
+                    t = max(t, max(soon(d, depth - 1), min(free[x] for x in engines(d))) + ops[d]["dur"] + LAT)
+        return t
+
+    for k in range(n):
+        if not missing[k]:
+            for e in engines(k):
+                pool[e].append(k)
+    left = n
+    while left:
+        t, e = min((max(free[e], min(ready[k] for k in pool[e])), e) for e in pool if pool[e])
+        now = [k for k in pool[e] if ready[k] <= t + 1e-9]
+        own = TUNE["own"]
+        k = max(now, key=lambda j: (level[j] + (0.0 if "alt" in ops[j] else own), -j))
+        bar = level[k] + TUNE["urgent"]
+        near = set(j for j in pool[e] if level[j] > bar)
+        rim = set(j for x in pool for j in pool[x] if level[j] > bar)
+        for _ in range(TUNE["hops"]):
+            rim = set(u for j in rim for u in users[j] if level[u] > bar)
+            near |= rim
+        due = [soon(j, TUNE["hops"]) for j in near if e in engines(j)]
+        due = min([x for x in due if x > t] or [1e9])
+        if due < t + span(k, e)[0] * TUNE["share"]:
+            fit = [j for j in now if t + span(j, e)[0] * TUNE["share"] <= due]
+            if not fit:
+                free[e] = min(due, t + 0.1)
+                continue
+            k = max(fit, key=lambda j: (level[j], -j))
+        for x in engines(k):
+            pool[x].remove(k)
+        issue, dur = span(k, e)
+        start[k], where[k], free[e] = t, e, t + issue
+        left -= 1
+        for u in users[k]:
+            ready[u] = max(ready[u], t + dur + (LAT if k in ops[u]["deps"] else 0.0))
+            missing[u] -= 1
+            if not missing[u]:
+                for x in engines(u):
+                    pool[x].append(u)
+    return start, where
+
+
 def pack(ops, before, rank, backward):
     n = len(ops)
     after = [[] for _ in range(n)]
@@ -632,7 +764,7 @@ def pack(ops, before, rank, backward):
             after[d].append(k)
     missing = [len(b) for b in before]
     ready, start, where = [0.0] * n, [0.0] * n, [None] * n
-    busy = {e: [] for e in "VSTGYX"}
+    busy = {e: [] for e in QUEUES}
     line_up = sorted((rank[k], k) for k in range(n) if not missing[k])
     while line_up:
         k = line_up.pop(0)[1]
@@ -694,7 +826,11 @@ def refine(ops):
         state[0] = (state[0] * 1103515245 + 12345) % 2147483648
         return state[0] / 2147483648.0
 
-    best = None
+    start, where = greedy(ops, [-x for x in rank])
+    order = [(k, where[k]) for k in sorted(range(n), key=lambda k: (start[k], k))]
+    ends = [replay(ops, order, case) for case in CASES]
+    best = (sum(ends), start, order, ends[0])
+    rank = start
     for turn in range(TUNE["turns"]):
         if turn:
             start, size = best[1], TUNE["shake"] * draw()
@@ -709,8 +845,99 @@ def refine(ops):
                 best = (sum(ends), start, order, ends[0])
             back, _ = pack(ops, after, [-start[k] - ops[k]["dur"] for k in range(n)], True)
             rank = [-back[k] - ops[k]["dur"] for k in range(n)]
-    ORDER["end"] = best[3]
-    return best[2]
+    order = polish(ops, best[2], after, draw)
+    ORDER["end"] = replay(ops, order, CASES[0])
+    return order
+
+
+def polish(ops, order, after, draw):
+    n = len(ops)
+    deps = [list(o["deps"]) for o in ops]
+    soft = [list(o["order"]) for o in ops]
+    users = [list(u) for u in after]
+    count = [len(deps[k]) + len(soft[k]) for k in range(n)]
+    cases = [(LAT * c["w"], c["weight"], {e: [((o["alt"][e][1],) * 2 if "alt" in o and e in "VS" else (o["issue"], o["dur"]))
+                                              for o in ops] for e in QUEUES}, [c[o["cls"]] for o in ops]) for c in CASES[:TUNE["cases"]]]
+    line = {e: [k for k, x in order if x == e] for e in QUEUES}
+
+    def run():
+        where, nxt, missing = [None] * n, [-1] * n, list(count)
+        for e, seq in line.items():
+            for j, k in enumerate(seq):
+                where[k] = e
+                if j:
+                    nxt[seq[j - 1]] = k
+                    missing[k] += 1
+        seq = [k for k in range(n) if not missing[k]]
+        for k in seq:
+            for u in users[k]:
+                missing[u] -= 1
+                if not missing[u]:
+                    seq.append(u)
+            u = nxt[k]
+            if u >= 0:
+                missing[u] -= 1
+                if not missing[u]:
+                    seq.append(u)
+        if len(seq) < n:
+            return None
+        total, chains = 0.0, []
+        for wake, weight, spans, factor in cases:
+            free, last, end, why = dict.fromkeys(line, 0.0), dict.fromkeys(line, -1), [0.0] * n, [-1] * n
+            for k in seq:
+                e = where[k]
+                t, w = free[e], last[e]
+                for d in deps[k]:
+                    if end[d] + wake > t:
+                        t, w = end[d] + wake, d
+                for d in soft[k]:
+                    if end[d] > t:
+                        t, w = end[d], d
+                issue, dur = spans[e][k]
+                free[e], end[k], why[k], last[e] = t + issue * factor[k], t + dur * factor[k], w, k
+            k = end.index(max(end))
+            total += weight * (end[k] + TUNE["pull"] * sum(end) / n)
+            chains.append((k, why))
+        return total, seq, where, chains
+
+    best = run()
+    for _ in range(TUNE["moves"]):
+        k, why = best[3][int(draw() * len(cases))]
+        if draw() < TUNE["any"]:
+            k = int(draw() * n)
+        where, links = best[2], []
+        while why[k] >= 0:
+            if where[why[k]] == where[k] and why[k] not in ops[k]["deps"] and why[k] not in ops[k]["order"]:
+                links.append((why[k], k))
+            k = why[k]
+        if not links:
+            continue
+        a, b = links[int(draw() * len(links))]
+        e, kind = where[a], draw()
+        saved = {x: list(line[x]) for x in {e, "V", "S"}}
+        seq = line[e]
+        j = seq.index(a)
+        if kind < 0.3 and ("alt" in ops[a] or "alt" in ops[b]):
+            m = a if "alt" in ops[a] and ("alt" not in ops[b] or draw() < 0.5) else b
+            other = line["S" if e == "V" else "V"]
+            place = {x: i for i, x in enumerate(best[1])}
+            seq.remove(m)
+            i = 0
+            while i < len(other) and place[other[i]] < place[m]:
+                i += 1
+            other.insert(max(0, i + int(draw() * 3) - 1), m)
+        elif kind < 0.65:
+            seq.remove(b)
+            seq.insert(max(0, j - int(draw() ** 3 * TUNE["far"])), b)
+        else:
+            seq.remove(a)
+            seq.insert(j + 1 + int(draw() ** 3 * TUNE["far"]), a)
+        new = run()
+        if new is not None and new[0] <= best[0] + TUNE["slack"] * draw():
+            best = new
+        else:
+            line.update(saved)
+    return [(k, best[2][k]) for k in best[1]]
 
 
 def replay(ops, order, case):

@@ -6,8 +6,7 @@ V = 2048
 BIG = 8192.0
 CUT = 8.5 * BIG
 HI = 6144.0
-FAR = 1.0e6
-LN2 = math.log(2.0)
+FUSED = 1280
 BF, F32, F16, I32, U16 = "bfloat16", "float32", "float16", "int32", "uint16"
 GAIN = [(0, 512), (512, 1024), (1024, 1536), (1536, 2048)]
 
@@ -18,48 +17,57 @@ def _sb(n, d):
 
 SCRATCH = {
     "W0": _sb(2 * V, F32), "W1": _sb(2 * V, F32), "CM0": _sb(V, BF), "CM1": _sb(V, BF), "PN": _sb(V, F16),
-    "PN0": _sb(V, F16), "TM": _sb(V, F16), "DA": _sb(V, BF), "DB": _sb(V, BF), "DL": _sb(V, BF), "E": _sb(V, BF),
+    "FD": _sb(2 * FUSED, BF), "ZB": _sb(FUSED, F16), "HX": _sb(2 * V, BF),
+    "PN0": _sb(V, F16), "TM": _sb(1536, F16), "DA": _sb(V, BF), "DB": _sb(V, BF), "DL": _sb(V, BF), "E": _sb(V, BF),
     "H": _sb(V, BF), "HW": _sb(2 * V, BF), "dH": ("dram", [128, V], F32),
-    "X": _sb(V, F32), "XR": _sb(V, F32), "XS": _sb(V, F32), "T1A": _sb(V, F16), "T1B": _sb(V, F16), "T2A": _sb(V, BF),
-    "T2B": _sb(V, BF), "T3A": _sb(V, BF), "T3B": _sb(V, BF), "AB": _sb(V, BF), "EX": _sb(7168, F32),
-    "YA": _sb(V, BF), "YB": _sb(V, BF), "THR": _sb(2560, BF), "SEL": _sb(2560, BF), "SELW": _sb(2560, BF),
+    "X": _sb(V, F32), "XR": _sb(V, F32), "T1A": _sb(V, F16), "T1B": _sb(V, F16), "T2A": _sb(V, BF),
+    "T2B": _sb(V, BF), "T3A": _sb(V, BF), "T3B": _sb(V, BF), "AB": _sb(V, BF), "EX": _sb(4608, F32),
+    "YA": _sb(V, BF), "YB": _sb(V, BF), "ED": _sb(V, BF), "THR": _sb(2 * V, BF), "MAT": _sb(1824, BF),
     "UNW": _sb(V, BF), "EN": _sb(V, BF), "GD": _sb(V, F32), "DLT": _sb(256, BF), "DH": _sb(512, BF), "DN": _sb(128, BF),
-    "IH": _sb(256, F32),
-    "LI": _sb(256, I32), "ZI": _sb(128, I32), "ZC": _sb(128, F16), "AB16": _sb(256, U16), "INV": _sb(256, U16),
-    "AP": _sb(128, F32), "BP": _sb(128, F32), "VP": _sb(128, F32), "LX": _sb(384, F32), "LY": _sb(128, F32),
+    "SELF": _sb(144, F32), "IV": _sb(256, U16), "DG": _sb(512, BF),
+    "LI": _sb(256, I32), "ZI": _sb(128, I32), "ZC": _sb(128, F16), "AB16": _sb(1024, U16), "INV": _sb(256, U16),
+    "AP": _sb(512, F32), "BP": _sb(512, F32), "VP": _sb(128, F32), "LX": _sb(384, F32), "LY": _sb(128, F32),
     "LZ": _sb(256, I32), "LS": _sb(13 * 128, U16), "LP": _sb(13 * 128, U16),
-    "SG": _sb(4 * 128, BF), "MW": _sb(128, BF), "CC": _sb(128, BF), "MM": _sb(384, BF), "UW": _sb(512, BF),
-    "RU": _sb(256, BF), "ADW": _sb(128, BF), "TI": _sb(512, I32), "TJ": _sb(512, I32), "IA": _sb(128, BF),
-    "IB": _sb(128, F32), "SP": _sb(256, BF), "C16": _sb(256, BF), "POW": _sb(2, BF),
-    "DJ": _sb(128, F32), "GJ": _sb(256, F32), "J16": _sb(16, F32), "PI": _sb(4, I32), "PF": _sb(12, F32),
-    "MK": _sb(16, F32), "MK4": _sb(16, F32), "BLK": _sb(160, BF), "II": _sb(256, BF), "NID": _sb(128, BF),
-    "N32M": _sb(128, BF), "N2M": _sb(128, BF), "WIN": _sb(256, BF), "M1": _sb(256, BF),
+    "SG": _sb(6 * 256, BF), "MW": _sb(256, BF), "CC": _sb(2048, BF), "UW": _sb(768, BF),
+    "RU": _sb(256, BF), "ADW": _sb(384, BF), "TI": _sb(256, I32), "TJ": _sb(256, I32),
+    "DJ": _sb(128, F32), "GJ": _sb(128, F32), "J16": _sb(16, F32), "PI": _sb(12, I32), "PF": _sb(28, F32),
+    "JP": _sb(192, F32), "YS": _sb(256, BF), "YG": _sb(224, BF), "YD": _sb(128, BF), "SGN": _sb(224, BF),
+    "MK": _sb(16, F32), "MK4": _sb(16, F32), "BLK": _sb(128, BF), "II": _sb(256, BF), "NID": _sb(128, BF),
+    "N32M": _sb(128, BF), "N2M": _sb(256, BF), "WIN": _sb(128, BF), "M1": _sb(256, BF),
     "M2": _sb(256, BF),
     "stL": ("dram", [4, 128, 64], I32), "lnL": ("dram", [4, 128, 64], I32),
     "stZ": ("dram", [4, 128, 32], I32), "lnZ": ("dram", [4, 128, 32], I32),
     "stH": ("dram", [4, 128, 512], BF), "lnH": ("dram", [4, 128, 512], BF),
     "stP": ("dram", [4, 128, 512], BF), "lnP": ("dram", [4, 128, 512], BF),
     "stE": ("dram", [4, 128, 512], BF), "lnE": ("dram", [4, 128, 512], BF),
-    "stT": ("dram", [4, 128, 640], BF), "lnT": ("dram", [4, 128, 640], BF),
+    "stT": ("dram", [8, 128, 256], BF), "lnT": ("dram", [8, 128, 256], BF),
+    "stI": ("dram", [8, 128, 32], U16), "lnI": ("dram", [8, 128, 32], U16),
     "stN": ("dram", [4, 128, 512], BF), "lnN": ("dram", [4, 128, 512], BF),
 }
 for _p, (_lo, _hi) in enumerate(GAIN):
     SCRATCH["stG%d" % _p] = SCRATCH["lnG%d" % _p] = ("dram", [4, 128, (_hi - _lo) // 4], F32)
+MATS, _at = {}, 0
+for _n, _w in (("sel", 144), ("vote0", 144), ("vote1", 208), ("over", 144), ("over2", 144), ("on", 208), ("out", 160),
+               ("sum", 192), ("sum1", 192), ("winA", 144), ("winB", 144)):
+    MATS[_n] = (_at, _w)
+    _at += _w
+COLS = ["p", "group", "row", "net", "and112", "and14", "and64", "and78", "and95", "slot", "odd", "mid", "net0", "slot0",
+        "even", "at", "at0", "at1", "to", "on", "home", "cut", "end", "none", "none0", "none1", "flip", "nine"]
 PSUM = {"P": 2048, "Q": 1024, "R": 1024}
 for _n in PSUM:
     SCRATCH[_n] = ("psum", [128, PSUM[_n]], F32)
 
-N_DMA_SEMS = 110
-SEMAPHORES = ["eV", "eS", "eT", "eG", "sent"] + ["rx%d" % k for k in range(14)] + ["d%d" % k for k in range(N_DMA_SEMS)]
+N_DMA_SEMS = 125
+SEMAPHORES = ["eV", "eS", "eT", "eG", "sent"] + ["rx%d" % k for k in range(17)] + ["d%d" % k for k in range(N_DMA_SEMS)]
 
 CY, PCY, GA, LAT = 0.00083, 0.00045, 1.56, 0.09
 ORDER = {}
 QUEUES = "VSTGYXZ"
-SIDE = ("X", "XR", "XS", "T1A", "T1B", "T2A", "T2B", "T3A", "T3B", "AB", "EX", "GD", "WIN", "LZ", "LP", "stG", "H32")
+SIDE = ("X", "XR", "XS", "YA", "T1A", "T1B", "T2A", "T2B", "T3B", "AB", "EX", "GD", "WIN")
 TUNE = {"pieces": [(1024, 2048), (0, 1024)], "cmp": 512, "last": 256,
-        "help": [[1, 0]] + [[1, 0], [1, 0], [0], [1, 0], [1, 0], [1, 0]] * 2,
-        "pull": 0.5, "any": 0.5, "cases": 3, "moves": 5000, "far": 12, "slack": 0.0, "lend": [], "own": 0.0, "urgent": 1.0, "hops": 1, "share": 0.6, "lean": 0.3, "early": 0.0, "side": 0.0, "walk": [(1536, 2048), (1024, 1536), (512, 1024), (0, 512)],
-        "join": 1024, "lent": 512, "with": 4, "back": True, "pace": [1, 5, 11], "t2": [0, 1, 2, 3], "v_db": [], "wide": 512, "v_abs": [[], [], [], []], "skew": 5.0, "acc": 0.9,
+        "help": [1024] * 13, "aid": 512, "banks": [1, 0], "fused": [(256, 1536)] * 13, "hold": 0,
+        "lists": [(0, 0, 1024), (0, 0, 512)] * 2, "apart": [1, 7], "pull": 0.5, "any": 0.5, "cases": 3, "moves": 14000, "far": 12, "slack": 0.0, "own": 0.0, "urgent": 1.0, "hops": 1, "share": 0.3, "lean": 0.1, "side": 3.0, "walk": [(512, 1024), (0, 512)],
+        "join": 1024, "with": 4, "back": True, "pace": [], "t2": [0, 1, 2, 3], "v_db": [], "wide": 512, "v_abs": [[], [], [], []], "skew": 5.0, "acc": 0.9,
         "passes": 4, "seed": 2, "turns": 1, "shake": 2.0, "span": 100.0}
 CASES = [{"g": 1.0, "c": 1.0, "p": 1.0, "d": 1.0, "w": 1.0, "weight": 1.0},
          {"g": 0.9, "c": 1.1, "p": 1.2, "d": 1.5, "w": 1.5, "weight": 0.6},
@@ -166,7 +174,7 @@ def build(g, core, T, topo):
                 if k == len(mms) - 1:
                     done.append(ins)
             return done
-        cyc = sum(max(64, width(m[2])) for m in mms)
+        cyc = sum(max(64, width(m[2])) * (1 if two(m[2]) else 4) for m in mms)
         add("T", fn, [m[1] for m in mms] + [m[2] for m in mms], [mms[0][0]], 0.06 + cyc * PCY, acc=acc)
 
     def group(o, pairs, first=True, last=True):
@@ -216,10 +224,20 @@ def build(g, core, T, topo):
     def cut(lo, hi, n):
         return [(a, min(a + n, hi)) for a in range(lo, hi, n)][::-1]
 
-    ID, ROT, NID, N2 = ("II", 0, 128), ("II", 96, 224), ("NID", 0, 128), ("N2M", 0, 128)
+    ID, NID, N2 = ("II", 0, 128), ("NID", 0, 128), ("N2M", 0, 128)
 
-    def sel(i, turn=0, name="SEL"):
-        return (name, 160 * i + 32 * turn, 160 * i + 32 * turn + 128)
+    def rot(t):
+        return ("II", 32 * t, 32 * t + 128)
+
+    def mat(name, shift=0, turn=0):
+        at = MATS[name][0] + 16 - shift + turn
+        return ("MAT", at, at + 128)
+
+    def whole(name):
+        return ("MAT", MATS[name][0], MATS[name][0] + MATS[name][1])
+
+    def pf(name):
+        return ("PF", COLS.index(name), COLS.index(name) + 1)
 
     def unw(i):
         return ("UNW", 128 * i, 128 * i + 128)
@@ -250,7 +268,8 @@ def build(g, core, T, topo):
     iota(("PI", 0, 1), [[0, 1]], 0, 1)
     iota(ch("X", 0), [[1, 512]], 32, 0)
     iota(("J16", 0, 16), [[1, 16]], 0, 0)
-    iota(("GJ", 0, 256), [[0, 2], [1, 8], [0, 16]], 0, 0)
+    iota(("JP", 48, 192), [[1, 144]], -16, 0)
+    iota(("GJ", 0, 128), [[1, 8], [0, 16]], 0, 0)
     iota(("DJ", 0, 128), [[1, 128]], 0, -1)
     iota(("VP", 0, 128), [[16, 128]], int(CUT), 0)
     exchange(0, "L", 1.3)
@@ -259,6 +278,13 @@ def build(g, core, T, topo):
     exchange(2, "P", 5.4)
     exchange(3, "E", 5.4)
     exchange(4, "Z", 1.0)
+    iota(("JP", 0, 48), [[1, 48]], -64, 0)
+    iota(("YS", 0, 192), [[64, 3], [0, 4], [1, 16]], -64, 0)
+    iota(("YS", 192, 256), [[0, 4], [1, 16]], 0, 0)
+    iota(("YG", 0, 160), [[32, 5], [0, 2], [1, 16]], -32, 0)
+    iota(("YG", 160, 224), [[32, 2], [0, 2], [1, 16]], 0, 0)
+    iota(("YD", 0, 128), [[64, 2], [0, 2], [1, 32]], 0, 0)
+    iota(("SGN", 0, 224), [[0, 7], [-4, 2], [0, 16]], 2, 0)
     line = [k for k in range(first_g, len(ops)) if ops[k]["eng"] == "G"]
     for a, b in zip(line, line[1:]):
         ops[b]["after"] = a
@@ -269,88 +295,117 @@ def build(g, core, T, topo):
     dma("Y", [(T.HW[32:128, V:2 * V], T.lnH[0:3]), (T.HW[0:32, V:2 * V], T.lnH[3])], [("lnH", 0, 4)], [("HW", V, 2 * V)], 3.6)
     dma("Y", [(T.H[:], T.lnH[:])], [("lnH", 0, 4)], [("H", 0, V)], 3.8)
     dma("Y", [(T.E[:], T.lnE[:])], [("lnE", 0, 4)], [("E", 0, V)], 2.8)
-    dma("Y", [(T.ZI[:], T.lnZ[:])], [("lnZ", 0, 4)], [("ZI", 0, 128)], 2.2)
+    dma("Y", [(T.ZI[32:128], T.lnZ[0:3]), (T.ZI[0:32], T.lnZ[3])], [("lnZ", 0, 4)], [("ZI", 0, 128)], 2.2)
 
     begin = len(ops)
-    add("V", lambda: [g.vector.memset(T.SEL[:], 0.0)], [], [("SEL", 0, 2560)], 0.06 + 1280 * CY)
-    v_ts(("PI", 1, 2), ("PI", 0, 1), 4, A.arith_shift_right)
-    v_ts(("PI", 2, 3), ("PI", 0, 1), 15, A.bitwise_and)
-    v_ts(("PI", 3, 4), ("PI", 0, 1), 4, A.arith_shift_right, 1, A.bitwise_and)
-    v_cp(("PF", 0, 4), ("PI", 0, 4))
-    v_ts(("MK", 0, 16), ("J16", 0, 16), ("PF", 2, 3), A.is_equal)
+    BITS = {"group": (4, A.arith_shift_right), "row": (15, A.bitwise_and), "net": (4, A.arith_shift_right, 1, A.bitwise_and),
+            "odd": (5, A.arith_shift_right, 1, A.bitwise_and), "slot": (1, A.bitwise_and)}
+    BITS.update({"and%d" % m: (m, A.bitwise_and) for m in (112, 14, 64, 78, 95)})
+
+    def bits(names):
+        for nm in names:
+            k = COLS.index(nm)
+            v_ts(("PI", k, k + 1), ("PI", 0, 1), *BITS[nm])
+        lo, hi = COLS.index(names[0]), COLS.index(names[-1]) + 1
+        v_cp(("PF", lo, hi), ("PI", lo, hi))
+
+    bits(COLS[1:6])
+    v_ts(("MK", 0, 16), ("J16", 0, 16), pf("row"), A.is_equal)
     v_ts(("MK4", 0, 16), ("MK", 0, 16), 4.0, A.mult)
-    v_ts(("BLK", 0, 160), ("GJ", 0, 160), ("PF", 1, 2), A.is_equal)
+    v_ts(("BLK", 0, 128), ("GJ", 0, 128), pf("group"), A.is_equal)
     for k in (1, 2, 3):
         s_act(ch("X", k), ch("X", 0), F.Identity, bias=512.0 * k)
 
     def matrices():
-        for i in range(16):
-            v_ts(("SEL", 160 * i + i, 160 * i + 160, 16), ("BLK", i, 160, 16), BIG, A.mult)
+        v_ts(("SELF", 0, 144), ("JP", 48, 192), pf("and112"), A.is_equal, 1.0 / 16, A.mult)
+        v_ts(pf("mid"), pf("and14"), -1.0, A.mult, -159.5 / 128, A.add)
+        v_ts(whole("sel"), ("JP", 48, 192), pf("and112"), A.is_equal, BIG, A.mult)
         v_ts(("II", 0, 128), ("DJ", 0, 128), 0.0, A.is_equal)
         v_ts(("II", 128, 256), ("DJ", 0, 128), 0.0, A.is_equal)
         v_ts(("NID", 0, 128), ID, -1.0, A.mult)
-        v_ts(("PF", 7, 8), ("PF", 2, 3), 4.0, A.mult)
-        v_ts(("VP", 0, 128), ("VP", 0, 128), ("PF", 2, 3), A.add)
-        v_ts(("N2M", 0, 128), ID, -2.0, A.mult)
+        v_ts(("VP", 0, 128), ("VP", 0, 128), pf("row"), A.add)
+        v_ts(("N2M", 0, 256), ("II", 0, 256), -2.0, A.mult)
 
     def more_matrices():
-        add("V", lambda: [g.vector.memset(T.C16[:, 0:128], 65536.0)], [], [("C16", 0, 128)], 0.12)
-        v_ts(("PF", 4, 5), ("PF", 3, 4), -1.0, A.mult, 1.0, A.add)
-        v_ts(("PF", 8, 9), ("PF", 2, 3), TUNE["lent"] / 128, A.is_ge)
-        v_ts(("M1", 0, 128), ("DJ", 0, 128), -16.0, A.is_equal, ("PF", 3, 4), A.mult)
-        v_ts(("M2", 0, 128), ("DJ", 0, 128), 16.0, A.is_equal, ("PF", 4, 5), A.mult)
-        v_ts(("C16", 128, 256), ("C16", 0, 128), ("PF", 8, 9), A.mult, 1.0, A.max)
+        v_ts(pf("net0"), pf("net"), -1.0, A.mult, 1.0, A.add)
+        v_ts(("M1", 0, 128), ("DJ", 0, 128), -16.0, A.is_equal, pf("net"), A.mult)
+        v_ts(("M2", 0, 128), ("DJ", 0, 128), 16.0, A.is_equal, pf("net0"), A.mult)
         v_tt(("M1", 0, 128), ("M1", 0, 128), N2, A.subtract)
         v_cp(("M2", 128, 256), ("M2", 0, 128))
         v_ts(("N32M", 0, 128), ID, -1.0 / 32, A.mult)
         v_cp(("M1", 128, 256), ("M1", 0, 128))
 
-    def votes(o, name, lo, hi):
-        pe(group(o, [(sel(i), (name, lo + i, hi, 16)) for i in range(16)]))
+    def walk_matrices():
+        jp = ("JP", 48, 192)
+        bits(COLS[6:11])
+        v_ts(pf("slot0"), pf("slot"), -1.0, A.mult, 1.0, A.add)
+        v_ts(pf("even"), pf("odd"), -1.0, A.mult, 1.0, A.add)
+        v_ts(pf("flip"), pf("and64"), -2.0, A.mult, 64.0, A.add)
+        v_ts(pf("at"), pf("net"), 32.0, A.mult, pf("odd"), A.add)
+        v_ts(pf("at0"), pf("and64"), pf("at"), A.add)
+        v_ts(pf("at1"), pf("flip"), pf("odd"), A.mult, pf("at0"), A.add)
+        v_ts(pf("to"), pf("odd"), 8.0, A.mult, pf("and64"), A.add)
+        v_ts(pf("on"), pf("slot"), pf("to"), A.add)
+        v_ts(pf("at"), pf("flip"), pf("slot0"), A.mult, pf("and78"), A.add)
+        v_ts(pf("at"), pf("slot"), 32.0, A.mult, pf("at"), A.add)
+        v_ts(pf("home"), pf("odd"), 16.0, A.mult, pf("at"), A.add)
+        v_ts(pf("cut"), pf("net"), -34.0, A.mult, 17.0, A.add)
+        v_ts(pf("nine"), pf("and14"), TUNE["fused"][3][0] / 128 - 1, A.is_gt, -16.0, A.mult)
+        v_ts(pf("at"), pf("and14"), TUNE["fused"][3][1] / 128 - 1, A.is_lt)
+        v_ts(pf("nine"), pf("nine"), pf("at"), A.mult, -1.0, A.add)
+        v_ts(whole("vote1"), ("YG", 16, 224), pf("at1"), A.is_equal, -1.0, A.mult)
+        v_ts(whole("vote0"), ("YG", 80, 224), pf("at0"), A.is_equal, -1.0, A.mult)
+        v_cp(whole("over"), part("MAT", 64, 208, MATS["vote1"][0]))
+        v_ts(whole("over2"), whole("over"), -2.0, A.mult)
+        v_tt(whole("vote1"), whole("vote1"), ("SGN", 16, 224), A.mult)
+        v_tt(whole("vote0"), whole("vote0"), ("SGN", 16, 160), A.mult)
+        v_ts(whole("on"), ("YS", 48, 256), pf("on"), A.is_equal)
+        v_ts(whole("out"), ("JP", 32, 192), pf("to"), A.is_equal, pf("slot0"), A.mult)
+        v_ts(whole("sum"), ("JP", 0, 192), pf("and78"), A.is_equal, pf("even"), A.mult)
+        v_ts(whole("sum1"), whole("sum"), pf("slot"), A.mult)
+        v_ts(pf("end"), pf("net"), -7.5, A.mult, 1.5, A.add)
+        v_ts(pf("end"), pf("end"), pf("slot"), A.mult, -2.0, A.add)
+        v_ts(pf("none"), pf("odd"), 2.0, A.mult, 2.0, A.add)
+        v_ts(pf("none0"), pf("none"), pf("net0"), A.mult)
+        v_ts(pf("none1"), pf("none"), pf("net"), A.mult)
+        v_ts(whole("winA"), jp, pf("home"), A.is_equal, pf("net"), A.mult)
+        v_ts(whole("winB"), whole("winA"), 0.5, A.mult)
+        v_ts(("YD", 0, 128), ("YD", 0, 128), pf("and95"), A.is_equal, 2.0, A.mult)
+        for n in range(2):
+            for b in range(2):
+                v_ts(ch("DG", 2 * n + b, 128), ("YD", 0, 128), pf("odd" if n else "even"), A.mult, pf("slot" if b else "slot0"), A.mult)
 
-    def compact(name, lo, hi, o, turn=0, first=True, last=True, weights="SEL"):
-        pairs = [(sel(i, turn, weights), (name, 128 * i, 128 * i + 128)) for i in range(lo // 128, hi // 128)]
+    def votes(o, name, lo, hi):
+        pe(group(o, [(mat("sel", i), (name, lo + i, hi, 16)) for i in range(16)]))
+
+    def compact(name, lo, hi, o, by, turn=0, n=256, first=True, last=True, base=0):
+        pairs = [(mat(by, i * n // 128, turn), (name, base + n * i, base + n * i + n)) for i in range(lo // n, hi // n)]
         pe(group(o, pairs, first, last), acc=not first)
 
-    def spread(o, k, small, first, last):
-        return [((o[0], o[1] + 128 * j, o[1] + 128 * j + 128), unw(4 * k + j), small, first, last and (first or j == 3))
-                for j in range(4)]
+    def spread(o, a, b, small, first, last):
+        return [((o[0], o[1] + c - a, o[1] + c - a + 128), unw(c // 128), small, first, last and (first or c + 128 == b))
+                for c in range(a, b, 128)]
 
     def summed(o, k, pairs, small=None, last=True):
         mm = group(o, [(l, ch(r, k)) for l, r in pairs], True, last and small is None)
-        return mm + (spread(o, k, small, not pairs, True) if small else [])
+        return mm + (spread(o, 512 * k, 512 * k + 512, small, not pairs, True) if small else [])
 
     v_cp(("INV", 0, 256), ("TI", 0, 256))
     add("V", lambda: [g.vector.tensor_copy(T.W1[:, 0:V].indirect(T.INV[:, 0:128]), T.X[:])],
         [("X", 0, V), ("INV", 0, 128)], [("W1", 0, V)], 2.4 * GA * V * CY)
     silu = add("S", lambda: [g.scalar.activation(T.W1[:, V:2 * V].indirect(T.INV[:, 128:256]), T.X[:], F.Silu)],
                [("X", 0, V), ("INV", 128, 256)], [("W1", V, 2 * V)], 1.3 + 2.4 * GA * V * CY)
-    v_ts(("TM", 0, V), ("W1", 0, V), -32.0, A.add)
-    s_act(("PN", 0, V), ("W1", V, 2 * V), F.Identity, bias=-32.0)
     matrices()
     for i in range(16):
-        s_act(unw(i), ("BLK", 0, 128), F.Identity, scale=("MK4", i, i + 1))
-    for s, R in enumerate(("TM", "PN")):
-        o = ("Q", 512 * s, 512 * s + 256)
-        votes((o[0], o[1], o[1] + 128), R, 0, V)
-        compact(R, 0, V, (o[0], o[1] + 128, o[2]))
-    s_act(("POW", 0, 1), ("PF", 2, 3), F.Exp, bias=-math.log(BIG), scale=LN2)
+        either(lambda: v_ts(unw(i), ("BLK", 0, 128), ("MK4", i, i + 1), A.mult),
+               lambda: s_act(unw(i), ("BLK", 0, 128), F.Identity, scale=("MK4", i, i + 1)))
+    for s in range(2):
+        pe(group(ch("Q", s, 128), [(("SELF", 16 - i, 144 - i), ("W1", V * s + i, V * s + V, 16)) for i in range(16)]))
     more_matrices()
     v_cp(("AB16", 0, 256), ("LI", 0, 256))
-    for s in range(2):
-        v_ts(ch("TI", s, 256), ("Q", 512 * s, 512 * s + 256), 1.0 / (16 * BIG), A.mult)
-    for s in range(2):
-        v_ts(ch("TJ", 2 + s, 128), ch("TI", 2 * s + 1, 128), 7, A.arith_shift_right)
-    for s in range(2):
-        v_cp(("IB" if s else "IA", 0, 128), ch("TJ", 2 + s, 128))
-    for s in range(2):
-        v_ts(ch("TJ", s, 128), ch("TI", 2 * s, 128), 127, A.bitwise_and)
-    s_act(ch("THR", 0, 128, V), ("IB", 0, 128), F.Exp, bias=-LN2, scale=-LN2)
-    s_act(ch("THR", 1, 128, V), ("IB", 0, 128), F.Exp, scale=LN2)
-    v_cp(("THR", V + 256, V + 512), ("TJ", 0, 256))
-    for k in range(4):
-        pe(summed(ch("R", k % 2), k, [], ("IA", 0, 128)))
-        v_ts(ch("THR", k), ch("R", k % 2), ("PF", 7, 8), A.not_equal, FAR, A.mult)
+    v_ts(("TI", 0, 256), ("Q", 0, 256), -32.0, A.add)
+    v_ts(("TJ", 0, 256), ("TI", 0, 256), 255, A.bitwise_and)
+    v_cp(("IV", 0, 256), ("TJ", 0, 256))
 
     for k in (3, 2, 1, 0):
         cp("S" if k else "*", ch("HW", k), ("HW", V, 2 * V), lst=lst("AB16", 0, 512 * k, 512 * k + 512))
@@ -370,122 +425,209 @@ def build(g, core, T, topo):
             s_act(ch("DB", k), ch("YB", k), F.Abs)
         pe(summed(ch("P", k), k, [(ID, "DA"), (NID, "DB")]))
         cp("*", ch("DL", k), ch("P", k))
-    dma("G", [(T.dH[:], T.HW[:, V:2 * V])], [("HW", V, 2 * V), ("W0", V, 2 * V)], [("dH", 0, 1)], 4.0)
 
-    for hf in range(2):
-        v_ts(ch("SELW", hf, 1280), ch("SEL", hf, 1280), ("POW", 0, 1), A.mult)
-    dma("Y", [(T.stT[:], T.THR[:])], [("THR", 0, 2560)], [("stT", 0, 4)], 3.0)
-    exchange(13, "T", 5.5)
-    ops[-3]["after"] = line[-1]
-    dma("Y", [(T.lnT[q], T.stT[q])], [("stT", 0, 4)], [("lnT", q, q + 1)], 2.4)
-    dma("Y", [(T.THR[:], T.lnT[:])], [("lnT", 0, 4)], [("THR", 0, 2560)], 3.2)
-    dma("Y", [(T.SP[0:96, :], T.lnT[1:4, 3::4, 128:384]), (T.SP[96:128, :], T.lnT[0, 3::4, 128:384])], [("lnT", 0, 4)],
-        [("SP", 0, 256)], 2.6)
-    v_cp(("IH", 0, 256), ("THR", V + 256, V + 512))
-    v_cp(("INV", 0, 256), ("IH", 0, 256))
+    def turned(eng, o, a, t, dur, **kw):
+        cutp = 128 - 32 * t
+        dma(eng, [(T[o[0]][0:cutp, o[1]:o[2]], T[a[0]][32 * t:128, a[1]:a[2]]), (T[o[0]][cutp:128, o[1]:o[2]], T[a[0]][0:32 * t, a[1]:a[2]])],
+            [a], [o], dur, **kw)
 
-    cur, steps = [0], [0]
+    OWN = min(TUNE["help"][1:])
+    edges = {0: ("DL", OWN), 1: ("H", 0), 2: ("HW", 0), 3: ("DA", 0)}
+    turned("Y", ("HX", 0, V), ("HW", 0, V), 1, 4.0)
+    dma("Y", [(T.HX[:, V:2 * V], T.lnH[:])], [("lnH", 0, 4), ("H", 0, V)], [("HX", V, 2 * V)], 3.6)
+    for t in (1, 2, 3):
+        turned("Y", ch("AB16", t, 256), ch("AB16", 0, 256), t, 2.3)
+        turned("Y", ch("BP", t, 128), ch("BP", 0, 128), t, 2.3)
+        if t > 1:
+            turned("Y", ch("AP", t, 128), ch("AP", 0, 128), t, 2.3)
+        if t < 3:
+            turned("Y", part(edges[t][0], 0, V - OWN, edges[t][1]), ("DL", OWN, V), t, 2.4 + 1.6 * (V - OWN) / V)
+    dma("Y", [(T.HW[0:64, V:2 * V], T.lnH[2:4]), (T.HW[64:128, V:2 * V], T.lnH[0:2])], [("lnH", 0, 4)], [("HW", V, 2 * V)], 3.6)
+    dma("G", [(T.dH[0:96], T.lnH[1:4]), (T.dH[96:128], T.lnH[0])], [("lnH", 0, 4), ("W0", V, 2 * V)], [("dH", 0, 1)], 4.0)
+    turned("Y", ("T2A", 0, V), ("DA", 0, V), 3, 4.0)
+    turned("Y", ("T2B", 0, V), ("DB", 0, V), 3, 4.0)
 
-    def make_list(CM, n, lo, hi, o, winners):
+    walk_matrices()
+    for k in range(8):
+        s_act(ch("THR", k), ch("W1", k), F.Abs, bias=pf("mid"), scale=1.0 / 128)
+    halves = [(s, h, slice(64 * h + 32 * s, 64 * h + 32 * s + 32)) for s in range(2) for h in range(2)]
+    dma("Y", [(T.stI[:, at, :], ap(ch("IV", 2 * s + h, 64))) for s, h, at in halves], [("IV", 0, 256)], [("stI", 0, 8)], 2.4)
+    dma("Y", [(T.stT[:, at, :], T.THR[0::2, 1024 * (2 * s + h):1024 * (2 * s + h + 1)]) for s, h, at in halves], [("THR", 0, 2 * V)],
+        [("stT", 0, 8)], 3.2)
+    for k, nm, dur in ((13, "I", 0.8), (15, "T", 2.8)):
+        st, ln = "st" + nm, "ln" + nm
+        for n in range(2):
+            send(k + n, [(r, T[st][2 * r + n], T[ln][2 * q + n]) for r in others], [(st, 0, 8)],
+                 [(ln, 2 * r + n, 2 * r + n + 1) for r in others], dur)
+            ops[-3]["after"] = line[-1]
+        dma("Y", [(T[ln][2 * q:2 * q + 2], T[st][2 * q:2 * q + 2])], [(st, 0, 8)], [(ln, 2 * q, 2 * q + 2)], 2.4)
+    dma("Y", [(ap(ch("INV", x, 64)), T.lnI[x::4]) for x in range(4)], [("lnI", 0, 8)], [("INV", 0, 256)], 2.4)
+    for x in range(4):
+        dma("Y", [(T.THR[b::2, 1024 * x:1024 * x + 1024], T.lnT[x::4]) for b in range(2)], [("lnT", 0, 8)], [ch("THR", x, 1024)], 3.0)
+
+    cur, steps, listed, terms = [0], [0], [0], [0]
+    free = [ch("R", 0), ch("R", 1)]
+
+    def bank():
+        terms[0] += 1
+        return free[terms[0] % len(free)]
+
+    def make_list(CM, n, t, lo, hi, o, winners):
         o, y = (o[0], o[1], o[1] + (hi - lo) // 16), lst("LX", 128 * (n % 3), lo, hi)
         votes(o, CM, lo, hi)
-        v_tt(y, o, lst("BP", 0, lo, hi), A.min)
+        v_tt(y, o, lst("BP", 128 * t, lo, hi), A.min)
         if winners:
             v_tt(lst("LY", 0, lo, hi), y, lst("VP", 0, lo, hi), A.max)
             v_ts(lst("LS", 128 * n, lo, hi), lst("LY", 0, lo, hi), -CUT - lo, A.add)
 
-    def predecessors(n):
-        v_tt(("LZ", 0, 128), ch("LX", n % 3, 128), ("AP", 0, 128), A.max)
+    def predecessors(n, t):
+        v_tt(("LZ", 0, 128), ch("LX", n % 3, 128), ch("AP", t, 128), A.max)
         v_ts(("LZ", 128, 256), ("LZ", 0, 128), V - 1, A.bitwise_and)
         v_cp(ch("LP", n, 128), ("LZ", 128, 256))
+        listed[0] = len(ops) - 1
 
-    def open_window(pairs, small=None):
+    def open_window(names):
         for k in (3, 2, 1, 0):
-            mm = group(ch("P", k), [(l, ch(r, k)) for l, r in pairs], True, False)
-            pe(mm + (spread(ch("P", k), k, small, False, False) if small else []))
+            pe(group(ch("P", k), [(ID, ch(r, k)) for r in names], True, False))
 
     def close_window(k, name, small=None):
         o = ch("P", k)
-        pe(spread(o, k, small, False, True) if small else group(o, [(ROT, ch(name, k))], False, True), acc=True)
+        pe(spread(o, 512 * k, 512 * k + 512, small, False, True) if small else group(o, [(ID, ch(name, k))], False, True), acc=True)
         cp("*", ch("W%d" % (1 - cur[0]), k, base=V), o)
+
+    QB = ("Q", 512, 768)
+
+    def gate(n):
+        return ch("SG", (n - 1) % 3 if n % 3 else 1 + n // 3, 256)
 
     def step(n, t, first, marks, PN):
         W, CM = "W%d" % cur[0], "CM%d" % (steps[0] % 2)
         steps[0] += 1
-        if t in (1, 2):
-            open_window([(ROT, "E"), (ROT, "DB")], marks)
-        if t == 3 and first:
-            CZ = "CM%d" % (steps[0] % 2)
-            steps[0] += 1
-            for k in (3, 2, 1, 0):
-                pe(group(ch("P", k), [(N2, ch("E", k)), (N2, ch("DB", k))], True, False) + spread(ch("P", k), k, ("ZC", 0, 128), False, False))
+        fixed = ["E", "DB"] if n in TUNE["apart"] else ["ED"]
         costs = (W, V, 2 * V) if t else ("T3A", 0, V)
         helped = TUNE["help"][n]
         begin = len(ops)
-        for k in helped:
-            cp("S", ch("TM", k), costs, lst=lst("AB16", 0, 512 * k, 512 * k + 512))
-            pe(summed(ch("Q", 1 - k % 2), k, [(ID, "TM")] + ([(ID, "DL")] if t else [(ID, "DA"), (NID, "DB")])))
-            cp("S", ch(W, k), ch("Q", 1 - k % 2))
+        for j, (a, b) in enumerate(cut(0, helped, TUNE["aid"])):
+            o = ch("P", TUNE["banks"][j % len(TUNE["banks"])])
+            o = (o[0], o[1], o[1] + b - a)
+            fix = [(rot(t), "DL")] if t else [(ID, "DA"), (NID, "DB")]
+            pe(group(o, [(l, part(r, a, b)) for l, r in fix], True, False))
+            cp("S", part("TM", a, b), costs, lst=lst("AB16", 256 * t, a, b))
+            pe(group(o, [(ID, part("TM", a, b))], False, True), acc=True)
+            cp("S", part(W, a, b), o)
+        f0, f1 = TUNE["fused"][n]
+        picked = [x for lo, hi in ((f1, V), (0, f0)) for k in (3, 2, 1, 0) for x in [(max(lo, 512 * k), min(hi, 512 * k + 512))] if x[0] < x[1]]
+        NEXT, small = "W%d" % (1 - cur[0]), ("ZC", 0, 128) if t == 3 else marks and ch("ADW", t, 128)
+        beside = ("ZB", -f0) if t == 3 else ("FD", FUSED * (t - 1) - f0)
+
+        def fixed_part(o, a, b, last):
+            turn = ("N2M", 96, 224) if t == 3 else rot(t)
+            mm = group(o, [(turn, part(x, a, b)) for x in fixed], True, last and not small)
+            pe(mm + (spread(o, a, b, small, False, last) if small else []))
+
+        if t in (1, 2) or t == 3 and first:
+            if t < 3 and not marks and n not in TUNE["apart"]:
+                turned("Y", part("FD", f0, f1, beside[1]), ("ED", f0, f1), t, 3.2)
+            elif t == 2 and marks and TUNE["fused"][n - 1] == (f0, f1):
+                turned("Y", part("FD", f0, f1, beside[1]), part("FD", f0, f1, -f0), 1, 3.2)
+            else:
+                for j, (a, b) in enumerate(cut(f0, f1, 512)):
+                    o, to = ch("P", 3 - j % 2), part(beside[0], a, b, beside[1])
+                    o = (o[0], o[1], o[1] + b - a)
+                    fixed_part(o, a, b, True)
+                    if t == 3:
+                        either(lambda: v_ts(to, o, 0.5, A.mult), lambda: s_act(to, o, F.Identity, scale=0.5))
+                    else:
+                        cp("*", to, o)
+            for a, b in picked:
+                fixed_part(part("P", a, b), a, b, False)
+        if t == 3 and first:
+            CZ = "CM%d" % (steps[0] % 2)
+            steps[0] += 1
+        counted = [0]
+
+        def count(a, b, by):
+            counted[0] += b - a
+            compact(CZ, a, b, QB, by, first=counted[0] == b - a, last=counted[0] == V)
+
+        def fused(lo, hi):
+            for a, b in cut(max(lo, f0), max(lo, min(hi, f1)), TUNE["cmp"]):
+                l = lst("LS", 128 * n, a, b)
+                if t < 3:
+                    v_tt(part(NEXT, a, b, V), (W, lo, 2 * V), part(beside[0], a, b, beside[1]), A.add, lst=l)
+                else:
+                    v_tt(part(CZ, a, b), (W, lo, 2 * V), part(beside[0], a, b, beside[1]), A.is_gt, lst=l)
+                    count(a, b, "over2")
 
         def winners(j, lo, hi):
-            make_list(CM, n, lo, hi, ("Q", 512 * (j % 2 if t < 3 else 0)), True)
-            for a, b in cut(lo, hi, 512):
-                for c, d in cut(a, b, TUNE["last"] if lo == 0 else 512):
+            make_list(CM, n, t, lo, hi, ("Q", 512 * (j % 2 if t < 3 else 0)), True)
+            if not t:
+                for c, d in cut(lo, hi, TUNE["last"] if lo == 0 else 512):
                     cp("*", part(PN, c, d), (W, lo, 2 * V), lst=lst("LS", 128 * n, c, d))
-                if t in (1, 2):
-                    close_window(a // 512, PN)
-                if t == 3:
+                return
+            for a, b in picked:
+                if lo <= a < hi:
                     o = part("P", a, b)
-                    pe(group(o, [(N2, part(PN, a, b))], False, True), acc=True)
-                    either(lambda: v_ts(part(CZ, a, b), o, -1.0, A.max, 1.0, A.min), lambda: s_act(part(CZ, a, b), o, F.Sign))
-                    compact(CZ, a, b, ("Q", 512, 640), first=b == V, last=a == 0)
+                    cp("S", part(PN, a, b), (W, lo, 2 * V), lst=lst("LS", 128 * n, a, b))
+                    pe(group(o, [(N2 if t == 3 else ID, part(PN, a, b))], False, True), acc=True)
+                    if t < 3:
+                        cp("*", part(NEXT, a, b, V), o)
+                    else:
+                        either(lambda: v_ts(part(CZ, a, b), o, -1.0, A.max, 1.0, A.min), lambda: s_act(part(CZ, a, b), o, F.Sign))
+                        count(a, b, "over")
+            mine.append((lo, hi))
 
+        vote = ("vote0", 0) if t == 2 else ("vote1", 32 * (t - 1))
+        late, mine = [], []
         waiting = []
         for j, (lo, hi) in enumerate(TUNE["pieces"]):
-            for a, b in cut(lo, hi, TUNE["cmp"]):
-                if a // 512 not in helped:
-                    v_tt(part(W, a, b), costs, part("DL", a, b), A.add, lst=lst("AB16", 0, a, b))
-                    while waiting:
-                        winners(*waiting.pop())
-            for a, b in cut(lo, hi, TUNE["cmp"]):
-                v_tt(part(CM, a, b), costs, part(W, a, b), A.is_lt, lst=lst("AB16", 128, a, b))
-                if t == 3 and not first:
-                    compact(CM, a, b, ("Q", 512, 640), first=b == V, last=a == 0)
+            for a, b in cut(max(lo, helped), max(hi, helped), TUNE["cmp"]):
+                v_tt(part(W, a, b), costs, part(edges[t][0], a, b, edges[t][1] - OWN), A.add, lst=lst("AB16", 256 * t, a, b))
                 while waiting:
+                    winners(*waiting.pop())
+            for a, b in cut(lo, hi, TUNE["cmp"]):
+                v_tt(part(CM, a, b), costs, part(W, a, b), A.is_lt, lst=lst("AB16", 256 * t + 128, a, b))
+                if t == 3 and not first:
+                    compact(CM, a, b, QB, *vote, first=b == V, last=a == 0)
+                    if a == lo:
+                        late.append((lo, hi))
+                while waiting and (a == lo or not TUNE["hold"]):
                     winners(*waiting.pop())
             if t < 3 or first:
                 waiting.append((j, lo, hi))
+        while mine and TUNE["hold"] < 2:
+            fused(*mine.pop(0))
         while waiting:
             winners(*waiting.pop())
+        while mine:
+            fused(*mine.pop(0))
         in_line(begin, "V")
-        sg = ch("SG", t, 128)
-        o = ("Q", 0, 128) if t == 3 and first else ("Q", 512, 640)
+        sg = gate(n)
+        o = ("Q", 0, 256) if t == 3 and first else QB
         if t in (1, 2) or t == 3 and first:
-            compact(CM, 0, V, o)
+            for a, b in cut(0, V, 512):
+                compact(CM, a, b, o, *vote, first=b == V, last=a == 0)
         if t in (1, 2):
             cur[0] = 1 - cur[0]
-        if t:
-            either(lambda: v_ts(sg, o, -1.0 / BIG, A.mult, 8.5, A.add), lambda: s_act(sg, o, F.Identity, bias=8.5, scale=-1.0 / BIG))
+            either(lambda: v_ts(sg, o, pf("cut"), A.add, 1.0, A.min), lambda: s_act(sg, o, F.Sign, bias=pf("cut")))
         if t == 3:
+            mw = ("MW", 0, 256)
+            s_act(sg, o, F.Sign, bias=pf("cut"))
             if first:
-                v_ts(("MW", 0, 128), ("Q", 512, 640), -BIG, A.is_le)
-            v_tt(("CC", 0, 128), ("MW", 0, 128), sg, A.mult)
-            if not first:
-                make_list(CM, n, 0, V, ("P", 0), False)
+                either(lambda: v_ts(mw, QB, pf("nine"), A.add, 1.0, A.min), lambda: s_act(mw, QB, F.Sign, bias=pf("nine")))
+            else:
+                for j, (lo, hi) in enumerate(late):
+                    make_list(CM, n, t, lo, hi, ("P", 512 * (j % 2)), False)
         if t > 1:
-            predecessors(n)
+            predecessors(n, t)
 
     def join_x():
         dma("Y", [(T.XR[:, 0:V], T.dH[:])], [("dH", 0, 1)], [("XR", 0, V)], 4.0)
         for a, b in cut(0, V, TUNE["join"]):
-            dma("G", [(T.XR[32:128, a:b], T.YA[0:96, a:b]), (T.XR[0:32, a:b], T.YA[96:128, a:b])], [("YA", a, b)], [("XR", a, b)],
-                4.5 + 4.5 * (b - a) / V, accum_op=A.add, max_dma_last_dim=4096)
+            dma("G", [(T.XR[:, a:b], T.YA[:, a:b])], [("YA", a, b)], [("XR", a, b)],
+                3.2 + 4.5 * (b - a) / V, accum_op=A.add, max_dma_last_dim=4096)
 
-    def turn_x():
-        for a, b in cut(0, V, 1024):
-            dma("Y", [(T.XS[32:128, a:b], T.X[0:96, a:b]), (T.XS[0:32, a:b], T.X[96:128, a:b])], [("X", a, b)], [("XS", a, b)], 4.8)
-
-    terms, slots = [0], [0]
+    slots = [0]
 
     def next_ex(n):
         if slots[0] + n > SCRATCH["EX"][1][1]:
@@ -499,12 +641,6 @@ def build(g, core, T, topo):
             dma("Y", pair, [e], wr, 3.2)
         else:
             dma("G", pair, [e], wr, 3.6 + width(e) / 512 * TUNE["acc"], accum_op=A.add, max_dma_last_dim=2048)
-
-    free = [ch("R", 0), ch("R", 1)]
-
-    def bank():
-        terms[0] += 1
-        return free[terms[0] % len(free)]
 
     def term(p, pairs, off, half, v_abs, plus):
         lo, hi = GAIN[p]
@@ -529,29 +665,49 @@ def build(g, core, T, topo):
     walked = [None] * 3
 
     def walk_back(f):
-        qa, qb = ("Q", 0, 128), ("Q", 512, 640)
-        for t in (3, 2, 1):
-            if t == 1:
-                pe(group(qa, [(ID, ch("MM", 0, 128)), (ID, ch("MM", 1, 128))], True, False))
-            lend = f in TUNE["lend"]
-            pe(group(qb, [(ID, ch("C16", int(lend), 128)), (NID, ("SP", 128, 256))], True, False))
-            for a, b in TUNE["walk"]:
-                v_tt(part("YA", a, b), ("CC", 0, 128), part("THR", a, b), A.is_gt, lst=lst("INV", 0, a, b))
-                if lend and b <= TUNE["lent"]:
-                    v_ts(part("YB", a, b), ("CC", 0, 128), -0.25, A.is_lt, 2.0, A.mult, lst=lst("INV", 128, a, b))
+        found, H = ["YB"] * 4, V // 2
+        apart = f % 2 == 0
+
+        def cc(n, x):
+            return ch("CC", 4 * n + x, 256)
+
+        def gates(n, x):
+            ahead = [(ch("DG", 2 * n + b, 128), gate(3 * f + 4 - b - x)) for b in range(2) if 0 < 4 - b - x < 4]
+            ahead += [(ch("DG", 2 * n + 1 - x, 128), ("MW", 0, 256))] if x < 2 else []
+            pe(group(("Q", 512 * n, 512 * n + 256), ahead, True, x == 0))
+
+        def marks(n, x):
+            s_act(cc(n, x), ("Q", 512 * n, 512 * n + 256), F.Sign, bias=pf("end") if x == 3 else -2.0)
+
+        for n in range(2):
+            gates(n, 0)
+            marks(n, 0)
+        for x in range(4):
+            for n in range(2):
+                tile = 2 * (x % 2) + n
+                o = ("Q", 512 * n * apart, 512 * n * apart + 128)
+                if x < 3:
+                    gates(n, x + 1)
                 else:
-                    s_act(part("YB", a, b), ("CC", 0, 128), F.Sign, bias=-0.25, scale=-1.0, lst=lst("INV", 128, a, b))
-                compact("YA", a, b, qa, 1, first=t > 1 and b == V, last=a == 0)
-                compact("YB", a, b, qb, 1, first=False, last=a == 0, weights="SELW")
-            m = ch("MM", 3 - t, 128)
-            walked[3 - t] = len(ops) - 1
-            v_tt(("TI", 0, 128), qb, ("SP", 0, 128), A.mult)
-            v_ts(("TJ", 0, 128), ("TI", 0, 128), 1, A.bitwise_and)
-            v_tt(m, qa, ("TJ", 0, 128), A.add)
-            if t > 1:
-                v_tt(("CC", 0, 128), m, ch("SG", t - 1, 128), A.mult)
-            else:
-                v_ts(ch("UW", f, 128), m, 0.0, A.is_gt)
+                    pe(group(o, [(mat("sum1" if y == 1 else "sum", 32 * (y % 2) + 16 * n + e, 48), part("CC", 128 * e, 128 * e + 128, cc(n, y)[1]))
+                                 for y in (1, 2, 3) for e in range(2)], apart or n == 0, False), acc=not (apart or n == 0))
+                for a, b in TUNE["walk"]:
+                    v_tt(part(found[x], a, b, H * n), cc(n, x), part("THR", a, b, H * tile), A.is_gt, lst=lst("INV", 64 * tile, a, b))
+                    if (x, n, b) == TUNE["lists"][f]:
+                        ops[-1]["after"] = listed[0]
+                    if x < 3:
+                        compact(found[x], a, b, ("Q", 512 * n, 512 * n + 256), "on", 64 * (1 - x % 2), first=False, last=a == 0, base=H * n)
+                    else:
+                        compact(found[x], a, b, o, "out", 16 - 16 * n, 128, first=False, last=a == 0 and n == 1 - apart, base=H * n)
+                if x < 3:
+                    walked[x] = len(ops) - 1
+                    marks(n, x + 1)
+                elif apart or n:
+                    uw = ch("UW", f if n else 4 + f // 2, 128)
+                    if apart and n:
+                        pe(group(o, [(ID, ch("UW", 4 + f // 2, 128))], False, True), acc=True)
+                    none = pf("none%d" % n if apart else "none")
+                    either(lambda: v_ts(uw, o, none, A.add, 0.0, A.is_gt), lambda: s_act(uw, o, F.Sign, bias=none))
 
     def forest(f, marks):
         first, last = f % 2 == 0, f == 3
@@ -561,29 +717,30 @@ def build(g, core, T, topo):
         for lo, hi in TUNE["pieces"]:
             for a, b in cut(lo, hi, wide):
                 l = lst("LS", 128 * (3 * f + 1), a, b)
-                either(lambda: v_ts(part("YA", a, b), ("HW", lo, 2 * V), 32.0, A.mult, lst=l),
-                       lambda: s_act(part("YA", a, b), ("HW", lo, 2 * V), F.Identity, scale=32.0, lst=l))
+                either(lambda: v_ts(part("YA", a, b), ("HX", lo, 2 * V), 32.0, A.mult, lst=l),
+                       lambda: s_act(part("YA", a, b), ("HX", lo, 2 * V), F.Identity, scale=32.0, lst=l))
         join_x()
         step(3 * f + 2, 2, first, marks, "PN")
         for a, b in cut(0, V, wide):
             cp("*", part("X", a, b), ("XR", 0, V), lst=lst("LP", 128 * (3 * f + 2), a, b))
-        turn_x()
         step(3 * f + 3, 3, first, marks, "PN")
         walk_back(f)
         for a, b in cut(0, V, wide)[::-1]:
             l = lst("LP", 128 * (3 * f + 3), a, b)
             cp("*", part("T3" + P, a, b), ("HW", V, 2 * V), lst=l)
-            cp("*", part("T1" + P, a, b), ("XS", 0, V), lst=l)
+            cp("*", part("T1" + P, a, b), ("X", 0, V), lst=l)
             if f in TUNE["t2"]:
                 v_ts(part("T2" + P, a, b), part("T1" + P, a, b), HI - 15.5, A.add)
             else:
                 either(lambda: v_ts(part("T2" + P, a, b), part("T1" + P, a, b), HI - 15.5, A.add),
                        lambda: s_act(part("T2" + P, a, b), part("T1" + P, a, b), F.Identity, bias=HI - 15.5))
-        v_ts(ch("WIN", min(f, 1), 128), ch("SG", 3, 128), 0.0, A.is_lt, 0.25 if first else 0.125, A.mult)
-        if f:
-            v_tt(ch("WIN", 0, 128), ch("WIN", 0, 128), ch("WIN", 1, 128), A.add)
         if last:
             free.extend(ch("P", k) for k in range(4))
+            o, win = bank(), ("WIN", 0, 128)
+            o = (o[0], o[1], o[1] + 128)
+            pe(group(o, [(mat("win" + "AB"[x % 2], e), part("SG", 128 * e, 128 * e + 128, gate(3 * x + 3)[1]))
+                         for x in range(4) for e in range(2)]))
+            either(lambda: v_ts(win, o, 0.125, A.mult, 0.375, A.add), lambda: s_act(win, o, F.Identity, bias=0.375, scale=0.125))
             for k in range(4):
                 o = bank()
                 pe(summed(o, k, [], ch("WIN", 0, 128)))
@@ -607,16 +764,21 @@ def build(g, core, T, topo):
 
     def new_tolls(o, k, small, old, new):
         pe(group(o, [(ID, ch(old, k))], True, False))
-        pe(spread(o, k, small, False, True), acc=True)
+        pe(spread(o, 512 * k, 512 * k + 512, small, False, True), acc=True)
         v_ts(ch(new, k), o, 0.0, A.max, 63.0, A.min)
 
+    def tolls_and_edges():
+        dma("Y", [(T.ED[:], T.DB[:])], [("DB", 0, V)], [("ED", 0, V)], 3.0)
+        dma("G", [(T.ED[:], T.E[:])], [("E", 0, V)], [("ED", 0, V)], 5.0, accum_op=A.add, max_dma_last_dim=4096)
+
     step(0, 0, True, None, "PN0")
+    turned("Y", ("DA", 0, V - OWN), ("DL", OWN, V), 3, 2.4 + 1.6 * (V - OWN) / V)
     for p, (lo, hi) in enumerate(GAIN):
         e, e2 = next_ex(hi - lo), next_ex(hi - lo)
         for k in range(lo // 512, hi // 512):
             ea, less = ch("EX", k, base=e[1] - lo), ch("EX", k, base=e2[1] - lo)
-            s_act(ea, ch("DA", k), F.Exp, bias=math.log(3.0), scale=-0.125)
-            s_act(ch("GD", k), ch("DB", k), F.Exp, scale=-0.125)
+            s_act(ea, ch("T2A", k), F.Exp, bias=math.log(3.0), scale=-0.125)
+            s_act(ch("GD", k), ch("T2B", k), F.Exp, scale=-0.125)
             either(lambda: v_ts(less, ea, -1.0 / 3, A.mult), lambda: s_act(less, ea, F.Identity, scale=-1.0 / 3))
         stage(e, p, True)
         dma("G", [(ap(("GD", lo, hi)), ap(e2))], [e2], [("GD", lo, hi)], 5.0, accum_op=A.add, max_dma_last_dim=2048)
@@ -624,28 +786,33 @@ def build(g, core, T, topo):
         f = 2 * rnd
         if rnd:
             v_tt(ch("DLT", 0, 128), ch("UW", 0, 128), ch("UW", 1, 128), A.subtract)
-            open_window([(ROT, "PN0"), (ROT, "DB")])
+            open_window(["PN0", "DB"])
             for k in (3, 2, 1, 0):
                 new_tolls(ch("Q", k % 2), k, ch("DLT", 0, 128), "E", "E")
                 close_window(k, "E")
+            tolls_and_edges()
             dma("Y", [(T.stN[:], T.E[:])], [("E", 0, V)], [("stN", 0, 4)], 3.0)
             exchange(7, "N", 4.4)
             dma("Y", [(T.lnN[q], T.stN[q])], [("stN", 0, 4)], [("lnN", q, q + 1)], 2.4)
             dma("Y", [(T.EN[:], T.lnN[:])], [("lnN", 0, 4)], [("EN", 0, V)], 3.0)
         else:
-            open_window([(ROT, "E"), (ROT, "DB")])
+            open_window(["E", "DB"])
             for k in (3, 2, 1, 0):
                 close_window(k, "PN0")
+            tolls_and_edges()
         cur[0] = 1 - cur[0]
         forest(f, None)
-        send(5 + rnd, [((q - 1) % 4, ap(ch("UW", f, 128)), ap(ch("RU", rnd, 128)))], [ch("UW", f, 128)], [ch("RU", rnd, 128)], 0.6)
-        open_window([(ROT, "PN0"), (ROT, "DB"), (ROT, "E")])
-        pe(group(("Q", 0, 128), [(("M1", 96, 224), ch("UW", f, 128)), (("M2", 96, 224), ch("RU", rnd, 128))]))
+        send(5 + rnd, [((q - 1) % 4, ap(ch("UW", 4 + rnd, 128)), ap(ch("RU", rnd, 128)))], [ch("UW", 4 + rnd, 128)], [ch("RU", rnd, 128)], 0.6)
+        open_window(["PN0", "ED"])
+        for t in range(3):
+            o = ("Q", 0, 128) if t == 0 else ("Q", 384 + 128 * t, 512 + 128 * t)
+            pe(group(o, [(("M1", 32 * t, 32 * t + 128), ch("UW", f, 128)), (("M2", 32 * t, 32 * t + 128), ch("RU", rnd, 128))]))
         cp("*", ("ADW", 0, 128), ("Q", 0, 128))
+        cp("*", ("ADW", 128, 384), ("Q", 512, 768))
         for k in (3, 2, 1, 0):
             close_window(k, None, ("ADW", 0, 128))
         cur[0] = 1 - cur[0]
-        forest(f + 1, ("ADW", 0, 128))
+        forest(f + 1, True)
 
     mine = ch("DLT", 1, 128)
     v_tt(mine, ch("UW", 2, 128), ch("UW", 3, 128), A.subtract)
@@ -659,9 +826,9 @@ def build(g, core, T, topo):
         dma("Y", [(T.tollout[:, 512 * k:512 * k + 512], ap(ch("W0", k)))], [ch("W0", k)], [], 2.5)
     for p, (lo, hi) in enumerate(GAIN):
         st, ln = "stG%d" % p, "lnG%d" % p
-        send(9 + p, [(r, T[st][(r + 3) % 4], T[ln][q]) for r in others], [(st, 0, 4)], [(ln, r, r + 1) for r in others],
+        send(9 + p, [(r, T[st][r], T[ln][q]) for r in others], [(st, 0, 4)], [(ln, r, r + 1) for r in others],
              2.7 * (hi - lo) / 512)
-        dma("Y", [(T.gain[rows, lo:hi], T[st][(q + 3) % 4])], [(st, 0, 4)], [], 2.8)
+        dma("Y", [(T.gain[rows, lo:hi], T[st][q])], [(st, 0, 4)], [], 2.8)
         dma("Y", [(T.gain[32 * r:32 * r + 32, lo:hi], T[ln][r]) for r in others], [(ln, r, r + 1) for r in others], [], 3.0)
     return ops
 

@@ -5,10 +5,11 @@ from concourse.mybir import AluOpType, ActivationFunctionType
 V = 2048
 BIG = 8192.0
 CUT = 8.5 * BIG
-HI = 6144.0
+HI = 192.0
+BOTH = 512
 FUSED = 1280
 BF, F32, F16, I32, U16 = "bfloat16", "float32", "float16", "int32", "uint16"
-GAIN = [(0, 512), (512, 1024), (1024, 1536), (1536, 2048)]
+GAIN = [(0, 512), (512, 1024), (1024, 1536), (1536, 1792), (1792, 2048)]
 
 
 def _sb(n, d):
@@ -17,23 +18,23 @@ def _sb(n, d):
 
 SCRATCH = {
     "W0": _sb(2 * V, F32), "W1": _sb(2 * V, F32), "CM0": _sb(V, BF), "CM1": _sb(V, BF), "PN": _sb(V, F16),
-    "FD": _sb(2 * FUSED, BF), "ZB": _sb(FUSED, F16), "HX": _sb(2 * V, BF),
+    "FD": _sb(2 * FUSED, BF), "ZB": _sb(FUSED, F16), "HX": _sb(2 * V, BF), "DC": _sb(V // 2, BF),
     "PN0": _sb(V, F16), "TM": _sb(1536, F16), "DA": _sb(V, BF), "DB": _sb(V, BF), "DL": _sb(V, BF), "E": _sb(V, BF),
     "H": _sb(V, BF), "HW": _sb(2 * V, BF), "dH": ("dram", [128, V], F32),
     "X": _sb(V, F32), "XR": _sb(V, F32), "T1A": _sb(V, F16), "T1B": _sb(V, F16), "T2A": _sb(V, BF),
-    "T2B": _sb(V, BF), "T3A": _sb(V, BF), "T3B": _sb(V, BF), "AB": _sb(V, BF), "EX": _sb(4608, F32),
-    "YA": _sb(V, BF), "YB": _sb(V, BF), "ED": _sb(V, BF), "THR": _sb(2 * V, BF), "MAT": _sb(1824, BF),
+    "T2B": _sb(V, BF), "YA": _sb(V, BF), "AB": _sb(2 * V, BF), "EX": _sb(5120, F32),
+    "YB": _sb(V, BF), "ED": _sb(V, BF), "THR": _sb(2 * V, BF), "MAT": _sb(1824, BF),
     "UNW": _sb(V, BF), "EN": _sb(V, BF), "GD": _sb(V, F32), "DLT": _sb(256, BF), "DH": _sb(512, BF), "DN": _sb(128, BF),
-    "SELF": _sb(144, F32), "IV": _sb(256, U16), "DG": _sb(512, BF),
+    "ROW": _sb(8, F32), "IF": _sb(128, F32), "LT": _sb(256, F32), "IV": _sb(256, U16), "DG": _sb(512, BF),
     "LI": _sb(256, I32), "ZI": _sb(128, I32), "ZC": _sb(128, F16), "AB16": _sb(1024, U16), "INV": _sb(256, U16),
     "AP": _sb(512, F32), "BP": _sb(512, F32), "VP": _sb(128, F32), "LX": _sb(384, F32), "LY": _sb(128, F32),
-    "LZ": _sb(256, I32), "LS": _sb(13 * 128, U16), "LP": _sb(13 * 128, U16),
+    "LZ": _sb(256, I32), "LS": _sb(384, U16), "LP": _sb(512, U16), "T3B": _sb(V, BF),
     "SG": _sb(6 * 256, BF), "MW": _sb(256, BF), "CC": _sb(2048, BF), "UW": _sb(768, BF),
     "RU": _sb(256, BF), "ADW": _sb(384, BF), "TI": _sb(256, I32), "TJ": _sb(256, I32),
-    "DJ": _sb(128, F32), "GJ": _sb(128, F32), "J16": _sb(16, F32), "PI": _sb(12, I32), "PF": _sb(28, F32),
+    "PI": _sb(16, I32), "PF": _sb(32, F32), "LIFT": _sb(64, BF),
     "JP": _sb(192, F32), "YS": _sb(256, BF), "YG": _sb(224, BF), "YD": _sb(128, BF), "SGN": _sb(224, BF),
-    "MK": _sb(16, F32), "MK4": _sb(16, F32), "BLK": _sb(128, BF), "II": _sb(256, BF), "NID": _sb(128, BF),
-    "N32M": _sb(128, BF), "N2M": _sb(256, BF), "WIN": _sb(128, BF), "M1": _sb(256, BF),
+    "II": _sb(256, BF), "NID": _sb(128, BF),
+    "M32": _sb(256, BF), "N2M": _sb(256, BF), "WIN": _sb(128, BF), "M1": _sb(256, BF),
     "M2": _sb(256, BF),
     "stL": ("dram", [4, 128, 64], I32), "lnL": ("dram", [4, 128, 64], I32),
     "stZ": ("dram", [4, 128, 32], I32), "lnZ": ("dram", [4, 128, 32], I32),
@@ -43,6 +44,7 @@ SCRATCH = {
     "stT": ("dram", [8, 128, 256], BF), "lnT": ("dram", [8, 128, 256], BF),
     "stI": ("dram", [8, 128, 32], U16), "lnI": ("dram", [8, 128, 32], U16),
     "stN": ("dram", [4, 128, 512], BF), "lnN": ("dram", [4, 128, 512], BF),
+    "dG": ("dram", [128, V], F32),
 }
 for _p, (_lo, _hi) in enumerate(GAIN):
     SCRATCH["stG%d" % _p] = SCRATCH["lnG%d" % _p] = ("dram", [4, 128, (_hi - _lo) // 4], F32)
@@ -51,28 +53,30 @@ for _n, _w in (("sel", 144), ("vote0", 144), ("vote1", 208), ("over", 144), ("ov
                ("sum", 192), ("sum1", 192), ("winA", 144), ("winB", 144)):
     MATS[_n] = (_at, _w)
     _at += _w
-COLS = ["p", "group", "row", "net", "and112", "and14", "and64", "and78", "and95", "slot", "odd", "mid", "net0", "slot0",
-        "even", "at", "at0", "at1", "to", "on", "home", "cut", "end", "none", "none0", "none1", "flip", "nine"]
+COLS = ["row", "net", "and112", "and14", "and64", "and78", "slot", "odd", "mid", "slot0",
+        "even", "at", "at0", "at1", "to", "on", "home", "cut", "end", "none", "none0", "none1", "flip", "nine", "cut2"]
 PSUM = {"P": 2048, "Q": 1024, "R": 1024}
 for _n in PSUM:
     SCRATCH[_n] = ("psum", [128, PSUM[_n]], F32)
 
-N_DMA_SEMS = 125
-SEMAPHORES = ["eV", "eS", "eT", "eG", "sent"] + ["rx%d" % k for k in range(17)] + ["d%d" % k for k in range(N_DMA_SEMS)]
+N_DMA_SEMS = 121
+SEMAPHORES = ["eV", "eS", "eT", "eG", "sent"] + ["rx%d" % k for k in range(24)] + ["d%d" % k for k in range(N_DMA_SEMS)]
 
 CY, PCY, GA, LAT = 0.00083, 0.00045, 1.56, 0.09
 ORDER = {}
-QUEUES = "VSTGYXZ"
+QUEUES = "VSTGYXDZ"
 SIDE = ("X", "XR", "XS", "YA", "T1A", "T1B", "T2A", "T2B", "T3B", "AB", "EX", "GD", "WIN")
 TUNE = {"pieces": [(1024, 2048), (0, 1024)], "cmp": 512, "last": 256,
         "help": [1024] * 13, "aid": 512, "banks": [1, 0], "fused": [(256, 1536)] * 13, "hold": 0,
-        "lists": [(0, 0, 1024), (0, 0, 512)] * 2, "apart": [1, 7], "pull": 0.5, "any": 0.5, "cases": 3, "moves": 14000, "far": 12, "slack": 0.0, "own": 0.0, "urgent": 1.0, "hops": 1, "share": 0.3, "lean": 0.1, "side": 3.0, "walk": [(512, 1024), (0, 512)],
-        "join": 1024, "with": 4, "back": True, "pace": [], "t2": [0, 1, 2, 3], "v_db": [], "wide": 512, "v_abs": [[], [], [], []], "skew": 5.0, "acc": 0.9,
-        "passes": 4, "seed": 2, "turns": 1, "shake": 2.0, "span": 100.0}
-CASES = [{"g": 1.0, "c": 1.0, "p": 1.0, "d": 1.0, "w": 1.0, "weight": 1.0},
-         {"g": 0.9, "c": 1.1, "p": 1.2, "d": 1.5, "w": 1.5, "weight": 0.6},
-         {"g": 1.6, "c": 1.3, "p": 1.3, "d": 1.0, "w": 1.0, "weight": 0.5},
-         {"g": 1.25, "c": 1.25, "p": 1.6, "d": 1.3, "w": 2.0, "weight": 0.4}]
+        "lists": [[None, (0, 0, 1024)], [None, (0, 0, 256)]] * 2, "apart": [1, 7], "walk": [(256, 1024), (0, 256)],
+        "terms": GAIN, "t2": [0, 1, 2, 3], "join": 1024, "gates": 512, "ends": 512, "broad": 512, "early": 15.0, "both": [6, 12], "third": 2, "head": 1024,
+        "wide": 512, "v_abs": [], "skew": 5.0, "acc": 0.9, "rate": 5e5, "dma": 0.85, "behind": None,
+        "own": 0.0, "urgent": 1.0, "hops": 1, "share": 0.3, "lean": 0.5, "side": 3.0, "passes": 4, "seed": 2,
+        "pull": 0.3, "cases": 3, "moves": 11000, "span": 10.0, "reach": 14.0, "batch": 16}
+CASES = [{"g": 1.0, "s": 1.0, "c": 1.0, "p": 1.0, "d": 1.0, "w": 1.0, "weight": 1.0},
+         {"g": 0.95, "s": 1.4, "c": 1.3, "p": 1.3, "d": 1.5, "w": 1.6, "weight": 0.8},
+         {"g": 1.6, "s": 1.8, "c": 1.25, "p": 1.25, "d": 1.1, "w": 1.2, "weight": 0.7},
+         {"g": 1.25, "s": 1.6, "c": 1.25, "p": 1.6, "d": 1.3, "w": 2.0, "weight": 0.4}]
 
 
 def split_engines(topo, src, dsts):
@@ -98,12 +102,14 @@ def build(g, core, T, topo):
     cores = list(T.cores)
     others = [r for r in range(4) if r != q]
     A, F = AluOpType, ActivationFunctionType
-    ops = []
+    ops, dmas = [], [0]
     bias = [0.0]
 
     def add(eng, fn, rd, wr, dur, kind="c", issue=None, after=None, acc=False, sem=None, count=0):
         listed = any(x[0] in ("AB16", "INV", "LS", "LP") for x in rd)
         cls = "p" if eng == "T" else "d" if kind != "c" else "g" if listed else "c"
+        if kind == "x":
+            dur, issue = dur * TUNE["dma"], issue and issue * TUNE["dma"]
         ops.append({"cls": cls, "eng": eng, "fn": fn, "rd": rd, "wr": wr, "dur": dur, "kind": kind, "acc": acc,
                     "bias": bias[0] - (TUNE["side"] if any(x[0] in SIDE for x in wr + rd) else 0.0),
                     "issue": dur if issue is None else issue, "after": after, "sem": sem, "count": count})
@@ -158,13 +164,15 @@ def build(g, core, T, topo):
         on_v()
         ops[-1]["alt"] = {"V": (ops[-1]["fn"], ops[-1]["dur"]), "S": (other["fn"], other["dur"])}
 
-    def cp(eng, o, a, lst=None):
-        if eng == "V":
+    def cp(eng, o, a, lst=None, times=1.0, plus=0.0):
+        if eng == "V" and (times, plus) == (1.0, 0.0):
             v_cp(o, a, lst)
+        elif eng == "V":
+            v_ts(o, a, times, A.mult, plus, A.add, lst=lst)
         elif eng == "S":
-            s_act(o, a, F.Identity, lst=lst)
+            s_act(o, a, F.Identity, bias=plus, scale=times, lst=lst)
         else:
-            either(lambda: v_cp(o, a, lst), lambda: s_act(o, a, F.Identity, lst=lst))
+            either(lambda: cp("V", o, a, lst, times, plus), lambda: cp("S", o, a, lst, times, plus))
 
     def pe(mms, acc=False):
         def fn():
@@ -181,9 +189,15 @@ def build(g, core, T, topo):
         return [(o, l, r, first and k == 0, last and k == len(pairs) - 1) for k, (l, r) in enumerate(pairs)]
 
     def dma(eng, pairs, rd, wr, dur, **kw):
-        queue = {"Y": g.sync, "S": g.scalar, "G": g}[eng]
-        return add(eng, lambda: [queue.dma_start(o, i, **kw) for o, i in pairs], rd, wr, dur, kind="d",
-                   issue=(1.3 if eng == "G" else 0.06) * len(pairs))
+        queue, done = {"Y": g.sync, "S": g.scalar, "G": g}[eng], {"sem": "d%d" % dmas[0], "count": 16 * len(pairs)}
+        dmas[0] += 1
+        size = sum((x[2] - x[1]) * (128 if len(SCRATCH[x[0]][1]) == 2 else math.prod(SCRATCH[x[0]][1][1:])) * (2 if two(x) else 4)
+                   for x in wr or rd)
+        hold, issue = size * (2 if kw else 1) / TUNE["rate"], (1.3 if eng == "G" else 0.06) * len(pairs)
+        me = add(eng, lambda: [queue.dma_start(o, i, **kw) for o, i in pairs], rd, wr, min(issue, 1.0), kind="d", issue=issue, **done)
+        moved = add("D", None, [], [], hold, kind="x", after=me, **done)
+        add("Z", None, rd, wr, max(dur - hold - min(issue, 1.0), 1.0), kind="x", issue=0.0, after=moved, **done)
+        return me
 
     def send(k, plan, rd, wr, dur):
         masks = split_engines(topo, core, [cores[r] for r, _, _ in plan])
@@ -216,7 +230,7 @@ def build(g, core, T, topo):
         return (name, base + k * n, base + (k + 1) * n)
 
     def part(name, lo, hi, base=0):
-        return (name, base + lo, base + hi)
+        return ("AB", V + lo, V + hi) if name == "T3A" else (name, base + lo, base + hi)
 
     def lst(name, base, lo, hi):
         return (name, base + lo // 16, base + hi // 16)
@@ -224,7 +238,7 @@ def build(g, core, T, topo):
     def cut(lo, hi, n):
         return [(a, min(a + n, hi)) for a in range(lo, hi, n)][::-1]
 
-    ID, NID, N2 = ("II", 0, 128), ("NID", 0, 128), ("N2M", 0, 128)
+    ID, NID, N2, N32, P32 = ("II", 0, 128), ("NID", 0, 128), ("N2M", 0, 128), ("M32", 0, 128), ("M32", 128, 256)
 
     def rot(t):
         return ("II", 32 * t, 32 * t + 128)
@@ -245,138 +259,139 @@ def build(g, core, T, topo):
     rows = slice(32 * q, 32 * q + 32)
     dma("Y", [(T.stL[:, 0:64, :], T.sa[:]), (T.stL[:, 64:128, :], T.sb[:])], [], [("stL", 0, 4)], 2.2)
     dma("S", [(T.TI[:, 0:128], T.sa[:]), (T.TI[:, 128:256], T.sb[:])], [], [("TI", 0, 256)], 2.4)
-    ops[-1]["bias"] = 50.0
-    dma("Y", [(T.stH[:], T.hf[:])], [], [("stH", 0, 4)], 2.8)
-    ops[-1]["bias"] = 50.0
+    ops[-3]["bias"] = 50.0
+    features = dma("Y", [(T.stH[:], T.hf[:])], [], [("stH", 0, 4)], 2.8)
+    ops[-3]["after"], ops[-2]["more"] = 0, 4
     dma("S", [(T.lnL[q, 0:64, :], T.sa[rows]), (T.lnL[q, 64:128, :], T.sb[rows])], [], [("lnL", q, q + 1)], 2.2)
     later = [("stH", 0, 4)]
-    dma("Y", [(T.stP[:], T.p0[:])], later, [("stP", 0, 4)], 2.8)
+    dma("S", [(T.AB[:, 0:V], T.p0[:])], [], [("AB", 0, V)], 2.8)
+    ops[-2]["more"] = features + 1
+    cp("V", ("AB", 0, V), ("AB", 0, V), plus=-128.0)
+    lowered = len(ops) - 1
+    dma("Y", [(T.stP[:], T.AB[:, 0:V]), (T.lnP[q], T.AB[rows, 0:V])], [("AB", 0, V)], [("stP", 0, 4), ("lnP", q, q + 1)], 3.2)
     dma("Y", [(T.stE[:], T.toll[:])], later, [("stE", 0, 4)], 3.0)
     dma("Y", [(T.stZ[:], T.lim[:])], later, [("stZ", 0, 4)], 2.6)
-    dma("Y", [(T.lnH[q], T.hf[rows]), (T.lnP[q], T.p0[rows]), (T.lnE[q], T.toll[rows]), (T.lnZ[q], T.lim[2 * q:2 * q + 2])],
-        later, [("lnH", q, q + 1), ("lnP", q, q + 1), ("lnE", q, q + 1), ("lnZ", q, q + 1)], 3.0)
+    dma("Y", [(T.lnH[q], T.hf[rows]), (T.lnE[q], T.toll[rows]), (T.lnZ[q], T.lim[2 * q:2 * q + 2])],
+        later, [("lnH", q, q + 1), ("lnE", q, q + 1), ("lnZ", q, q + 1)], 3.0)
 
     def iota(o, pat, base, cm):
         small = SCRATCH[o[0]][2] != I32
         add("G", lambda: [g.iota(ap(o), pat, base, cm, allow_small_or_imprecise_dtypes=small)], [], [o], 0.13 + 2 * width(o) * CY)
 
-    def exchange(k, nm, dur):
-        send(k, [(r, T["st" + nm][r], T["ln" + nm][q]) for r in others], [("st" + nm, 0, 4)],
+    def select(o, a, pat, op, fill, base, cm=-1):
+        add("G", lambda: [g.affine_select(ap(o), ap(a), pat, op, fill, base, cm)], [a], [o], 0.17 + 2 * width(o) * CY)
+
+    def exchange(k, nm, dur, behind=()):
+        send(k, [(r, T["st" + nm][r], T["ln" + nm][q]) for r in others], [("st" + nm, 0, 4), *behind],
              [("ln" + nm, r, r + 1) for r in others], dur)
 
     first_g = len(ops)
-    iota(("PI", 0, 1), [[0, 1]], 0, 1)
+    iota(("PI", 8, 9), [[0, 1]], 0, 1)
     iota(ch("X", 0), [[1, 512]], 32, 0)
-    iota(("J16", 0, 16), [[1, 16]], 0, 0)
-    iota(("JP", 48, 192), [[1, 144]], -16, 0)
-    iota(("GJ", 0, 128), [[1, 8], [0, 16]], 0, 0)
-    iota(("DJ", 0, 128), [[1, 128]], 0, -1)
+    iota(("JP", 0, 192), [[1, 192]], -64, 0)
     iota(("VP", 0, 128), [[16, 128]], int(CUT), 0)
     exchange(0, "L", 1.3)
     ops[-3]["dur"] = ops[-3]["issue"] = 5.5
     exchange(1, "H", 5.4)
-    exchange(2, "P", 5.4)
-    exchange(3, "E", 5.4)
-    exchange(4, "Z", 1.0)
-    iota(("JP", 0, 48), [[1, 48]], -64, 0)
-    iota(("YS", 0, 192), [[64, 3], [0, 4], [1, 16]], -64, 0)
-    iota(("YS", 192, 256), [[0, 4], [1, 16]], 0, 0)
+    turn, nil = [[0, 2], [1, 128]], ("DG", 0, 256)
+    iota(nil, [[0, 256]], 0, 0)
+    select(("II", 0, 256), nil, turn, A.not_equal, 1.0, 0)
+    select(("ROW", 0, 8), ("DG", 0, 8), [[16, 8]], A.not_equal, 1.0, 0)
+    select(("IF", 0, 128), ("DG", 0, 128), [[1, 128]], A.not_equal, 1.0, 0)
+    select(NID, ("DG", 0, 128), [[1, 128]], A.not_equal, -1.0, 0)
     iota(("YG", 0, 160), [[32, 5], [0, 2], [1, 16]], -32, 0)
     iota(("YG", 160, 224), [[32, 2], [0, 2], [1, 16]], 0, 0)
-    iota(("YD", 0, 128), [[64, 2], [0, 2], [1, 32]], 0, 0)
     iota(("SGN", 0, 224), [[0, 7], [-4, 2], [0, 16]], 2, 0)
+    exchange(2, "P", 5.4)
+    iota(("YS", 0, 192), [[64, 3], [0, 4], [1, 16]], -64, 0)
+    iota(("YS", 192, 256), [[0, 4], [1, 16]], 0, 0)
+    select(("N2M", 0, 256), nil, turn, A.not_equal, -2.0, 0)
+    select(N32, ("DG", 0, 128), [[1, 128]], A.not_equal, -32.0, 0)
+    select(P32, ("DG", 0, 128), [[1, 128]], A.not_equal, 32.0, 0)
+    select(("LIFT", 0, 64), ("DG", 0, 64), [[1, 64]], A.is_ge, 8 * BIG, -BOTH // 16, 0)
+    exchange(3, "E", 5.4, [("lnH", 0, 4)])
+    exchange(4, "Z", 1.0)
+    for k in range(4):
+        iota(ch("UNW", k), [[0, 512]], 4, 0)
+        select(ch("UNW", k), ch("UNW", k), [[1, 4], [16, 8], [0, 16]], A.is_equal, 0.0, 4 * k)
+    for name, on in (("M1", -1), ("M2", 1)):
+        iota((name, 0, 256), [[0, 8], [on, 2], [0, 16]], (1 - on) // 2, 0)
+        select((name, 0, 256), (name, 0, 256), turn, A.is_equal, 0.0, -16 * on)
+    select(("M1", 0, 256), ("M1", 0, 256), turn, A.not_equal, 2.0, 0)
+    for b in range(2):
+        iota(("YD", 0, 128), [[0, 64], [4 * b - 2, 2]], 2 - 2 * b, 0)
+        for n in range(2):
+            select(ch("DG", 2 * n + b, 128), ("YD", 0, 128), [[64, 2], [0, 2], [1, 32]], A.is_equal, 0.0, 32 * n)
     line = [k for k in range(first_g, len(ops)) if ops[k]["eng"] == "G"]
     for a, b in zip(line, line[1:]):
         ops[b]["after"] = a
-    dma("Y", [(T.T3A[:], T.lnP[:])], [("lnP", 0, 4)], [("T3A", 0, V)], 3.2)
-    dma("G", [(T.W0[:, V:2 * V], T.T3A[:])], [("T3A", 0, V)], [("W0", V, 2 * V)], 5.0)
-    ops[-1]["after"] = line[-1]
+    dma("Y", [(T.AB[:, V:2 * V], T.lnP[:])], [("lnP", 0, 4)], [("AB", V, 2 * V)], 3.2)
     dma("Y", [(T.LI[:, 0:128], T.lnL[:, 0:64, :]), (T.LI[:, 128:256], T.lnL[:, 64:128, :])], [("lnL", 0, 4)], [("LI", 0, 256)], 2.2)
-    dma("Y", [(T.HW[32:128, V:2 * V], T.lnH[0:3]), (T.HW[0:32, V:2 * V], T.lnH[3])], [("lnH", 0, 4)], [("HW", V, 2 * V)], 3.6)
-    dma("Y", [(T.H[:], T.lnH[:])], [("lnH", 0, 4)], [("H", 0, V)], 3.8)
-    dma("Y", [(T.E[:], T.lnE[:])], [("lnE", 0, 4)], [("E", 0, V)], 2.8)
+    window = dma("Y", [(T.HW[32:128, V:2 * V], T.lnH[0:3]), (T.HW[0:32, V:2 * V], T.lnH[3])], [("lnH", 0, 4)], [("HW", V, 2 * V)], 3.6)
+    ops[dma("Y", [(T.H[:], T.lnH[:])], [("lnH", 0, 4)], [("H", 0, V)], 3.6)]["after"] = window
+    ops[-2]["more"] = window + 1
+    tolls = dma("Y", [(T.E[:], T.lnE[:])], [("lnE", 0, 4)], [("E", 0, V)], 2.8) + 1
     dma("Y", [(T.ZI[32:128], T.lnZ[0:3]), (T.ZI[0:32], T.lnZ[3])], [("lnZ", 0, 4)], [("ZI", 0, 128)], 2.2)
 
     begin = len(ops)
-    BITS = {"group": (4, A.arith_shift_right), "row": (15, A.bitwise_and), "net": (4, A.arith_shift_right, 1, A.bitwise_and),
+    BITS = {"row": (15, A.bitwise_and), "net": (4, A.arith_shift_right, 1, A.bitwise_and),
             "odd": (5, A.arith_shift_right, 1, A.bitwise_and), "slot": (1, A.bitwise_and)}
-    BITS.update({"and%d" % m: (m, A.bitwise_and) for m in (112, 14, 64, 78, 95)})
+    BITS.update({"and%d" % m: (m, A.bitwise_and) for m in (112, 14, 64, 78)})
 
     def bits(names):
         for nm in names:
             k = COLS.index(nm)
-            v_ts(("PI", k, k + 1), ("PI", 0, 1), *BITS[nm])
+            v_ts(("PI", k, k + 1), ("PI", 8, 9), *BITS[nm])
         lo, hi = COLS.index(names[0]), COLS.index(names[-1]) + 1
         v_cp(("PF", lo, hi), ("PI", lo, hi))
 
-    bits(COLS[1:6])
-    v_ts(("MK", 0, 16), ("J16", 0, 16), pf("row"), A.is_equal)
-    v_ts(("MK4", 0, 16), ("MK", 0, 16), 4.0, A.mult)
-    v_ts(("BLK", 0, 128), ("GJ", 0, 128), pf("group"), A.is_equal)
+    bits(COLS[0:8])
+    v_ts(whole("sel"), ("JP", 48, 192), pf("and112"), A.is_equal, BIG, A.mult)
     for k in (1, 2, 3):
         s_act(ch("X", k), ch("X", 0), F.Identity, bias=512.0 * k)
 
-    def matrices():
-        v_ts(("SELF", 0, 144), ("JP", 48, 192), pf("and112"), A.is_equal, 1.0 / 16, A.mult)
-        v_ts(pf("mid"), pf("and14"), -1.0, A.mult, -159.5 / 128, A.add)
-        v_ts(whole("sel"), ("JP", 48, 192), pf("and112"), A.is_equal, BIG, A.mult)
-        v_ts(("II", 0, 128), ("DJ", 0, 128), 0.0, A.is_equal)
-        v_ts(("II", 128, 256), ("DJ", 0, 128), 0.0, A.is_equal)
-        v_ts(("NID", 0, 128), ID, -1.0, A.mult)
-        v_ts(("VP", 0, 128), ("VP", 0, 128), pf("row"), A.add)
-        v_ts(("N2M", 0, 256), ("II", 0, 256), -2.0, A.mult)
-
-    def more_matrices():
-        v_ts(pf("net0"), pf("net"), -1.0, A.mult, 1.0, A.add)
-        v_ts(("M1", 0, 128), ("DJ", 0, 128), -16.0, A.is_equal, pf("net"), A.mult)
-        v_ts(("M2", 0, 128), ("DJ", 0, 128), 16.0, A.is_equal, pf("net0"), A.mult)
-        v_tt(("M1", 0, 128), ("M1", 0, 128), N2, A.subtract)
-        v_cp(("M2", 128, 256), ("M2", 0, 128))
-        v_ts(("N32M", 0, 128), ID, -1.0 / 32, A.mult)
-        v_cp(("M1", 128, 256), ("M1", 0, 128))
+    def lin(o, a, times, plus=0.0):
+        cp("*", pf(o), pf(a), None, pf(times) if isinstance(times, str) else times, pf(plus) if isinstance(plus, str) else plus)
 
     def walk_matrices():
         jp = ("JP", 48, 192)
-        bits(COLS[6:11])
-        v_ts(pf("slot0"), pf("slot"), -1.0, A.mult, 1.0, A.add)
-        v_ts(pf("even"), pf("odd"), -1.0, A.mult, 1.0, A.add)
-        v_ts(pf("flip"), pf("and64"), -2.0, A.mult, 64.0, A.add)
-        v_ts(pf("at"), pf("net"), 32.0, A.mult, pf("odd"), A.add)
-        v_ts(pf("at0"), pf("and64"), pf("at"), A.add)
-        v_ts(pf("at1"), pf("flip"), pf("odd"), A.mult, pf("at0"), A.add)
-        v_ts(pf("to"), pf("odd"), 8.0, A.mult, pf("and64"), A.add)
-        v_ts(pf("on"), pf("slot"), pf("to"), A.add)
-        v_ts(pf("at"), pf("flip"), pf("slot0"), A.mult, pf("and78"), A.add)
-        v_ts(pf("at"), pf("slot"), 32.0, A.mult, pf("at"), A.add)
-        v_ts(pf("home"), pf("odd"), 16.0, A.mult, pf("at"), A.add)
-        v_ts(pf("cut"), pf("net"), -34.0, A.mult, 17.0, A.add)
+        lin("slot0", "slot", -1.0, 1.0)
+        lin("even", "odd", -1.0, 1.0)
+        lin("flip", "and64", -2.0, 64.0)
+        lin("at", "net", 32.0, "odd")
+        lin("at0", "and64", 1.0, "at")
+        lin("at1", "flip", "odd", "at0")
+        lin("to", "odd", 8.0, "and64")
+        lin("on", "slot", 1.0, "to")
+        lin("home", "flip", "slot0", "and78")
+        lin("home", "slot", 32.0, "home")
+        lin("home", "odd", 16.0, "home")
+        lin("cut", "net", -34.0, 17.0)
+        v_ts(pf("cut2"), pf("and14"), BOTH / 128 - 1, A.is_gt, 15.0 / 17, A.mult)
+        v_ts(pf("cut2"), pf("cut2"), 2.0 / 17, A.add, pf("cut"), A.mult)
         v_ts(pf("nine"), pf("and14"), TUNE["fused"][3][0] / 128 - 1, A.is_gt, -16.0, A.mult)
-        v_ts(pf("at"), pf("and14"), TUNE["fused"][3][1] / 128 - 1, A.is_lt)
-        v_ts(pf("nine"), pf("nine"), pf("at"), A.mult, -1.0, A.add)
+        v_ts(pf("at"), pf("and14"), TUNE["fused"][3][1] / 128 - 1, A.is_lt, pf("nine"), A.mult)
+        lin("nine", "at", 1.0, -1.0)
         v_ts(whole("vote1"), ("YG", 16, 224), pf("at1"), A.is_equal, -1.0, A.mult)
         v_ts(whole("vote0"), ("YG", 80, 224), pf("at0"), A.is_equal, -1.0, A.mult)
-        v_cp(whole("over"), part("MAT", 64, 208, MATS["vote1"][0]))
-        v_ts(whole("over2"), whole("over"), -2.0, A.mult)
+        cp("*", whole("over"), part("MAT", 64, 208, MATS["vote1"][0]))
+        cp("*", whole("over2"), whole("over"), None, -2.0)
         v_tt(whole("vote1"), whole("vote1"), ("SGN", 16, 224), A.mult)
         v_tt(whole("vote0"), whole("vote0"), ("SGN", 16, 160), A.mult)
         v_ts(whole("on"), ("YS", 48, 256), pf("on"), A.is_equal)
         v_ts(whole("out"), ("JP", 32, 192), pf("to"), A.is_equal, pf("slot0"), A.mult)
         v_ts(whole("sum"), ("JP", 0, 192), pf("and78"), A.is_equal, pf("even"), A.mult)
-        v_ts(whole("sum1"), whole("sum"), pf("slot"), A.mult)
-        v_ts(pf("end"), pf("net"), -7.5, A.mult, 1.5, A.add)
-        v_ts(pf("end"), pf("end"), pf("slot"), A.mult, -2.0, A.add)
-        v_ts(pf("none"), pf("odd"), 2.0, A.mult, 2.0, A.add)
-        v_ts(pf("none0"), pf("none"), pf("net0"), A.mult)
-        v_ts(pf("none1"), pf("none"), pf("net"), A.mult)
+        cp("*", whole("sum1"), whole("sum"), None, pf("slot"))
+        lin("end", "net", -7.5, 1.5)
+        lin("end", "end", "slot", -2.0)
+        lin("none", "odd", 2.0, 2.0)
+        lin("none1", "none", "net")
+        lin("none0", "none1", -1.0, "none")
         v_ts(whole("winA"), jp, pf("home"), A.is_equal, pf("net"), A.mult)
-        v_ts(whole("winB"), whole("winA"), 0.5, A.mult)
-        v_ts(("YD", 0, 128), ("YD", 0, 128), pf("and95"), A.is_equal, 2.0, A.mult)
-        for n in range(2):
-            for b in range(2):
-                v_ts(ch("DG", 2 * n + b, 128), ("YD", 0, 128), pf("odd" if n else "even"), A.mult, pf("slot" if b else "slot0"), A.mult)
+        cp("*", whole("winB"), whole("winA"), None, 0.5)
 
-    def votes(o, name, lo, hi):
-        pe(group(o, [(mat("sel", i), (name, lo + i, hi, 16)) for i in range(16)]))
+    def votes(o, name, lo, hi, first=True):
+        pe(group(o, [(mat("sel", i), (name, lo + i, hi, 16)) for i in range(16)], first), acc=not first)
 
     def compact(name, lo, hi, o, by, turn=0, n=256, first=True, last=True, base=0):
         pairs = [(mat(by, i * n // 128, turn), (name, base + n * i, base + n * i + n)) for i in range(lo // n, hi // n)]
@@ -393,71 +408,81 @@ def build(g, core, T, topo):
     v_cp(("INV", 0, 256), ("TI", 0, 256))
     add("V", lambda: [g.vector.tensor_copy(T.W1[:, 0:V].indirect(T.INV[:, 0:128]), T.X[:])],
         [("X", 0, V), ("INV", 0, 128)], [("W1", 0, V)], 2.4 * GA * V * CY)
-    silu = add("S", lambda: [g.scalar.activation(T.W1[:, V:2 * V].indirect(T.INV[:, 128:256]), T.X[:], F.Silu)],
-               [("X", 0, V), ("INV", 128, 256)], [("W1", V, 2 * V)], 1.3 + 2.4 * GA * V * CY)
-    matrices()
-    for i in range(16):
-        either(lambda: v_ts(unw(i), ("BLK", 0, 128), ("MK4", i, i + 1), A.mult),
-               lambda: s_act(unw(i), ("BLK", 0, 128), F.Identity, scale=("MK4", i, i + 1)))
+    add("S", lambda: [g.scalar.activation(T.W1[:, V:2 * V].indirect(T.INV[:, 128:256]), T.X[:], F.Silu)],
+        [("X", 0, V), ("INV", 128, 256)], [("W1", V, 2 * V)], 1.3 + 2.4 * GA * V * CY)
+    for o in ops[-2:]:
+        o["cls"], o["bias"] = "s", 50.0
+    ops[-2]["more"] = lowered
+    lin("mid", "and14", -1.0, -159.5 / 128)
     for s in range(2):
-        pe(group(ch("Q", s, 128), [(("SELF", 16 - i, 144 - i), ("W1", V * s + i, V * s + V, 16)) for i in range(16)]))
-    more_matrices()
+        for j in range(0, 16, 4):
+            pe([(("R", 512 * s + i, 512 * s + 128, 16), ("W1", V * s + i, V * s + V, 16), ("ROW", 0, 8), True, True)
+                for i in range(j, j + 4)], acc=j > 0)
+    v_ts(("VP", 0, 128), ("VP", 0, 128), pf("row"), A.add)
     v_cp(("AB16", 0, 256), ("LI", 0, 256))
-    v_ts(("TI", 0, 256), ("Q", 0, 256), -32.0, A.add)
-    v_ts(("TJ", 0, 256), ("TI", 0, 256), 255, A.bitwise_and)
-    v_cp(("IV", 0, 256), ("TJ", 0, 256))
 
     for k in (3, 2, 1, 0):
-        cp("S" if k else "*", ch("HW", k), ("HW", V, 2 * V), lst=lst("AB16", 0, 512 * k, 512 * k + 512))
+        cp("S" if k > 1 else "V", ch("HW", k), ("HW", V, 2 * V), lst("AB16", 0, 512 * k, 512 * k + 512))
+    for k in (3, 2, 1, 0):
         v_tt(ch("YB", k), ("HW", V, 2 * V), ch("H", k), A.subtract, lst=lst("AB16", 128, 512 * k, 512 * k + 512))
-    in_line(begin)
-    v_ts(("AP", 0, 128), ("LI", 0, 128), CUT, A.add)
-    v_ts(("BP", 0, 128), ("LI", 128, 256), CUT + V, A.add)
-    v_ts(("ZC", 0, 128), ("ZI", 0, 128), 0.5, A.mult, 0.25, A.add)
     for k in (3, 2, 1, 0):
         pe(summed(ch("P", k), k, [(ID, "HW"), (NID, "H")]))
         s_act(ch("DA", k), ch("P", k), F.Abs)
-        if k in TUNE["v_db"]:
-            v_ts(ch("YA", k), ch("YB", k), -2.0, A.mult, 0.0, A.max)
-            pe(summed(ch("R", k % 2), k, [(ID, "YA"), (ID, "YB")]))
-            cp("*", ch("DB", k), ch("R", k % 2))
-        else:
-            s_act(ch("DB", k), ch("YB", k), F.Abs)
+        s_act(ch("DB", k), ch("YB", k), F.Abs)
         pe(summed(ch("P", k), k, [(ID, "DA"), (NID, "DB")]))
-        cp("*", ch("DL", k), ch("P", k))
+        if k > 1:
+            cp("V", ch("DL", k), ch("P", k))
+    in_line(begin)
+    for s in range(2):
+        cp("*", ch("LT", s, 128), part("R", 0, 128, 512 * s), plus=-32.0)
+    for s in range(2):
+        pe([(ch("R", s, 128), ch("LT", s, 128), ("IF", 0, 128), True, True)])
+    bias[0], children = 30.0, len(ops)
+    v_cp(("TI", 0, 256), ("R", 0, 256))
+    v_ts(("TJ", 0, 256), ("TI", 0, 256), 255, A.bitwise_and)
+    v_cp(("IV", 0, 256), ("TJ", 0, 256))
+    bias[0] = 0.0
+    v_ts(("AP", 0, 128), ("LI", 0, 128), CUT, A.add)
+    v_ts(("BP", 0, 128), ("LI", 128, 256), CUT + V, A.add)
+    v_ts(("ZC", 0, 128), ("ZI", 0, 128), 0.5, A.mult, 0.25, A.add)
 
-    def turned(eng, o, a, t, dur, **kw):
+    def turned(eng, o, a, t, dur, behind=(), **kw):
         cutp = 128 - 32 * t
         dma(eng, [(T[o[0]][0:cutp, o[1]:o[2]], T[a[0]][32 * t:128, a[1]:a[2]]), (T[o[0]][cutp:128, o[1]:o[2]], T[a[0]][0:32 * t, a[1]:a[2]])],
-            [a], [o], dur, **kw)
+            [a, *behind], [o], dur, **kw)
 
     OWN = min(TUNE["help"][1:])
-    edges = {0: ("DL", OWN), 1: ("H", 0), 2: ("HW", 0), 3: ("DA", 0)}
-    turned("Y", ("HX", 0, V), ("HW", 0, V), 1, 4.0)
-    dma("Y", [(T.HX[:, V:2 * V], T.lnH[:])], [("lnH", 0, 4), ("H", 0, V)], [("HX", V, 2 * V)], 3.6)
+    edges = {0: ("DL", OWN), 1: ("H", 0), 2: ("H", V // 2), 3: ("DC", 0)}
     for t in (1, 2, 3):
-        turned("Y", ch("AB16", t, 256), ch("AB16", 0, 256), t, 2.3)
-        turned("Y", ch("BP", t, 128), ch("BP", 0, 128), t, 2.3)
-        if t > 1:
-            turned("Y", ch("AP", t, 128), ch("AP", 0, 128), t, 2.3)
-        if t < 3:
-            turned("Y", part(edges[t][0], 0, V - OWN, edges[t][1]), ("DL", OWN, V), t, 2.4 + 1.6 * (V - OWN) / V)
-    dma("Y", [(T.HW[0:64, V:2 * V], T.lnH[2:4]), (T.HW[64:128, V:2 * V], T.lnH[0:2])], [("lnH", 0, 4)], [("HW", V, 2 * V)], 3.6)
-    dma("G", [(T.dH[0:96], T.lnH[1:4]), (T.dH[96:128], T.lnH[0])], [("lnH", 0, 4), ("W0", V, 2 * V)], [("dH", 0, 1)], 4.0)
-    turned("Y", ("T2A", 0, V), ("DA", 0, V), 3, 4.0)
-    turned("Y", ("T2B", 0, V), ("DB", 0, V), 3, 4.0)
+        for name, n in (("AB16", 256), ("BP", 128), ("AP", 128))[:2 + (t > 1)]:
+            turned("Y", ch(name, t, n), ch(name, 0, n), t, 2.3)
+            ops[-3]["after"] = window + 4
+        turned("Y", part(edges[t][0], 0, V - OWN, edges[t][1]), ("DL", OWN, V), t, 2.4 + 1.6 * (V - OWN) / V)
+    later = [("lnH", 0, 4), ("E", 0, V)]
+    bias[0] = TUNE["early"]
+    dma("G", [(T.dH[0:96], T.lnH[1:4]), (T.dH[96:128], T.lnH[0])], later, [("dH", 0, V)], 5.0)
+    ops[-3]["after"] = line[-1]
+    dma("Y", [(T.HX[:, V:2 * V], T.lnH[:])], later, [("HX", V, 2 * V)], 3.6)
+    turned("Y", ("HX", 0, V), ("HW", 0, V), 1, 4.0, later)
+    bias[0] = 0.0
+    later += [("HX", 0, 2 * V)]
+    dma("Y", [(T.HW[0:64, V:2 * V], T.lnH[2:4]), (T.HW[64:128, V:2 * V], T.lnH[0:2])], later, [("HW", V, 2 * V)], 3.6)
+    turned("Y", ("T2A", 0, V), ("DA", 0, V), 3, 4.0, later)
+    turned("Y", ("T2B", 0, V), ("DB", 0, V), 3, 4.0, later)
 
     walk_matrices()
     for k in range(8):
         s_act(ch("THR", k), ch("W1", k), F.Abs, bias=pf("mid"), scale=1.0 / 128)
     halves = [(s, h, slice(64 * h + 32 * s, 64 * h + 32 * s + 32)) for s in range(2) for h in range(2)]
     dma("Y", [(T.stI[:, at, :], ap(ch("IV", 2 * s + h, 64))) for s, h, at in halves], [("IV", 0, 256)], [("stI", 0, 8)], 2.4)
+    ops[-3]["after"] = tolls
     dma("Y", [(T.stT[:, at, :], T.THR[0::2, 1024 * (2 * s + h):1024 * (2 * s + h + 1)]) for s, h, at in halves], [("THR", 0, 2 * V)],
         [("stT", 0, 8)], 3.2)
+    ops[-3]["after"] = tolls
     for k, nm, dur in ((13, "I", 0.8), (15, "T", 2.8)):
         st, ln = "st" + nm, "ln" + nm
         for n in range(2):
-            send(k + n, [(r, T[st][2 * r + n], T[ln][2 * q + n]) for r in others], [(st, 0, 8)],
+            send(k + n, [(r, T[st][2 * r + n], T[ln][2 * q + n]) for r in others], [(st, 0, 8), ("ZI", 0, 128)],
                  [(ln, 2 * r + n, 2 * r + n + 1) for r in others], dur)
             ops[-3]["after"] = line[-1]
         dma("Y", [(T[ln][2 * q:2 * q + 2], T[st][2 * q:2 * q + 2])], [(st, 0, 8)], [(ln, 2 * q, 2 * q + 2)], 2.4)
@@ -465,26 +490,31 @@ def build(g, core, T, topo):
     for x in range(4):
         dma("Y", [(T.THR[b::2, 1024 * x:1024 * x + 1024], T.lnT[x::4]) for b in range(2)], [("lnT", 0, 8)], [ch("THR", x, 1024)], 3.0)
 
-    cur, steps, listed, terms = [0], [0], [0], [0]
+    cur, steps, listed, terms = [0], [0], [0, 0], [0]
     free = [ch("R", 0), ch("R", 1)]
 
-    def bank():
+    def bank(n=512):
         terms[0] += 1
-        return free[terms[0] % len(free)]
+        step = n // 512
+        return free[terms[0] % (len(free) // step) * step]
 
     def make_list(CM, n, t, lo, hi, o, winners):
         o, y = (o[0], o[1], o[1] + (hi - lo) // 16), lst("LX", 128 * (n % 3), lo, hi)
-        votes(o, CM, lo, hi)
+        signed = lo == 0 and n in TUNE["both"]
+        if signed:
+            pe([(o, ID, ("LIFT", 0, width(o)), True, False)])
+        votes(o, CM, lo, hi, not signed)
         v_tt(y, o, lst("BP", 128 * t, lo, hi), A.min)
         if winners:
             v_tt(lst("LY", 0, lo, hi), y, lst("VP", 0, lo, hi), A.max)
-            v_ts(lst("LS", 128 * n, lo, hi), lst("LY", 0, lo, hi), -CUT - lo, A.add)
+            v_ts(lst("LS", 128 * (n % 3), lo, hi), lst("LY", 0, lo, hi), -CUT - lo, A.add)
 
     def predecessors(n, t):
-        v_tt(("LZ", 0, 128), ch("LX", n % 3, 128), ch("AP", t, 128), A.max)
-        v_ts(("LZ", 128, 256), ("LZ", 0, 128), V - 1, A.bitwise_and)
-        v_cp(ch("LP", n, 128), ("LZ", 128, 256))
-        listed[0] = len(ops) - 1
+        z = ch("LZ", t - 2, 128)
+        v_tt(z, ch("LX", n % 3, 128), ch("AP", t, 128), A.max)
+        v_ts(z, z, V - 1, A.bitwise_and)
+        v_cp(ch("LP", 2 * ((n - 1) // 3 % 2) + t - 2, 128), z)
+        listed[t - 2] = len(ops) - 1
 
     def open_window(names):
         for k in (3, 2, 1, 0):
@@ -501,18 +531,21 @@ def build(g, core, T, topo):
         return ch("SG", (n - 1) % 3 if n % 3 else 1 + n // 3, 256)
 
     def step(n, t, first, marks, PN):
-        W, CM = "W%d" % cur[0], "CM%d" % (steps[0] % 2)
+        W, CM = "W%d" % cur[0] if t else "AB", "CM%d" % (steps[0] % 2)
         steps[0] += 1
         fixed = ["E", "DB"] if n in TUNE["apart"] else ["ED"]
-        costs = (W, V, 2 * V) if t else ("T3A", 0, V)
+        costs = (W, V, 2 * V)
         helped = TUNE["help"][n]
-        begin = len(ops)
+        begin, both = len(ops), BOTH * (n in TUNE["both"])
         for j, (a, b) in enumerate(cut(0, helped, TUNE["aid"])):
-            o = ch("P", TUNE["banks"][j % len(TUNE["banks"])])
+            if b <= both and t == 3 and not first:
+                cp("S", part("TM", a, b), costs, lst("AB16", 256 * t, a, b))
+                continue
+            o = ch("P", TUNE["banks"][j % len(TUNE["banks"])] + 2 * (t == 0))
             o = (o[0], o[1], o[1] + b - a)
             fix = [(rot(t), "DL")] if t else [(ID, "DA"), (NID, "DB")]
             pe(group(o, [(l, part(r, a, b)) for l, r in fix], True, False))
-            cp("S", part("TM", a, b), costs, lst=lst("AB16", 256 * t, a, b))
+            cp("S", part("TM", a, b), costs, lst("AB16", 256 * t, a, b))
             pe(group(o, [(ID, part("TM", a, b))], False, True), acc=True)
             cp("S", part(W, a, b), o)
         f0, f1 = TUNE["fused"][n]
@@ -535,10 +568,7 @@ def build(g, core, T, topo):
                     o, to = ch("P", 3 - j % 2), part(beside[0], a, b, beside[1])
                     o = (o[0], o[1], o[1] + b - a)
                     fixed_part(o, a, b, True)
-                    if t == 3:
-                        either(lambda: v_ts(to, o, 0.5, A.mult), lambda: s_act(to, o, F.Identity, scale=0.5))
-                    else:
-                        cp("*", to, o)
+                    cp("*", to, o, None, 0.5 if t == 3 else 1.0)
             for a, b in picked:
                 fixed_part(part("P", a, b), a, b, False)
         if t == 3 and first:
@@ -552,7 +582,7 @@ def build(g, core, T, topo):
 
         def fused(lo, hi):
             for a, b in cut(max(lo, f0), max(lo, min(hi, f1)), TUNE["cmp"]):
-                l = lst("LS", 128 * n, a, b)
+                l = lst("LS", 128 * (n % 3), a, b)
                 if t < 3:
                     v_tt(part(NEXT, a, b, V), (W, lo, 2 * V), part(beside[0], a, b, beside[1]), A.add, lst=l)
                 else:
@@ -563,12 +593,12 @@ def build(g, core, T, topo):
             make_list(CM, n, t, lo, hi, ("Q", 512 * (j % 2 if t < 3 else 0)), True)
             if not t:
                 for c, d in cut(lo, hi, TUNE["last"] if lo == 0 else 512):
-                    cp("*", part(PN, c, d), (W, lo, 2 * V), lst=lst("LS", 128 * n, c, d))
+                    cp("*", part(PN, c, d), (W, lo, 2 * V), lst("LS", 0, c, d), plus=128.0)
                 return
             for a, b in picked:
                 if lo <= a < hi:
                     o = part("P", a, b)
-                    cp("S", part(PN, a, b), (W, lo, 2 * V), lst=lst("LS", 128 * n, a, b))
+                    cp("S", part(PN, a, b), (W, lo, 2 * V), lst("LS", 128 * (n % 3), a, b))
                     pe(group(o, [(N2 if t == 3 else ID, part(PN, a, b))], False, True), acc=True)
                     if t < 3:
                         cp("*", part(NEXT, a, b, V), o)
@@ -581,12 +611,21 @@ def build(g, core, T, topo):
         late, mine = [], []
         waiting = []
         for j, (lo, hi) in enumerate(TUNE["pieces"]):
-            for a, b in cut(max(lo, helped), max(hi, helped), TUNE["cmp"]):
+            for a, b in cut(max(lo, helped), max(hi, helped), TUNE["head" if t else "cmp"]):
                 v_tt(part(W, a, b), costs, part(edges[t][0], a, b, edges[t][1] - OWN), A.add, lst=lst("AB16", 256 * t, a, b))
                 while waiting:
                     winners(*waiting.pop())
-            for a, b in cut(lo, hi, TUNE["cmp"]):
-                v_tt(part(CM, a, b), costs, part(W, a, b), A.is_lt, lst=lst("AB16", 256 * t + 128, a, b))
+            for a, b in cut(max(lo, both), hi, TUNE["cmp" if j or not t else "head"]) + [(0, both)] * (lo < both):
+                if b > both:
+                    v_tt(part(CM, a, b), costs, part(W, a, b), A.is_lt, lst=lst("AB16", 256 * t + 128, a, b))
+                    if n == 0:
+                        ops[children]["after"] = len(ops) - 1
+                else:
+                    o = part("P", a, b, 512 * TUNE["third"])
+                    pe(group(o, [(rot(t), part("DL", a, b)), (ID, part("TM", a, b))], True, False))
+                    cp("S", part("TM", a, b, helped), costs, lst("AB16", 256 * t + 128, a, b))
+                    pe(group(o, [(NID, part("TM", a, b, helped))], False, True), acc=True)
+                    s_act(part(CM, a, b), o, F.Sign, bias=-0.5)
                 if t == 3 and not first:
                     compact(CM, a, b, QB, *vote, first=b == V, last=a == 0)
                     if a == lo:
@@ -602,17 +641,17 @@ def build(g, core, T, topo):
         while mine:
             fused(*mine.pop(0))
         in_line(begin, "V")
-        sg = gate(n)
+        sg, bar = gate(n), pf("cut2" if both else "cut")
         o = ("Q", 0, 256) if t == 3 and first else QB
         if t in (1, 2) or t == 3 and first:
-            for a, b in cut(0, V, 512):
+            for a, b in cut(0, V, TUNE["gates"]):
                 compact(CM, a, b, o, *vote, first=b == V, last=a == 0)
         if t in (1, 2):
             cur[0] = 1 - cur[0]
-            either(lambda: v_ts(sg, o, pf("cut"), A.add, 1.0, A.min), lambda: s_act(sg, o, F.Sign, bias=pf("cut")))
+            either(lambda: v_ts(sg, o, bar, A.add, 1.0, A.min), lambda: s_act(sg, o, F.Sign, bias=bar))
         if t == 3:
             mw = ("MW", 0, 256)
-            s_act(sg, o, F.Sign, bias=pf("cut"))
+            s_act(sg, o, F.Sign, bias=bar)
             if first:
                 either(lambda: v_ts(mw, QB, pf("nine"), A.add, 1.0, A.min), lambda: s_act(mw, QB, F.Sign, bias=pf("nine")))
             else:
@@ -622,7 +661,7 @@ def build(g, core, T, topo):
             predecessors(n, t)
 
     def join_x():
-        dma("Y", [(T.XR[:, 0:V], T.dH[:])], [("dH", 0, 1)], [("XR", 0, V)], 4.0)
+        dma("Y", [(T.XR[:, 0:V], T.dH[:])], [("dH", 0, V)], [("XR", 0, V)], 4.6)
         for a, b in cut(0, V, TUNE["join"]):
             dma("G", [(T.XR[:, a:b], T.YA[:, a:b])], [("YA", a, b)], [("XR", a, b)],
                 3.2 + 4.5 * (b - a) / V, accum_op=A.add, max_dma_last_dim=4096)
@@ -635,32 +674,26 @@ def build(g, core, T, topo):
         slots[0] += n
         return ("EX", slots[0] - n, slots[0])
 
-    def stage(e, p, first=False):
-        pair, wr = [(T["stG%d" % p][:], ap(e))], [("stG%d" % p, 0, 4)]
+    def summed_up(e, lo, first=False):
+        to = ("dG", lo, lo + width(e))
         if first:
-            dma("Y", pair, [e], wr, 3.2)
+            dma("Y", [(ap(to), ap(e))], [e], [to], 2.4 + width(e) / 640)
         else:
-            dma("G", pair, [e], wr, 3.6 + width(e) / 512 * TUNE["acc"], accum_op=A.add, max_dma_last_dim=2048)
+            dma("G", [(ap(to), ap(e))], [e], [to], 3.2 + width(e) / 400, accum_op=A.add, max_dma_last_dim=2048)
 
-    def term(p, pairs, off, half, v_abs, plus):
-        lo, hi = GAIN[p]
-        lnw = math.log(0.5) if half else 0.0
-        e = ("GD", lo, hi) if plus else next_ex(hi - lo)
-        for k in range(lo // 512, hi // 512):
-            o = bank()
-            ab, out = ch("AB", terms[0] % 4), o if plus else ch("EX", k, base=e[1] - lo)
-            pe(summed(o, k, pairs))
-            if v_abs:
-                v_ts(ab, o, -off, A.add, 0.0, A.max)
-                pe(group(o, [(l, ch(r, k)) for l, r in pairs] + [(N2, ab)]))
-                s_act(out, o, F.Exp, bias=lnw - off / 8, scale=0.125)
-            else:
-                s_act(ab, o, F.Abs, bias=-off)
-                s_act(out, ab, F.Exp, bias=lnw, scale=-0.125)
-            if plus:
-                v_tt(ch("GD", k), o, ch("GD", k), A.add)
-        if plus != 1:
-            stage(e, p, plus == 2 and TUNE["back"])
+    def term(lo, hi, pairs, off, half, last):
+        n = 512 if hi - lo <= 512 else 1024
+        o = bank(n)
+        o, ab = part(o[0], 0, hi - lo, o[1]), part("AB", 0, hi - lo, n * (terms[0] % (V // n)))
+        out = o if last else next_ex(hi - lo)
+        for a, b in cut(lo, hi, 512):
+            pe(group(part(o[0], a, b, o[1] - lo), [(l, part(r, a, b)) for l, r in pairs]))
+        s_act(ab, o, F.Abs, bias=-off)
+        s_act(out, ab, F.Exp, bias=math.log(0.5) if half else 0.0, scale=-0.125)
+        if last:
+            v_tt(("GD", lo, hi), o, ("GD", lo, hi), A.add)
+        else:
+            summed_up(out, lo)
 
     walked = [None] * 3
 
@@ -693,8 +726,9 @@ def build(g, core, T, topo):
                                  for y in (1, 2, 3) for e in range(2)], apart or n == 0, False), acc=not (apart or n == 0))
                 for a, b in TUNE["walk"]:
                     v_tt(part(found[x], a, b, H * n), cc(n, x), part("THR", a, b, H * tile), A.is_gt, lst=lst("INV", 64 * tile, a, b))
-                    if (x, n, b) == TUNE["lists"][f]:
-                        ops[-1]["after"] = listed[0]
+                    for j in range(2):
+                        if (x, n, b) == TUNE["lists"][f][j]:
+                            ops[-1]["after"] = listed[j]
                     if x < 3:
                         compact(found[x], a, b, ("Q", 512 * n, 512 * n + 256), "on", 64 * (1 - x % 2), first=False, last=a == 0, base=H * n)
                     else:
@@ -716,51 +750,40 @@ def build(g, core, T, topo):
         step(3 * f + 1, 1, first, marks, "PN")
         for lo, hi in TUNE["pieces"]:
             for a, b in cut(lo, hi, wide):
-                l = lst("LS", 128 * (3 * f + 1), a, b)
-                either(lambda: v_ts(part("YA", a, b), ("HX", lo, 2 * V), 32.0, A.mult, lst=l),
-                       lambda: s_act(part("YA", a, b), ("HX", lo, 2 * V), F.Identity, scale=32.0, lst=l))
+                cp("*", part("YA", a, b), ("HX", lo, 2 * V), lst("LS", 128, a, b), 1.0 / 32)
         join_x()
         step(3 * f + 2, 2, first, marks, "PN")
         for a, b in cut(0, V, wide):
-            cp("*", part("X", a, b), ("XR", 0, V), lst=lst("LP", 128 * (3 * f + 2), a, b))
+            cp("*", part("X", a, b), ("XR", 0, V), lst("LP", 256 * (f % 2), a, b))
         step(3 * f + 3, 3, first, marks, "PN")
         walk_back(f)
         for a, b in cut(0, V, wide)[::-1]:
-            l = lst("LP", 128 * (3 * f + 3), a, b)
+            l = lst("LP", 128 * (2 * (f % 2) + 1), a, b)
             cp("*", part("T3" + P, a, b), ("HW", V, 2 * V), lst=l)
             cp("*", part("T1" + P, a, b), ("X", 0, V), lst=l)
-            if f in TUNE["t2"]:
-                v_ts(part("T2" + P, a, b), part("T1" + P, a, b), HI - 15.5, A.add)
-            else:
-                either(lambda: v_ts(part("T2" + P, a, b), part("T1" + P, a, b), HI - 15.5, A.add),
-                       lambda: s_act(part("T2" + P, a, b), part("T1" + P, a, b), F.Identity, bias=HI - 15.5))
+            cp("V" if f in TUNE["t2"] else "*", part("T2" + P, a, b), part("T1" + P, a, b), plus=HI - 15.5 / 32)
         if last:
             free.extend(ch("P", k) for k in range(4))
             o, win = bank(), ("WIN", 0, 128)
             o = (o[0], o[1], o[1] + 128)
             pe(group(o, [(mat("win" + "AB"[x % 2], e), part("SG", 128 * e, 128 * e + 128, gate(3 * x + 3)[1]))
                          for x in range(4) for e in range(2)]))
-            either(lambda: v_ts(win, o, 0.125, A.mult, 0.375, A.add), lambda: s_act(win, o, F.Identity, bias=0.375, scale=0.125))
+            cp("*", win, o, None, 0.125, 0.375)
             for k in range(4):
                 o = bank()
-                pe(summed(o, k, [], ch("WIN", 0, 128)))
+                pe(summed(o, k, [], win))
                 v_tt(ch("GD", k), o, ch("GD", k), A.mult)
-                if TUNE["back"]:
-                    dma("G", [(ap(ch("GD", k)), T["stG%d" % k][:])], [("stG%d" % k, 0, 4)], [ch("GD", k)], 4.6,
-                        accum_op=A.add, max_dma_last_dim=2048)
+                dma("G", [(ap(ch("GD", k)), ap(ch("dG", k)))], [ch("dG", k)], [ch("GD", k)], 4.6, accum_op=A.add, max_dma_last_dim=2048)
         if first:
             return
-        todo = [([(ID, "T1B"), (NID, "T2B"), (NID, "T3A")], -HI, True),
-                ([(ID, "T1A"), (NID, "T2A"), (NID, "T3B")], -HI, False),
-                ([(ID, "T1B"), (NID, "T2B"), (("N32M", 0, 128), "T2A")], -HI - HI / 32, False),
-                ([(ID, "T1A"), (NID, "T2A"), (("N32M", 0, 128), "T2B")], -HI - HI / 32, True)]
+        todo = [([(ID, "T3B"), (NID, "T2A")], -HI, False),
+                ([(ID, "T3A"), (NID, "T2B")], -HI, True),
+                ([(P32, "T1B"), (N32, "T2B"), (NID, "T2A")], -33 * HI, True),
+                ([(P32, "T1A"), (N32, "T2A"), (NID, "T2B")], -33 * HI, False)]
         skew = TUNE["skew"] if last else 0.1
-        for m, (_, j, p) in enumerate(sorted((j + skew * p, j, p) for j in range(4) for p in range(len(GAIN)))):
-            begin = len(ops)
-            term(p, todo[j][0], todo[j][1], todo[j][2], j in TUNE["v_abs"][f],
-                 0 if not last or j < 4 - TUNE["with"] else 1 + (j == 3))
-            if last and m in TUNE["pace"]:
-                ops[begin + 1]["after"] = walked[TUNE["pace"].index(m)]
+        pieces = TUNE["terms"] if last else cut(0, V, TUNE["broad"])[::-1]
+        for _, j, p in sorted((j + skew * p, j, p) for j in range(len(todo)) for p in range(len(pieces))):
+            term(*pieces[p], *todo[j], last)
 
     def new_tolls(o, k, small, old, new):
         pe(group(o, [(ID, ch(old, k))], True, False))
@@ -772,16 +795,16 @@ def build(g, core, T, topo):
         dma("G", [(T.ED[:], T.E[:])], [("E", 0, V)], [("ED", 0, V)], 5.0, accum_op=A.add, max_dma_last_dim=4096)
 
     step(0, 0, True, None, "PN0")
-    turned("Y", ("DA", 0, V - OWN), ("DL", OWN, V), 3, 2.4 + 1.6 * (V - OWN) / V)
-    for p, (lo, hi) in enumerate(GAIN):
-        e, e2 = next_ex(hi - lo), next_ex(hi - lo)
-        for k in range(lo // 512, hi // 512):
-            ea, less = ch("EX", k, base=e[1] - lo), ch("EX", k, base=e2[1] - lo)
-            s_act(ea, ch("T2A", k), F.Exp, bias=math.log(3.0), scale=-0.125)
-            s_act(ch("GD", k), ch("T2B", k), F.Exp, scale=-0.125)
-            either(lambda: v_ts(less, ea, -1.0 / 3, A.mult), lambda: s_act(less, ea, F.Identity, scale=-1.0 / 3))
-        stage(e, p, True)
-        dma("G", [(ap(("GD", lo, hi)), ap(e2))], [e2], [("GD", lo, hi)], 5.0, accum_op=A.add, max_dma_last_dim=2048)
+    for k in (1, 0):
+        cp("*", ch("DL", k), ch("P", k))
+    n = TUNE["ends"]
+    for k in range(V // n):
+        ea, less = next_ex(n), next_ex(n)
+        s_act(ea, ch("T2A", k, n), F.Exp, bias=math.log(3.0), scale=-0.125)
+        s_act(ch("GD", k, n), ch("T2B", k, n), F.Exp, scale=-0.125)
+        cp("*", less, ea, None, -1.0 / 3)
+        summed_up(ea, k * n, True)
+        dma("G", [(ap(ch("GD", k, n)), ap(less))], [less], [ch("GD", k, n)], 3.6 + n / 400, accum_op=A.add, max_dma_last_dim=2048)
     for rnd in range(2):
         f = 2 * rnd
         if rnd:
@@ -796,8 +819,9 @@ def build(g, core, T, topo):
             dma("Y", [(T.lnN[q], T.stN[q])], [("stN", 0, 4)], [("lnN", q, q + 1)], 2.4)
             dma("Y", [(T.EN[:], T.lnN[:])], [("lnN", 0, 4)], [("EN", 0, V)], 3.0)
         else:
-            open_window(["E", "DB"])
+            open_window(["DB"])
             for k in (3, 2, 1, 0):
+                pe(group(ch("P", k), [(ID, ch("E", k))], False, False), acc=True)
                 close_window(k, "PN0")
             tolls_and_edges()
         cur[0] = 1 - cur[0]
@@ -816,20 +840,23 @@ def build(g, core, T, topo):
 
     mine = ch("DLT", 1, 128)
     v_tt(mine, ch("UW", 2, 128), ch("UW", 3, 128), A.subtract)
-    send(8, [(r, ap(mine), ap(ch("DH", q, 128))) for r in others], [mine], [ch("DH", r, 128) for r in others], 1.1)
+    told = send(8, [(r, ap(mine), ap(ch("DH", q, 128))) for r in others], [mine], [ch("DH", r, 128) for r in others], 1.1)
     tiles = [mine if r == q else ch("DH", r, 128) for r in range(4)]
     add("T", lambda: [[g.tensor.matmul(T.Q[32 * r:32 * r + 32, 0:128], T.II[:, 32 * q:32 * q + 32], ap(tiles[r]), True, True)
-                       for r in range(4)][-1]], tiles + [ID], [("Q", 0, 128)], 0.06 + 512 * PCY)
+                       for r in range(4)][-1]], tiles + [ID, ("GD", 0, V)], [("Q", 0, 128)], 0.06 + 512 * PCY)
     cp("*", ("DN", 0, 128), ("Q", 0, 128))
-    for k in range(4):
-        new_tolls(ch("P", k), k, ("DN", 0, 128), "EN", "W0")
-        dma("Y", [(T.tollout[:, 512 * k:512 * k + 512], ap(ch("W0", k)))], [ch("W0", k)], [], 2.5)
+    for p, (lo, hi) in enumerate(GAIN):
+        st, ln, w = "stG%d" % p, "lnG%d" % p, hi - lo
+        staged = dma("Y", [(T[st][:], T.GD[:, lo:hi])], [("GD", lo, hi)], [(st, 0, 4)], 2.4 + 0.8 * w / 512)
+        send(17 + p, [(r, T[st][r], T[ln][q]) for r in others], [(st, 0, 4)], [(ln, r, r + 1) for r in others], 2.7 * w / 512)
+        ops[-3]["after"] = TUNE["behind"] and told if p == len(GAIN) - 1 else None
     for p, (lo, hi) in enumerate(GAIN):
         st, ln = "stG%d" % p, "lnG%d" % p
-        send(9 + p, [(r, T[st][r], T[ln][q]) for r in others], [(st, 0, 4)], [(ln, r, r + 1) for r in others],
-             2.7 * (hi - lo) / 512)
-        dma("Y", [(T.gain[rows, lo:hi], T[st][q])], [(st, 0, 4)], [], 2.8)
-        dma("Y", [(T.gain[32 * r:32 * r + 32, lo:hi], T[ln][r]) for r in others], [(ln, r, r + 1) for r in others], [], 3.0)
+        ops[dma("Y", [(T.gain[32 * r:32 * r + 32, lo:hi], T[st if r == q else ln][r]) for r in range(4)],
+                [(st, q, q + 1)] + [(ln, r, r + 1) for r in others], [], 2.4 + 0.8 * (hi - lo) / 512)]["after"] = staged
+    for k in range(4):
+        new_tolls(ch("P", k), k, ("DN", 0, 128), "EN", "W0")
+        ops[dma("Y", [(T.tollout[:, 512 * k:512 * k + 512], ap(ch("W0", k)))], [ch("W0", k)], [], 2.5)]["after"] = staged
     return ops
 
 
@@ -853,8 +880,7 @@ def dependencies(ops):
             if w:
                 old = [e for e in old if not (lo <= e[0] and e[1] <= hi)]
             log[name] = old + [(lo, hi, n, w)]
-        if o["after"] is not None:
-            order.add(o["after"])
+        order.update(x for x in (o["after"], o.get("more")) if x is not None)
         o["deps"], o["order"] = deps, order - deps
 
 
@@ -996,115 +1022,155 @@ def refine(ops):
     start, where = greedy(ops, [-x for x in rank])
     order = [(k, where[k]) for k in sorted(range(n), key=lambda k: (start[k], k))]
     ends = [replay(ops, order, case) for case in CASES]
-    best = (sum(ends), start, order, ends[0])
+    best = (sum(ends), order)
     rank = start
-    for turn in range(TUNE["turns"]):
-        if turn:
-            start, size = best[1], TUNE["shake"] * draw()
-            lo = draw() * best[3]
-            hi = lo + TUNE["span"] * (0.3 + draw())
-            rank = [start[k] + (size * (draw() - 0.5) if lo <= start[k] < hi else 0.0) for k in range(n)]
-        for _ in range(TUNE["passes"] if turn == 0 else 2):
-            start, where = pack(ops, before, rank, False)
-            order = [(k, where[k]) for k in sorted(range(n), key=lambda k: (start[k], k))]
-            ends = [replay(ops, order, case) for case in CASES]
-            if best is None or sum(ends) < best[0]:
-                best = (sum(ends), start, order, ends[0])
-            back, _ = pack(ops, after, [-start[k] - ops[k]["dur"] for k in range(n)], True)
-            rank = [-back[k] - ops[k]["dur"] for k in range(n)]
-    order = polish(ops, best[2], after, draw)
-    ORDER["end"] = replay(ops, order, CASES[0])
-    return order
+    for _ in range(TUNE["passes"]):
+        start, where = pack(ops, before, rank, False)
+        order = [(k, where[k]) for k in sorted(range(n), key=lambda k: (start[k], k))]
+        ends = [replay(ops, order, case) for case in CASES]
+        if sum(ends) < best[0]:
+            best = (sum(ends), order)
+        back, _ = pack(ops, after, [-start[k] - ops[k]["dur"] for k in range(n)], True)
+        rank = [-back[k] - ops[k]["dur"] for k in range(n)]
+    return polish(ops, best[1], after, draw)
 
 
 def polish(ops, order, after, draw):
     n = len(ops)
-    deps = [list(o["deps"]) for o in ops]
-    soft = [list(o["order"]) for o in ops]
-    users = [list(u) for u in after]
-    count = [len(deps[k]) + len(soft[k]) for k in range(n)]
-    cases = [(LAT * c["w"], c["weight"], {e: [((o["alt"][e][1],) * 2 if "alt" in o and e in "VS" else (o["issue"], o["dur"]))
-                                              for o in ops] for e in QUEUES}, [c[o["cls"]] for o in ops]) for c in CASES[:TUNE["cases"]]]
-    line = {e: [k for k, x in order if x == e] for e in QUEUES}
+    deps, soft = [list(o["deps"]) for o in ops], [list(o["order"]) for o in ops]
+    before, users = [deps[k] + soft[k] for k in range(n)], [list(u) for u in after]
+    gaps = [[(u, LAT if k in ops[u]["deps"] else 0.0) for u in users[k]] for k in range(n)]
+    factors = [[c[o["cls"]] for o in ops] for c in CASES]
+    where, prv, nxt, last = [None] * n, [-1] * n, [-1] * n, {}
 
-    def run():
-        where, nxt, missing = [None] * n, [-1] * n, list(count)
-        for e, seq in line.items():
-            for j, k in enumerate(seq):
-                where[k] = e
-                if j:
-                    nxt[seq[j - 1]] = k
-                    missing[k] += 1
-        seq = [k for k in range(n) if not missing[k]]
+    def span(k, e):
+        return (ops[k]["alt"][e][1],) * 2 if "alt" in ops[k] else (ops[k]["issue"], ops[k]["dur"])
+
+    def link(p, k, u):
+        prv[k], nxt[k] = p, u
+        if p >= 0:
+            nxt[p] = k
+        if u >= 0:
+            prv[u] = k
+
+    for k, e in order:
+        where[k] = e
+        link(last.get(e, -1), k, -1)
+        last[e] = k
+    issue, dur = [span(k, where[k])[0] for k in range(n)], [span(k, where[k])[1] for k in range(n)]
+
+    def sort(part, inside, waits, led):
+        missing, seq = dict(waits), []
+        for k in part:
+            if prv[k] >= 0 and inside[prv[k]]:
+                missing[k] += 1
+            elif not missing[k]:
+                seq.append(k)
         for k in seq:
-            for u in users[k]:
+            for u in led[k]:
                 missing[u] -= 1
                 if not missing[u]:
                     seq.append(u)
             u = nxt[k]
-            if u >= 0:
+            if u >= 0 and inside[u]:
                 missing[u] -= 1
                 if not missing[u]:
                     seq.append(u)
-        if len(seq) < n:
-            return None
-        total, chains = 0.0, []
-        for wake, weight, spans, factor in cases:
-            free, last, end, why = dict.fromkeys(line, 0.0), dict.fromkeys(line, -1), [0.0] * n, [-1] * n
-            for k in seq:
-                e = where[k]
-                t, w = free[e], last[e]
-                for d in deps[k]:
-                    if end[d] + wake > t:
-                        t, w = end[d] + wake, d
-                for d in soft[k]:
-                    if end[d] > t:
-                        t, w = end[d], d
-                issue, dur = spans[e][k]
-                free[e], end[k], why[k], last[e] = t + issue * factor[k], t + dur * factor[k], w, k
-            k = end.index(max(end))
-            total += weight * (end[k] + TUNE["pull"] * sum(end) / n)
-            chains.append((k, why))
-        return total, seq, where, chains
+        return seq
 
-    best = run()
+    def heads(seq, c, start, end):
+        wake, f = LAT * CASES[c]["w"], factors[c]
+        for k in seq:
+            p = prv[k]
+            t = start[p] + issue[p] * f[p] if p >= 0 else 0.0
+            for d in deps[k]:
+                if end[d] + wake > t:
+                    t = end[d] + wake
+            for d in soft[k]:
+                if end[d] > t:
+                    t = end[d]
+            start[k], end[k] = t, t + dur[k] * f[k]
+
+    def tails(seq, rest):
+        for k in reversed(seq):
+            t = 0.0
+            for u, gap in gaps[k]:
+                if rest[u] + gap > t:
+                    t = rest[u] + gap
+            t, u = t + dur[k], nxt[k]
+            rest[k] = issue[k] + rest[u] if u >= 0 and issue[k] + rest[u] > t else t
+
+    def value(seq):
+        total = 0.0
+        for c in range(TUNE["cases"] - 1, -1, -1):
+            start, end = [0.0] * n, [0.0] * n
+            heads(seq, c, start, end)
+            total += CASES[c]["weight"] * (max(end) + TUNE["pull"] * sum(end) / n)
+        return total, seq, start, end
+
+    def insert(k, stretch, lines, start, end, rest, hold, wait, lean):
+        part, seq = stretch[0], sort(*stretch)
+        heads(seq, 0, start, end)
+        tails(seq, rest)
+        top, ready, tail, best = max(start[j] + rest[j] for j in part), start[k], rest[k] - dur[k], None
+        for e in ("VS" if "alt" in ops[k] else ops[k]["eng"]):
+            (s, d), (line, first, final) = span(k, e), lines[e]
+            a, b = 0, len(line)
+            while a < len(line) and start[line[a]] + issue[line[a]] <= ready + 1e-9:
+                a += 1
+            while b > 0 and rest[line[b - 1]] <= tail + 1e-9:
+                b -= 1
+            for j in range(min(a, b), max(a, b) + 1):
+                p, u = line[j - 1] if j else first, line[j] if j < len(line) else final
+                t = max(ready, start[p] + issue[p]) if p >= 0 else ready
+                long, late = (max(t + d + tail, t + s + rest[u]), max(0.0, t + s - start[u])) if u >= 0 else (t + d + tail, 0.0)
+                cost = 50.0 * max(0.0, long - top) + hold * late + wait * (t - ready) + 0.01 * draw() + lean * s * (e == "V")
+                if best is None or cost < best[0]:
+                    best = (cost, e, j, p, u)
+        _, e, j, p, u = best
+        lines[e][0].insert(j, k)
+        where[k] = e
+        issue[k], dur[k] = span(k, e)
+        link(p, k, u)
+
+    now, rest = value([k for k, _ in order]), [0.0] * n
+    tails(now[1], rest)
     for _ in range(TUNE["moves"]):
-        k, why = best[3][int(draw() * len(cases))]
-        if draw() < TUNE["any"]:
-            k = int(draw() * n)
-        where, links = best[2], []
-        while why[k] >= 0:
-            if where[why[k]] == where[k] and why[k] not in ops[k]["deps"] and why[k] not in ops[k]["order"]:
-                links.append((why[k], k))
-            k = why[k]
-        if not links:
+        seq, start = now[1], now[2]
+        t, wide = draw() * max(start), TUNE["span"] * (0.3 + draw())
+        lo, hi, queues = t - 2.0, t + wide + TUNE["reach"], ("VS", "ST", "VST", "T", "S", "VSTGYD", "GYXD")[int(draw() * 7)]
+        inside = [lo <= x < hi for x in start]
+        part = [k for k in seq if inside[k]]
+        pick = [k for k in part if t <= start[k] < t + wide and where[k] in queues]
+        while len(pick) > TUNE["batch"]:
+            pick.pop(int(draw() * len(pick)))
+        lines = {e: [k for k in part if where[k] == e] for e in QUEUES}
+        if not pick or not lines["V"] or not lines["S"]:
             continue
-        a, b = links[int(draw() * len(links))]
-        e, kind = where[a], draw()
-        saved = {x: list(line[x]) for x in {e, "V", "S"}}
-        seq = line[e]
-        j = seq.index(a)
-        if kind < 0.3 and ("alt" in ops[a] or "alt" in ops[b]):
-            m = a if "alt" in ops[a] and ("alt" not in ops[b] or draw() < 0.5) else b
-            other = line["S" if e == "V" else "V"]
-            place = {x: i for i, x in enumerate(best[1])}
-            seq.remove(m)
-            i = 0
-            while i < len(other) and place[other[i]] < place[m]:
-                i += 1
-            other.insert(max(0, i + int(draw() * 3) - 1), m)
-        elif kind < 0.65:
-            seq.remove(b)
-            seq.insert(max(0, j - int(draw() ** 3 * TUNE["far"])), b)
+        lines = {e: (line, prv[line[0]], nxt[line[-1]]) for e, line in lines.items() if line}
+        saved = (list(prv), list(nxt), list(where), list(issue), list(dur))
+        for k in pick:
+            lines[where[k]][0].remove(k)
+            if prv[k] >= 0:
+                nxt[prv[k]] = nxt[k]
+            if nxt[k] >= 0:
+                prv[nxt[k]] = prv[k]
+            prv[k] = nxt[k] = -1
+        weights = (3.0 * draw() ** 2, 0.3 * draw() ** 3 - 0.02, draw())
+        key = start if draw() < 0.5 else [-x for x in rest]
+        pick.sort(key=lambda k: key[k] + 2.0 * draw())
+        work = (list(start), list(now[3]), list(rest))
+        stretch = (part, inside, {k: sum(inside[d] for d in before[k]) for k in part},
+                   {k: [u for u in users[k] if inside[u]] for k in part})
+        for k in pick:
+            insert(k, stretch, lines, *work, *weights)
+        new = value([k for k in seq if start[k] < lo] + sort(*stretch) + [k for k in seq if start[k] >= hi])
+        if new[0] <= now[0] and len(new[1]) == n:
+            now = new
+            tails(now[1], rest)
         else:
-            seq.remove(a)
-            seq.insert(j + 1 + int(draw() ** 3 * TUNE["far"]), a)
-        new = run()
-        if new is not None and new[0] <= best[0] + TUNE["slack"] * draw():
-            best = new
-        else:
-            line.update(saved)
-    return [(k, best[2][k]) for k in best[1]]
+            prv[:], nxt[:], where[:], issue[:], dur[:] = saved
+    return [(k, where[k]) for k in now[1]]
 
 
 def replay(ops, order, case):
@@ -1129,7 +1195,7 @@ def replay(ops, order, case):
 
 def emit(g, T, ops, order):
     queue = {"V": g.vector, "S": g.scalar, "T": g.tensor, "G": g, "Y": g.sync}
-    total, seen, dmas = {"sent": 0}, {}, [0]
+    total, seen = {"sent": 0}, {}
     for k, e in order:
         o = ops[k]
         if o["kind"] == "x":
@@ -1151,8 +1217,7 @@ def emit(g, T, ops, order):
             total["sent"] += o["count"]
             continue
         if o["kind"] == "d":
-            s, step = "d%d" % dmas[0], 16
-            dmas[0] += 1
+            s, step = o["sem"], 16
         else:
             s, step = "e" + e, 1
         for ins in made:

import math
from concourse.bass import DstId, RemoteDMATransfer
from concourse.mybir import AluOpType, ActivationFunctionType

V = 2048
BIG = 8192.0
CUT = 8.5 * BIG
HI = 192.0
BOTH = 512
FUSED = 1280
BF, F32, F16, I32, U16 = "bfloat16", "float32", "float16", "int32", "uint16"
GAIN = [(0, 512), (512, 1024), (1024, 1536), (1536, 1792), (1792, 2048)]


def _sb(n, d):
    return ("sbuf", [128, n], d)


SCRATCH = {
    "W0": _sb(2 * V, F32), "W1": _sb(2 * V, F32), "CM0": _sb(V, BF), "CM1": _sb(V, BF), "PN": _sb(V, F16),
    "FD": _sb(2 * FUSED, BF), "ZB": _sb(FUSED, F16), "HX": _sb(2 * V, BF), "DC": _sb(V // 2, BF),
    "PN0": _sb(V, F16), "TM": _sb(1536, F16), "DA": _sb(V, BF), "DB": _sb(V, BF), "DL": _sb(V, BF), "E": _sb(V, BF),
    "H": _sb(V, BF), "HW": _sb(2 * V, BF), "dH": ("dram", [128, V], F32),
    "X": _sb(V, F32), "XR": _sb(V, F32), "T1A": _sb(V, F16), "T1B": _sb(V, F16), "T2A": _sb(V, BF),
    "T2B": _sb(V, BF), "YA": _sb(V, BF), "AB": _sb(2 * V, BF), "EX": _sb(5120, F32),
    "YB": _sb(V, BF), "ED": _sb(V, BF), "THR": _sb(2 * V, BF), "MAT": _sb(1824, BF),
    "UNW": _sb(V, BF), "EN": _sb(V, BF), "GD": _sb(V, F32), "DLT": _sb(256, BF), "DH": _sb(512, BF), "DN": _sb(128, BF),
    "ROW": _sb(8, F32), "IF": _sb(128, F32), "LT": _sb(256, F32), "IV": _sb(256, U16), "DG": _sb(512, BF),
    "LI": _sb(256, I32), "ZI": _sb(128, I32), "ZC": _sb(128, F16), "AB16": _sb(1024, U16), "INV": _sb(256, U16),
    "AP": _sb(512, F32), "BP": _sb(512, F32), "VP": _sb(128, F32), "LX": _sb(384, F32), "LY": _sb(128, F32),
    "LZ": _sb(256, I32), "LS": _sb(384, U16), "LP": _sb(512, U16), "T3B": _sb(V, BF),
    "SG": _sb(6 * 256, BF), "MW": _sb(256, BF), "CC": _sb(2048, BF), "UW": _sb(768, BF),
    "RU": _sb(256, BF), "ADW": _sb(384, BF), "TI": _sb(256, I32), "TJ": _sb(256, I32),
    "PI": _sb(16, I32), "PF": _sb(32, F32), "LIFT": _sb(64, BF),
    "JP": _sb(192, F32), "YS": _sb(256, BF), "YG": _sb(224, BF), "YD": _sb(128, BF), "SGN": _sb(224, BF),
    "II": _sb(256, BF), "NID": _sb(128, BF),
    "M32": _sb(256, BF), "N2M": _sb(256, BF), "WIN": _sb(128, BF), "M1": _sb(256, BF),
    "M2": _sb(256, BF),
    "stL": ("dram", [4, 128, 64], I32), "lnL": ("dram", [4, 128, 64], I32),
    "stZ": ("dram", [4, 128, 32], I32), "lnZ": ("dram", [4, 128, 32], I32),
    "stH": ("dram", [4, 128, 512], BF), "lnH": ("dram", [4, 128, 512], BF),
    "stP": ("dram", [4, 128, 512], BF), "lnP": ("dram", [4, 128, 512], BF),
    "stE": ("dram", [4, 128, 512], BF), "lnE": ("dram", [4, 128, 512], BF),
    "stT": ("dram", [8, 128, 256], BF), "lnT": ("dram", [8, 128, 256], BF),
    "stI": ("dram", [8, 128, 32], U16), "lnI": ("dram", [8, 128, 32], U16),
    "stN": ("dram", [4, 128, 512], BF), "lnN": ("dram", [4, 128, 512], BF),
    "dG": ("dram", [128, V], F32),
}
for _p, (_lo, _hi) in enumerate(GAIN):
    SCRATCH["stG%d" % _p] = SCRATCH["lnG%d" % _p] = ("dram", [4, 128, (_hi - _lo) // 4], F32)
MATS, _at = {}, 0
for _n, _w in (("sel", 144), ("vote0", 144), ("vote1", 208), ("over", 144), ("over2", 144), ("on", 208), ("out", 160),
               ("sum", 192), ("sum1", 192), ("winA", 144), ("winB", 144)):
    MATS[_n] = (_at, _w)
    _at += _w
COLS = ["row", "net", "and112", "and14", "and64", "and78", "slot", "odd", "mid", "slot0",
        "even", "at", "at0", "at1", "to", "on", "home", "cut", "end", "none", "none0", "none1", "flip", "nine", "cut2"]
PSUM = {"P": 2048, "Q": 1024, "R": 1024}
for _n in PSUM:
    SCRATCH[_n] = ("psum", [128, PSUM[_n]], F32)

N_DMA_SEMS = 121
SEMAPHORES = ["eV", "eS", "eT", "eG", "sent"] + ["rx%d" % k for k in range(24)] + ["d%d" % k for k in range(N_DMA_SEMS)]

CY, PCY, GA, LAT = 0.00083, 0.00045, 1.56, 0.09
ORDER = {}
QUEUES = "VSTGYXDZ"
SIDE = ("X", "XR", "XS", "YA", "T1A", "T1B", "T2A", "T2B", "T3B", "AB", "EX", "GD", "WIN")
TUNE = {"pieces": [(1024, 2048), (0, 1024)], "cmp": 512, "last": 256,
        "help": [1024] * 13, "aid": 512, "banks": [1, 0], "fused": [(256, 1536)] * 13, "hold": 0,
        "lists": [[None, (0, 0, 1024)], [None, (0, 0, 256)]] * 2, "apart": [1, 7], "walk": [(256, 1024), (0, 256)],
        "terms": GAIN, "t2": [0, 1, 2, 3], "join": 1024, "gates": 512, "ends": 512, "broad": 512, "early": 15.0, "both": [6, 12], "third": 2, "head": 1024,
        "wide": 512, "v_abs": [], "skew": 5.0, "acc": 0.9, "rate": 5e5, "dma": 0.85, "behind": None,
        "own": 0.0, "urgent": 1.0, "hops": 1, "share": 0.3, "lean": 0.5, "side": 3.0, "passes": 4, "seed": 2,
        "pull": 0.3, "cases": 3, "moves": 11000, "span": 10.0, "reach": 14.0, "batch": 16}
CASES = [{"g": 1.0, "s": 1.0, "c": 1.0, "p": 1.0, "d": 1.0, "w": 1.0, "weight": 1.0},
         {"g": 0.95, "s": 1.4, "c": 1.3, "p": 1.3, "d": 1.5, "w": 1.6, "weight": 0.8},
         {"g": 1.6, "s": 1.8, "c": 1.25, "p": 1.25, "d": 1.1, "w": 1.2, "weight": 0.7},
         {"g": 1.25, "s": 1.6, "c": 1.25, "p": 1.6, "d": 1.3, "w": 2.0, "weight": 0.4}]


def split_engines(topo, src, dsts):
    far = [d for d in dsts if topo.chip(d) != topo.chip(src)]
    near = [d for d in dsts if topo.chip(d) == topo.chip(src)]
    out, used = {}, []
    for group in (far, near):
        if not group:
            continue
        pool = [e for e in topo.engines(src, group[0]) if e not in used]
        n = 1
        while 2 * n * len(group) <= len(pool) and (not out or n < min(m for _, m in out.values())):
            n *= 2
        for k, d in enumerate(group):
            mine = pool[k * n:(k + 1) * n]
            used.extend(mine)
            out[d] = (sum(1 << e for e in mine), n)
    return out


def build(g, core, T, topo):
    q = T.rank_of(core)
    cores = list(T.cores)
    others = [r for r in range(4) if r != q]
    A, F = AluOpType, ActivationFunctionType
    ops, dmas = [], [0]
    bias = [0.0]

    def add(eng, fn, rd, wr, dur, kind="c", issue=None, after=None, acc=False, sem=None, count=0):
        listed = any(x[0] in ("AB16", "INV", "LS", "LP") for x in rd)
        cls = "p" if eng == "T" else "d" if kind != "c" else "g" if listed else "c"
        if kind == "x":
            dur, issue = dur * TUNE["dma"], issue and issue * TUNE["dma"]
        ops.append({"cls": cls, "eng": eng, "fn": fn, "rd": rd, "wr": wr, "dur": dur, "kind": kind, "acc": acc,
                    "bias": bias[0] - (TUNE["side"] if any(x[0] in SIDE for x in wr + rd) else 0.0),
                    "issue": dur if issue is None else issue, "after": after, "sem": sem, "count": count})
        return len(ops) - 1

    def ap(x):
        return T[x[0]][:, x[1]:x[2]:x[3]] if len(x) > 3 else T[x[0]][:, x[1]:x[2]]

    def width(x):
        return (x[2] - x[1] + (x[3] - 1 if len(x) > 3 else 0)) // (x[3] if len(x) > 3 else 1)

    def two(x):
        return SCRATCH[x[0]][2] in (BF, F16, U16)

    def src(x, lst):
        return ap(x).indirect(ap(lst)) if lst else ap(x)

    def cols(*xs):
        return [x for x in xs if isinstance(x, tuple)]

    def val(x):
        return ap(x) if isinstance(x, tuple) else x

    def v_tt(o, a, b, op, lst=None):
        n = width(o)
        f = GA if lst else (1.0 if a[0] in PSUM or b[0] in PSUM else 2.0)
        add("V", lambda: [g.vector.tensor_tensor(ap(o), src(a, lst), ap(b), op)], cols(a, b, lst), [o], 0.06 + max(64, n * f) * CY)

    def v_ts(o, a, s1, op0, s2=None, op1=None, lst=None):
        n = width(o)
        f = GA if lst else (0.5 if two(o) and two(a) else 1.0)

        def fn():
            if op1 is None:
                return [g.vector.tensor_scalar(ap(o), src(a, lst), val(s1), None, op0)]
            return [g.vector.tensor_scalar(ap(o), src(a, lst), val(s1), val(s2), op0, op1)]
        add("V", fn, cols(a, s1, s2, lst), [o], 0.06 + max(64, n * f) * CY)

    def v_cp(o, a, lst=None):
        n = width(o)
        f = GA if lst else (0.5 if two(o) and two(a) else 1.0)
        add("V", lambda: [g.vector.tensor_copy(ap(o), src(a, lst))], cols(a, lst), [o], 0.06 + max(64, n * f) * CY)

    def s_act(o, a, func, bias=0.0, scale=1.0, lst=None, after=None):
        n = width(o)
        add("S", lambda: [g.scalar.activation(ap(o), src(a, lst), func, bias=val(bias), scale=val(scale))],
            cols(a, bias, scale, lst), [o], 0.075 + max(64, n * (GA if lst else 1.0)) * CY, after=after)

    def either(on_v, on_s):
        on_s()
        other = ops.pop()
        on_v()
        ops[-1]["alt"] = {"V": (ops[-1]["fn"], ops[-1]["dur"]), "S": (other["fn"], other["dur"])}

    def cp(eng, o, a, lst=None, times=1.0, plus=0.0):
        if eng == "V" and (times, plus) == (1.0, 0.0):
            v_cp(o, a, lst)
        elif eng == "V":
            v_ts(o, a, times, A.mult, plus, A.add, lst=lst)
        elif eng == "S":
            s_act(o, a, F.Identity, bias=plus, scale=times, lst=lst)
        else:
            either(lambda: cp("V", o, a, lst, times, plus), lambda: cp("S", o, a, lst, times, plus))

    def pe(mms, acc=False):
        def fn():
            done = []
            for k, (o, l, r, st, sp) in enumerate(mms):
                ins = g.tensor.matmul(ap(o), ap(l), ap(r), st, sp)
                if k == len(mms) - 1:
                    done.append(ins)
            return done
        cyc = sum(max(64, width(m[2])) * (1 if two(m[2]) else 4) for m in mms)
        add("T", fn, [m[1] for m in mms] + [m[2] for m in mms], [mms[0][0]], 0.06 + cyc * PCY, acc=acc)

    def group(o, pairs, first=True, last=True):
        return [(o, l, r, first and k == 0, last and k == len(pairs) - 1) for k, (l, r) in enumerate(pairs)]

    def dma(eng, pairs, rd, wr, dur, **kw):
        queue, done = {"Y": g.sync, "S": g.scalar, "G": g}[eng], {"sem": "d%d" % dmas[0], "count": 16 * len(pairs)}
        dmas[0] += 1
        size = sum((x[2] - x[1]) * (128 if len(SCRATCH[x[0]][1]) == 2 else math.prod(SCRATCH[x[0]][1][1:])) * (2 if two(x) else 4)
                   for x in wr or rd)
        hold, issue = size * (2 if kw else 1) / TUNE["rate"], (1.3 if eng == "G" else 0.06) * len(pairs)
        me = add(eng, lambda: [queue.dma_start(o, i, **kw) for o, i in pairs], rd, wr, min(issue, 1.0), kind="d", issue=issue, **done)
        moved = add("D", None, [], [], hold, kind="x", after=me, **done)
        add("Z", None, rd, wr, max(dur - hold - min(issue, 1.0), 1.0), kind="x", issue=0.0, after=moved, **done)
        return me

    def send(k, plan, rd, wr, dur):
        masks = split_engines(topo, core, [cores[r] for r, _, _ in plan])
        sem = T.sem["rx%d" % k]

        def fn():
            tr = []
            for r, s, d in plan:
                rid, pid, _ = topo.addr(cores[r])
                tr.append(RemoteDMATransfer(dst_ids=[DstId(rid=rid, pnc=pid)], dma_engine_mask=masks[cores[r]][0],
                                            remote_sem=sem, src=s, dst=d))
            g.remote_dma_fused(tr, local_sem=T.sem.sent)
            return []
        me = add("G", fn, rd, [], 0.5, kind="r", count=sum(n for _, n in masks.values()))
        got = 0
        for r, _, _ in plan:
            s = (2 * q - r) % 4
            got += split_engines(topo, cores[s], [cores[(s + x - q) % 4] for x, _, _ in plan])[core][1]
        link = add("X", None, [], [("link", 0, 1)] * (k < 5), dur, kind="x", after=me, sem="rx%d" % k, count=got)
        add("Z", None, [], wr, 2.6, kind="x", issue=0.0, after=link, sem="rx%d" % k, count=got)
        return me

    def in_line(begin, engines="VS"):
        for e in engines:
            line = [k for k in range(begin, len(ops)) if ops[k]["eng"] == e and "alt" not in ops[k] and ops[k]["kind"] == "c"]
            for a, b in zip(line, line[1:]):
                ops[b]["after"] = a

    def ch(name, k, n=512, base=0):
        return (name, base + k * n, base + (k + 1) * n)

    def part(name, lo, hi, base=0):
        return ("AB", V + lo, V + hi) if name == "T3A" else (name, base + lo, base + hi)

    def lst(name, base, lo, hi):
        return (name, base + lo // 16, base + hi // 16)

    def cut(lo, hi, n):
        return [(a, min(a + n, hi)) for a in range(lo, hi, n)][::-1]

    ID, NID, N2, N32, P32 = ("II", 0, 128), ("NID", 0, 128), ("N2M", 0, 128), ("M32", 0, 128), ("M32", 128, 256)

    def rot(t):
        return ("II", 32 * t, 32 * t + 128)

    def mat(name, shift=0, turn=0):
        at = MATS[name][0] + 16 - shift + turn
        return ("MAT", at, at + 128)

    def whole(name):
        return ("MAT", MATS[name][0], MATS[name][0] + MATS[name][1])

    def pf(name):
        return ("PF", COLS.index(name), COLS.index(name) + 1)

    def unw(i):
        return ("UNW", 128 * i, 128 * i + 128)

    rows = slice(32 * q, 32 * q + 32)
    dma("Y", [(T.stL[:, 0:64, :], T.sa[:]), (T.stL[:, 64:128, :], T.sb[:])], [], [("stL", 0, 4)], 2.2)
    dma("S", [(T.TI[:, 0:128], T.sa[:]), (T.TI[:, 128:256], T.sb[:])], [], [("TI", 0, 256)], 2.4)
    ops[-3]["bias"] = 50.0
    features = dma("Y", [(T.stH[:], T.hf[:])], [], [("stH", 0, 4)], 2.8)
    ops[-3]["after"], ops[-2]["more"] = 0, 4
    dma("S", [(T.lnL[q, 0:64, :], T.sa[rows]), (T.lnL[q, 64:128, :], T.sb[rows])], [], [("lnL", q, q + 1)], 2.2)
    later = [("stH", 0, 4)]
    dma("S", [(T.AB[:, 0:V], T.p0[:])], [], [("AB", 0, V)], 2.8)
    ops[-2]["more"] = features + 1
    cp("V", ("AB", 0, V), ("AB", 0, V), plus=-128.0)
    lowered = len(ops) - 1
    dma("Y", [(T.stP[:], T.AB[:, 0:V]), (T.lnP[q], T.AB[rows, 0:V])], [("AB", 0, V)], [("stP", 0, 4), ("lnP", q, q + 1)], 3.2)
    dma("Y", [(T.stE[:], T.toll[:])], later, [("stE", 0, 4)], 3.0)
    dma("Y", [(T.stZ[:], T.lim[:])], later, [("stZ", 0, 4)], 2.6)
    dma("Y", [(T.lnH[q], T.hf[rows]), (T.lnE[q], T.toll[rows]), (T.lnZ[q], T.lim[2 * q:2 * q + 2])],
        later, [("lnH", q, q + 1), ("lnE", q, q + 1), ("lnZ", q, q + 1)], 3.0)

    def iota(o, pat, base, cm):
        small = SCRATCH[o[0]][2] != I32
        add("G", lambda: [g.iota(ap(o), pat, base, cm, allow_small_or_imprecise_dtypes=small)], [], [o], 0.13 + 2 * width(o) * CY)

    def select(o, a, pat, op, fill, base, cm=-1):
        add("G", lambda: [g.affine_select(ap(o), ap(a), pat, op, fill, base, cm)], [a], [o], 0.17 + 2 * width(o) * CY)

    def exchange(k, nm, dur, behind=()):
        send(k, [(r, T["st" + nm][r], T["ln" + nm][q]) for r in others], [("st" + nm, 0, 4), *behind],
             [("ln" + nm, r, r + 1) for r in others], dur)

    first_g = len(ops)
    iota(("PI", 8, 9), [[0, 1]], 0, 1)
    iota(ch("X", 0), [[1, 512]], 32, 0)
    iota(("JP", 0, 192), [[1, 192]], -64, 0)
    iota(("VP", 0, 128), [[16, 128]], int(CUT), 0)
    exchange(0, "L", 1.3)
    ops[-3]["dur"] = ops[-3]["issue"] = 5.5
    exchange(1, "H", 5.4)
    turn, nil = [[0, 2], [1, 128]], ("DG", 0, 256)
    iota(nil, [[0, 256]], 0, 0)
    select(("II", 0, 256), nil, turn, A.not_equal, 1.0, 0)
    select(("ROW", 0, 8), ("DG", 0, 8), [[16, 8]], A.not_equal, 1.0, 0)
    select(("IF", 0, 128), ("DG", 0, 128), [[1, 128]], A.not_equal, 1.0, 0)
    select(NID, ("DG", 0, 128), [[1, 128]], A.not_equal, -1.0, 0)
    iota(("YG", 0, 160), [[32, 5], [0, 2], [1, 16]], -32, 0)
    iota(("YG", 160, 224), [[32, 2], [0, 2], [1, 16]], 0, 0)
    iota(("SGN", 0, 224), [[0, 7], [-4, 2], [0, 16]], 2, 0)
    exchange(2, "P", 5.4)
    iota(("YS", 0, 192), [[64, 3], [0, 4], [1, 16]], -64, 0)
    iota(("YS", 192, 256), [[0, 4], [1, 16]], 0, 0)
    select(("N2M", 0, 256), nil, turn, A.not_equal, -2.0, 0)
    select(N32, ("DG", 0, 128), [[1, 128]], A.not_equal, -32.0, 0)
    select(P32, ("DG", 0, 128), [[1, 128]], A.not_equal, 32.0, 0)
    select(("LIFT", 0, 64), ("DG", 0, 64), [[1, 64]], A.is_ge, 8 * BIG, -BOTH // 16, 0)
    exchange(3, "E", 5.4, [("lnH", 0, 4)])
    exchange(4, "Z", 1.0)
    for k in range(4):
        iota(ch("UNW", k), [[0, 512]], 4, 0)
        select(ch("UNW", k), ch("UNW", k), [[1, 4], [16, 8], [0, 16]], A.is_equal, 0.0, 4 * k)
    for name, on in (("M1", -1), ("M2", 1)):
        iota((name, 0, 256), [[0, 8], [on, 2], [0, 16]], (1 - on) // 2, 0)
        select((name, 0, 256), (name, 0, 256), turn, A.is_equal, 0.0, -16 * on)
    select(("M1", 0, 256), ("M1", 0, 256), turn, A.not_equal, 2.0, 0)
    for b in range(2):
        iota(("YD", 0, 128), [[0, 64], [4 * b - 2, 2]], 2 - 2 * b, 0)
        for n in range(2):
            select(ch("DG", 2 * n + b, 128), ("YD", 0, 128), [[64, 2], [0, 2], [1, 32]], A.is_equal, 0.0, 32 * n)
    line = [k for k in range(first_g, len(ops)) if ops[k]["eng"] == "G"]
    for a, b in zip(line, line[1:]):
        ops[b]["after"] = a
    dma("Y", [(T.AB[:, V:2 * V], T.lnP[:])], [("lnP", 0, 4)], [("AB", V, 2 * V)], 3.2)
    dma("Y", [(T.LI[:, 0:128], T.lnL[:, 0:64, :]), (T.LI[:, 128:256], T.lnL[:, 64:128, :])], [("lnL", 0, 4)], [("LI", 0, 256)], 2.2)
    window = dma("Y", [(T.HW[32:128, V:2 * V], T.lnH[0:3]), (T.HW[0:32, V:2 * V], T.lnH[3])], [("lnH", 0, 4)], [("HW", V, 2 * V)], 3.6)
    ops[dma("Y", [(T.H[:], T.lnH[:])], [("lnH", 0, 4)], [("H", 0, V)], 3.6)]["after"] = window
    ops[-2]["more"] = window + 1
    tolls = dma("Y", [(T.E[:], T.lnE[:])], [("lnE", 0, 4)], [("E", 0, V)], 2.8) + 1
    dma("Y", [(T.ZI[32:128], T.lnZ[0:3]), (T.ZI[0:32], T.lnZ[3])], [("lnZ", 0, 4)], [("ZI", 0, 128)], 2.2)

    begin = len(ops)
    BITS = {"row": (15, A.bitwise_and), "net": (4, A.arith_shift_right, 1, A.bitwise_and),
            "odd": (5, A.arith_shift_right, 1, A.bitwise_and), "slot": (1, A.bitwise_and)}
    BITS.update({"and%d" % m: (m, A.bitwise_and) for m in (112, 14, 64, 78)})

    def bits(names):
        for nm in names:
            k = COLS.index(nm)
            v_ts(("PI", k, k + 1), ("PI", 8, 9), *BITS[nm])
        lo, hi = COLS.index(names[0]), COLS.index(names[-1]) + 1
        v_cp(("PF", lo, hi), ("PI", lo, hi))

    bits(COLS[0:8])
    v_ts(whole("sel"), ("JP", 48, 192), pf("and112"), A.is_equal, BIG, A.mult)
    for k in (1, 2, 3):
        s_act(ch("X", k), ch("X", 0), F.Identity, bias=512.0 * k)

    def lin(o, a, times, plus=0.0):
        cp("*", pf(o), pf(a), None, pf(times) if isinstance(times, str) else times, pf(plus) if isinstance(plus, str) else plus)

    def walk_matrices():
        jp = ("JP", 48, 192)
        lin("slot0", "slot", -1.0, 1.0)
        lin("even", "odd", -1.0, 1.0)
        lin("flip", "and64", -2.0, 64.0)
        lin("at", "net", 32.0, "odd")
        lin("at0", "and64", 1.0, "at")
        lin("at1", "flip", "odd", "at0")
        lin("to", "odd", 8.0, "and64")
        lin("on", "slot", 1.0, "to")
        lin("home", "flip", "slot0", "and78")
        lin("home", "slot", 32.0, "home")
        lin("home", "odd", 16.0, "home")
        lin("cut", "net", -34.0, 17.0)
        v_ts(pf("cut2"), pf("and14"), BOTH / 128 - 1, A.is_gt, 15.0 / 17, A.mult)
        v_ts(pf("cut2"), pf("cut2"), 2.0 / 17, A.add, pf("cut"), A.mult)
        v_ts(pf("nine"), pf("and14"), TUNE["fused"][3][0] / 128 - 1, A.is_gt, -16.0, A.mult)
        v_ts(pf("at"), pf("and14"), TUNE["fused"][3][1] / 128 - 1, A.is_lt, pf("nine"), A.mult)
        lin("nine", "at", 1.0, -1.0)
        v_ts(whole("vote1"), ("YG", 16, 224), pf("at1"), A.is_equal, -1.0, A.mult)
        v_ts(whole("vote0"), ("YG", 80, 224), pf("at0"), A.is_equal, -1.0, A.mult)
        cp("*", whole("over"), part("MAT", 64, 208, MATS["vote1"][0]))
        cp("*", whole("over2"), whole("over"), None, -2.0)
        v_tt(whole("vote1"), whole("vote1"), ("SGN", 16, 224), A.mult)
        v_tt(whole("vote0"), whole("vote0"), ("SGN", 16, 160), A.mult)
        v_ts(whole("on"), ("YS", 48, 256), pf("on"), A.is_equal)
        v_ts(whole("out"), ("JP", 32, 192), pf("to"), A.is_equal, pf("slot0"), A.mult)
        v_ts(whole("sum"), ("JP", 0, 192), pf("and78"), A.is_equal, pf("even"), A.mult)
        cp("*", whole("sum1"), whole("sum"), None, pf("slot"))
        lin("end", "net", -7.5, 1.5)
        lin("end", "end", "slot", -2.0)
        lin("none", "odd", 2.0, 2.0)
        lin("none1", "none", "net")
        lin("none0", "none1", -1.0, "none")
        v_ts(whole("winA"), jp, pf("home"), A.is_equal, pf("net"), A.mult)
        cp("*", whole("winB"), whole("winA"), None, 0.5)

    def votes(o, name, lo, hi, first=True):
        pe(group(o, [(mat("sel", i), (name, lo + i, hi, 16)) for i in range(16)], first), acc=not first)

    def compact(name, lo, hi, o, by, turn=0, n=256, first=True, last=True, base=0):
        pairs = [(mat(by, i * n // 128, turn), (name, base + n * i, base + n * i + n)) for i in range(lo // n, hi // n)]
        pe(group(o, pairs, first, last), acc=not first)

    def spread(o, a, b, small, first, last):
        return [((o[0], o[1] + c - a, o[1] + c - a + 128), unw(c // 128), small, first, last and (first or c + 128 == b))
                for c in range(a, b, 128)]

    def summed(o, k, pairs, small=None, last=True):
        mm = group(o, [(l, ch(r, k)) for l, r in pairs], True, last and small is None)
        return mm + (spread(o, 512 * k, 512 * k + 512, small, not pairs, True) if small else [])

    v_cp(("INV", 0, 256), ("TI", 0, 256))
    add("V", lambda: [g.vector.tensor_copy(T.W1[:, 0:V].indirect(T.INV[:, 0:128]), T.X[:])],
        [("X", 0, V), ("INV", 0, 128)], [("W1", 0, V)], 2.4 * GA * V * CY)
    add("S", lambda: [g.scalar.activation(T.W1[:, V:2 * V].indirect(T.INV[:, 128:256]), T.X[:], F.Silu)],
        [("X", 0, V), ("INV", 128, 256)], [("W1", V, 2 * V)], 1.3 + 2.4 * GA * V * CY)
    for o in ops[-2:]:
        o["cls"], o["bias"] = "s", 50.0
    ops[-2]["more"] = lowered
    lin("mid", "and14", -1.0, -159.5 / 128)
    for s in range(2):
        for j in range(0, 16, 4):
            pe([(("R", 512 * s + i, 512 * s + 128, 16), ("W1", V * s + i, V * s + V, 16), ("ROW", 0, 8), True, True)
                for i in range(j, j + 4)], acc=j > 0)
    v_ts(("VP", 0, 128), ("VP", 0, 128), pf("row"), A.add)
    v_cp(("AB16", 0, 256), ("LI", 0, 256))

    for k in (3, 2, 1, 0):
        cp("S" if k > 1 else "V", ch("HW", k), ("HW", V, 2 * V), lst("AB16", 0, 512 * k, 512 * k + 512))
    for k in (3, 2, 1, 0):
        v_tt(ch("YB", k), ("HW", V, 2 * V), ch("H", k), A.subtract, lst=lst("AB16", 128, 512 * k, 512 * k + 512))
    for k in (3, 2, 1, 0):
        pe(summed(ch("P", k), k, [(ID, "HW"), (NID, "H")]))
        s_act(ch("DA", k), ch("P", k), F.Abs)
        s_act(ch("DB", k), ch("YB", k), F.Abs)
        pe(summed(ch("P", k), k, [(ID, "DA"), (NID, "DB")]))
        if k > 1:
            cp("V", ch("DL", k), ch("P", k))
    in_line(begin)
    for s in range(2):
        cp("*", ch("LT", s, 128), part("R", 0, 128, 512 * s), plus=-32.0)
    for s in range(2):
        pe([(ch("R", s, 128), ch("LT", s, 128), ("IF", 0, 128), True, True)])
    bias[0], children = 30.0, len(ops)
    v_cp(("TI", 0, 256), ("R", 0, 256))
    v_ts(("TJ", 0, 256), ("TI", 0, 256), 255, A.bitwise_and)
    v_cp(("IV", 0, 256), ("TJ", 0, 256))
    bias[0] = 0.0
    v_ts(("AP", 0, 128), ("LI", 0, 128), CUT, A.add)
    v_ts(("BP", 0, 128), ("LI", 128, 256), CUT + V, A.add)
    v_ts(("ZC", 0, 128), ("ZI", 0, 128), 0.5, A.mult, 0.25, A.add)

    def turned(eng, o, a, t, dur, behind=(), **kw):
        cutp = 128 - 32 * t
        dma(eng, [(T[o[0]][0:cutp, o[1]:o[2]], T[a[0]][32 * t:128, a[1]:a[2]]), (T[o[0]][cutp:128, o[1]:o[2]], T[a[0]][0:32 * t, a[1]:a[2]])],
            [a, *behind], [o], dur, **kw)

    OWN = min(TUNE["help"][1:])
    edges = {0: ("DL", OWN), 1: ("H", 0), 2: ("H", V // 2), 3: ("DC", 0)}
    for t in (1, 2, 3):
        for name, n in (("AB16", 256), ("BP", 128), ("AP", 128))[:2 + (t > 1)]:
            turned("Y", ch(name, t, n), ch(name, 0, n), t, 2.3)
            ops[-3]["after"] = window + 4
        turned("Y", part(edges[t][0], 0, V - OWN, edges[t][1]), ("DL", OWN, V), t, 2.4 + 1.6 * (V - OWN) / V)
    later = [("lnH", 0, 4), ("E", 0, V)]
    bias[0] = TUNE["early"]
    dma("G", [(T.dH[0:96], T.lnH[1:4]), (T.dH[96:128], T.lnH[0])], later, [("dH", 0, V)], 5.0)
    ops[-3]["after"] = line[-1]
    dma("Y", [(T.HX[:, V:2 * V], T.lnH[:])], later, [("HX", V, 2 * V)], 3.6)
    turned("Y", ("HX", 0, V), ("HW", 0, V), 1, 4.0, later)
    bias[0] = 0.0
    later += [("HX", 0, 2 * V)]
    dma("Y", [(T.HW[0:64, V:2 * V], T.lnH[2:4]), (T.HW[64:128, V:2 * V], T.lnH[0:2])], later, [("HW", V, 2 * V)], 3.6)
    turned("Y", ("T2A", 0, V), ("DA", 0, V), 3, 4.0, later)
    turned("Y", ("T2B", 0, V), ("DB", 0, V), 3, 4.0, later)

    walk_matrices()
    for k in range(8):
        s_act(ch("THR", k), ch("W1", k), F.Abs, bias=pf("mid"), scale=1.0 / 128)
    halves = [(s, h, slice(64 * h + 32 * s, 64 * h + 32 * s + 32)) for s in range(2) for h in range(2)]
    dma("Y", [(T.stI[:, at, :], ap(ch("IV", 2 * s + h, 64))) for s, h, at in halves], [("IV", 0, 256)], [("stI", 0, 8)], 2.4)
    ops[-3]["after"] = tolls
    dma("Y", [(T.stT[:, at, :], T.THR[0::2, 1024 * (2 * s + h):1024 * (2 * s + h + 1)]) for s, h, at in halves], [("THR", 0, 2 * V)],
        [("stT", 0, 8)], 3.2)
    ops[-3]["after"] = tolls
    for k, nm, dur in ((13, "I", 0.8), (15, "T", 2.8)):
        st, ln = "st" + nm, "ln" + nm
        for n in range(2):
            send(k + n, [(r, T[st][2 * r + n], T[ln][2 * q + n]) for r in others], [(st, 0, 8), ("ZI", 0, 128)],
                 [(ln, 2 * r + n, 2 * r + n + 1) for r in others], dur)
            ops[-3]["after"] = line[-1]
        dma("Y", [(T[ln][2 * q:2 * q + 2], T[st][2 * q:2 * q + 2])], [(st, 0, 8)], [(ln, 2 * q, 2 * q + 2)], 2.4)
    dma("Y", [(ap(ch("INV", x, 64)), T.lnI[x::4]) for x in range(4)], [("lnI", 0, 8)], [("INV", 0, 256)], 2.4)
    for x in range(4):
        dma("Y", [(T.THR[b::2, 1024 * x:1024 * x + 1024], T.lnT[x::4]) for b in range(2)], [("lnT", 0, 8)], [ch("THR", x, 1024)], 3.0)

    cur, steps, listed, terms = [0], [0], [0, 0], [0]
    free = [ch("R", 0), ch("R", 1)]

    def bank(n=512):
        terms[0] += 1
        step = n // 512
        return free[terms[0] % (len(free) // step) * step]

    def make_list(CM, n, t, lo, hi, o, winners):
        o, y = (o[0], o[1], o[1] + (hi - lo) // 16), lst("LX", 128 * (n % 3), lo, hi)
        signed = lo == 0 and n in TUNE["both"]
        if signed:
            pe([(o, ID, ("LIFT", 0, width(o)), True, False)])
        votes(o, CM, lo, hi, not signed)
        v_tt(y, o, lst("BP", 128 * t, lo, hi), A.min)
        if winners:
            v_tt(lst("LY", 0, lo, hi), y, lst("VP", 0, lo, hi), A.max)
            v_ts(lst("LS", 128 * (n % 3), lo, hi), lst("LY", 0, lo, hi), -CUT - lo, A.add)

    def predecessors(n, t):
        z = ch("LZ", t - 2, 128)
        v_tt(z, ch("LX", n % 3, 128), ch("AP", t, 128), A.max)
        v_ts(z, z, V - 1, A.bitwise_and)
        v_cp(ch("LP", 2 * ((n - 1) // 3 % 2) + t - 2, 128), z)
        listed[t - 2] = len(ops) - 1

    def open_window(names):
        for k in (3, 2, 1, 0):
            pe(group(ch("P", k), [(ID, ch(r, k)) for r in names], True, False))

    def close_window(k, name, small=None):
        o = ch("P", k)
        pe(spread(o, 512 * k, 512 * k + 512, small, False, True) if small else group(o, [(ID, ch(name, k))], False, True), acc=True)
        cp("*", ch("W%d" % (1 - cur[0]), k, base=V), o)

    QB = ("Q", 512, 768)

    def gate(n):
        return ch("SG", (n - 1) % 3 if n % 3 else 1 + n // 3, 256)

    def step(n, t, first, marks, PN):
        W, CM = "W%d" % cur[0] if t else "AB", "CM%d" % (steps[0] % 2)
        steps[0] += 1
        fixed = ["E", "DB"] if n in TUNE["apart"] else ["ED"]
        costs = (W, V, 2 * V)
        helped = TUNE["help"][n]
        begin, both = len(ops), BOTH * (n in TUNE["both"])
        for j, (a, b) in enumerate(cut(0, helped, TUNE["aid"])):
            if b <= both and t == 3 and not first:
                cp("S", part("TM", a, b), costs, lst("AB16", 256 * t, a, b))
                continue
            o = ch("P", TUNE["banks"][j % len(TUNE["banks"])] + 2 * (t == 0))
            o = (o[0], o[1], o[1] + b - a)
            fix = [(rot(t), "DL")] if t else [(ID, "DA"), (NID, "DB")]
            pe(group(o, [(l, part(r, a, b)) for l, r in fix], True, False))
            cp("S", part("TM", a, b), costs, lst("AB16", 256 * t, a, b))
            pe(group(o, [(ID, part("TM", a, b))], False, True), acc=True)
            cp("S", part(W, a, b), o)
        f0, f1 = TUNE["fused"][n]
        picked = [x for lo, hi in ((f1, V), (0, f0)) for k in (3, 2, 1, 0) for x in [(max(lo, 512 * k), min(hi, 512 * k + 512))] if x[0] < x[1]]
        NEXT, small = "W%d" % (1 - cur[0]), ("ZC", 0, 128) if t == 3 else marks and ch("ADW", t, 128)
        beside = ("ZB", -f0) if t == 3 else ("FD", FUSED * (t - 1) - f0)

        def fixed_part(o, a, b, last):
            turn = ("N2M", 96, 224) if t == 3 else rot(t)
            mm = group(o, [(turn, part(x, a, b)) for x in fixed], True, last and not small)
            pe(mm + (spread(o, a, b, small, False, last) if small else []))

        if t in (1, 2) or t == 3 and first:
            if t < 3 and not marks and n not in TUNE["apart"]:
                turned("Y", part("FD", f0, f1, beside[1]), ("ED", f0, f1), t, 3.2)
            elif t == 2 and marks and TUNE["fused"][n - 1] == (f0, f1):
                turned("Y", part("FD", f0, f1, beside[1]), part("FD", f0, f1, -f0), 1, 3.2)
            else:
                for j, (a, b) in enumerate(cut(f0, f1, 512)):
                    o, to = ch("P", 3 - j % 2), part(beside[0], a, b, beside[1])
                    o = (o[0], o[1], o[1] + b - a)
                    fixed_part(o, a, b, True)
                    cp("*", to, o, None, 0.5 if t == 3 else 1.0)
            for a, b in picked:
                fixed_part(part("P", a, b), a, b, False)
        if t == 3 and first:
            CZ = "CM%d" % (steps[0] % 2)
            steps[0] += 1
        counted = [0]

        def count(a, b, by):
            counted[0] += b - a
            compact(CZ, a, b, QB, by, first=counted[0] == b - a, last=counted[0] == V)

        def fused(lo, hi):
            for a, b in cut(max(lo, f0), max(lo, min(hi, f1)), TUNE["cmp"]):
                l = lst("LS", 128 * (n % 3), a, b)
                if t < 3:
                    v_tt(part(NEXT, a, b, V), (W, lo, 2 * V), part(beside[0], a, b, beside[1]), A.add, lst=l)
                else:
                    v_tt(part(CZ, a, b), (W, lo, 2 * V), part(beside[0], a, b, beside[1]), A.is_gt, lst=l)
                    count(a, b, "over2")

        def winners(j, lo, hi):
            make_list(CM, n, t, lo, hi, ("Q", 512 * (j % 2 if t < 3 else 0)), True)
            if not t:
                for c, d in cut(lo, hi, TUNE["last"] if lo == 0 else 512):
                    cp("*", part(PN, c, d), (W, lo, 2 * V), lst("LS", 0, c, d), plus=128.0)
                return
            for a, b in picked:
                if lo <= a < hi:
                    o = part("P", a, b)
                    cp("S", part(PN, a, b), (W, lo, 2 * V), lst("LS", 128 * (n % 3), a, b))
                    pe(group(o, [(N2 if t == 3 else ID, part(PN, a, b))], False, True), acc=True)
                    if t < 3:
                        cp("*", part(NEXT, a, b, V), o)
                    else:
                        either(lambda: v_ts(part(CZ, a, b), o, -1.0, A.max, 1.0, A.min), lambda: s_act(part(CZ, a, b), o, F.Sign))
                        count(a, b, "over")
            mine.append((lo, hi))

        vote = ("vote0", 0) if t == 2 else ("vote1", 32 * (t - 1))
        late, mine = [], []
        waiting = []
        for j, (lo, hi) in enumerate(TUNE["pieces"]):
            for a, b in cut(max(lo, helped), max(hi, helped), TUNE["head" if t else "cmp"]):
                v_tt(part(W, a, b), costs, part(edges[t][0], a, b, edges[t][1] - OWN), A.add, lst=lst("AB16", 256 * t, a, b))
                while waiting:
                    winners(*waiting.pop())
            for a, b in cut(max(lo, both), hi, TUNE["cmp" if j or not t else "head"]) + [(0, both)] * (lo < both):
                if b > both:
                    v_tt(part(CM, a, b), costs, part(W, a, b), A.is_lt, lst=lst("AB16", 256 * t + 128, a, b))
                    if n == 0:
                        ops[children]["after"] = len(ops) - 1
                else:
                    o = part("P", a, b, 512 * TUNE["third"])
                    pe(group(o, [(rot(t), part("DL", a, b)), (ID, part("TM", a, b))], True, False))
                    cp("S", part("TM", a, b, helped), costs, lst("AB16", 256 * t + 128, a, b))
                    pe(group(o, [(NID, part("TM", a, b, helped))], False, True), acc=True)
                    s_act(part(CM, a, b), o, F.Sign, bias=-0.5)
                if t == 3 and not first:
                    compact(CM, a, b, QB, *vote, first=b == V, last=a == 0)
                    if a == lo:
                        late.append((lo, hi))
                while waiting and (a == lo or not TUNE["hold"]):
                    winners(*waiting.pop())
            if t < 3 or first:
                waiting.append((j, lo, hi))
        while mine and TUNE["hold"] < 2:
            fused(*mine.pop(0))
        while waiting:
            winners(*waiting.pop())
        while mine:
            fused(*mine.pop(0))
        in_line(begin, "V")
        sg, bar = gate(n), pf("cut2" if both else "cut")
        o = ("Q", 0, 256) if t == 3 and first else QB
        if t in (1, 2) or t == 3 and first:
            for a, b in cut(0, V, TUNE["gates"]):
                compact(CM, a, b, o, *vote, first=b == V, last=a == 0)
        if t in (1, 2):
            cur[0] = 1 - cur[0]
            either(lambda: v_ts(sg, o, bar, A.add, 1.0, A.min), lambda: s_act(sg, o, F.Sign, bias=bar))
        if t == 3:
            mw = ("MW", 0, 256)
            s_act(sg, o, F.Sign, bias=bar)
            if first:
                either(lambda: v_ts(mw, QB, pf("nine"), A.add, 1.0, A.min), lambda: s_act(mw, QB, F.Sign, bias=pf("nine")))
            else:
                for j, (lo, hi) in enumerate(late):
                    make_list(CM, n, t, lo, hi, ("P", 512 * (j % 2)), False)
        if t > 1:
            predecessors(n, t)

    def join_x():
        dma("Y", [(T.XR[:, 0:V], T.dH[:])], [("dH", 0, V)], [("XR", 0, V)], 4.6)
        for a, b in cut(0, V, TUNE["join"]):
            dma("G", [(T.XR[:, a:b], T.YA[:, a:b])], [("YA", a, b)], [("XR", a, b)],
                3.2 + 4.5 * (b - a) / V, accum_op=A.add, max_dma_last_dim=4096)

    slots = [0]

    def next_ex(n):
        if slots[0] + n > SCRATCH["EX"][1][1]:
            slots[0] = 0
        slots[0] += n
        return ("EX", slots[0] - n, slots[0])

    def summed_up(e, lo, first=False):
        to = ("dG", lo, lo + width(e))
        if first:
            dma("Y", [(ap(to), ap(e))], [e], [to], 2.4 + width(e) / 640)
        else:
            dma("G", [(ap(to), ap(e))], [e], [to], 3.2 + width(e) / 400, accum_op=A.add, max_dma_last_dim=2048)

    def term(lo, hi, pairs, off, half, last):
        n = 512 if hi - lo <= 512 else 1024
        o = bank(n)
        o, ab = part(o[0], 0, hi - lo, o[1]), part("AB", 0, hi - lo, n * (terms[0] % (V // n)))
        out = o if last else next_ex(hi - lo)
        for a, b in cut(lo, hi, 512):
            pe(group(part(o[0], a, b, o[1] - lo), [(l, part(r, a, b)) for l, r in pairs]))
        s_act(ab, o, F.Abs, bias=-off)
        s_act(out, ab, F.Exp, bias=math.log(0.5) if half else 0.0, scale=-0.125)
        if last:
            v_tt(("GD", lo, hi), o, ("GD", lo, hi), A.add)
        else:
            summed_up(out, lo)

    walked = [None] * 3

    def walk_back(f):
        found, H = ["YB"] * 4, V // 2
        apart = f % 2 == 0

        def cc(n, x):
            return ch("CC", 4 * n + x, 256)

        def gates(n, x):
            ahead = [(ch("DG", 2 * n + b, 128), gate(3 * f + 4 - b - x)) for b in range(2) if 0 < 4 - b - x < 4]
            ahead += [(ch("DG", 2 * n + 1 - x, 128), ("MW", 0, 256))] if x < 2 else []
            pe(group(("Q", 512 * n, 512 * n + 256), ahead, True, x == 0))

        def marks(n, x):
            s_act(cc(n, x), ("Q", 512 * n, 512 * n + 256), F.Sign, bias=pf("end") if x == 3 else -2.0)

        for n in range(2):
            gates(n, 0)
            marks(n, 0)
        for x in range(4):
            for n in range(2):
                tile = 2 * (x % 2) + n
                o = ("Q", 512 * n * apart, 512 * n * apart + 128)
                if x < 3:
                    gates(n, x + 1)
                else:
                    pe(group(o, [(mat("sum1" if y == 1 else "sum", 32 * (y % 2) + 16 * n + e, 48), part("CC", 128 * e, 128 * e + 128, cc(n, y)[1]))
                                 for y in (1, 2, 3) for e in range(2)], apart or n == 0, False), acc=not (apart or n == 0))
                for a, b in TUNE["walk"]:
                    v_tt(part(found[x], a, b, H * n), cc(n, x), part("THR", a, b, H * tile), A.is_gt, lst=lst("INV", 64 * tile, a, b))
                    for j in range(2):
                        if (x, n, b) == TUNE["lists"][f][j]:
                            ops[-1]["after"] = listed[j]
                    if x < 3:
                        compact(found[x], a, b, ("Q", 512 * n, 512 * n + 256), "on", 64 * (1 - x % 2), first=False, last=a == 0, base=H * n)
                    else:
                        compact(found[x], a, b, o, "out", 16 - 16 * n, 128, first=False, last=a == 0 and n == 1 - apart, base=H * n)
                if x < 3:
                    walked[x] = len(ops) - 1
                    marks(n, x + 1)
                elif apart or n:
                    uw = ch("UW", f if n else 4 + f // 2, 128)
                    if apart and n:
                        pe(group(o, [(ID, ch("UW", 4 + f // 2, 128))], False, True), acc=True)
                    none = pf("none%d" % n if apart else "none")
                    either(lambda: v_ts(uw, o, none, A.add, 0.0, A.is_gt), lambda: s_act(uw, o, F.Sign, bias=none))

    def forest(f, marks):
        first, last = f % 2 == 0, f == 3
        P = "A" if first else "B"
        wide = TUNE["wide"]
        step(3 * f + 1, 1, first, marks, "PN")
        for lo, hi in TUNE["pieces"]:
            for a, b in cut(lo, hi, wide):
                cp("*", part("YA", a, b), ("HX", lo, 2 * V), lst("LS", 128, a, b), 1.0 / 32)
        join_x()
        step(3 * f + 2, 2, first, marks, "PN")
        for a, b in cut(0, V, wide):
            cp("*", part("X", a, b), ("XR", 0, V), lst("LP", 256 * (f % 2), a, b))
        step(3 * f + 3, 3, first, marks, "PN")
        walk_back(f)
        for a, b in cut(0, V, wide)[::-1]:
            l = lst("LP", 128 * (2 * (f % 2) + 1), a, b)
            cp("*", part("T3" + P, a, b), ("HW", V, 2 * V), lst=l)
            cp("*", part("T1" + P, a, b), ("X", 0, V), lst=l)
            cp("V" if f in TUNE["t2"] else "*", part("T2" + P, a, b), part("T1" + P, a, b), plus=HI - 15.5 / 32)
        if last:
            free.extend(ch("P", k) for k in range(4))
            o, win = bank(), ("WIN", 0, 128)
            o = (o[0], o[1], o[1] + 128)
            pe(group(o, [(mat("win" + "AB"[x % 2], e), part("SG", 128 * e, 128 * e + 128, gate(3 * x + 3)[1]))
                         for x in range(4) for e in range(2)]))
            cp("*", win, o, None, 0.125, 0.375)
            for k in range(4):
                o = bank()
                pe(summed(o, k, [], win))
                v_tt(ch("GD", k), o, ch("GD", k), A.mult)
                dma("G", [(ap(ch("GD", k)), ap(ch("dG", k)))], [ch("dG", k)], [ch("GD", k)], 4.6, accum_op=A.add, max_dma_last_dim=2048)
        if first:
            return
        todo = [([(ID, "T3B"), (NID, "T2A")], -HI, False),
                ([(ID, "T3A"), (NID, "T2B")], -HI, True),
                ([(P32, "T1B"), (N32, "T2B"), (NID, "T2A")], -33 * HI, True),
                ([(P32, "T1A"), (N32, "T2A"), (NID, "T2B")], -33 * HI, False)]
        skew = TUNE["skew"] if last else 0.1
        pieces = TUNE["terms"] if last else cut(0, V, TUNE["broad"])[::-1]
        for _, j, p in sorted((j + skew * p, j, p) for j in range(len(todo)) for p in range(len(pieces))):
            term(*pieces[p], *todo[j], last)

    def new_tolls(o, k, small, old, new):
        pe(group(o, [(ID, ch(old, k))], True, False))
        pe(spread(o, 512 * k, 512 * k + 512, small, False, True), acc=True)
        v_ts(ch(new, k), o, 0.0, A.max, 63.0, A.min)

    def tolls_and_edges():
        dma("Y", [(T.ED[:], T.DB[:])], [("DB", 0, V)], [("ED", 0, V)], 3.0)
        dma("G", [(T.ED[:], T.E[:])], [("E", 0, V)], [("ED", 0, V)], 5.0, accum_op=A.add, max_dma_last_dim=4096)

    step(0, 0, True, None, "PN0")
    for k in (1, 0):
        cp("*", ch("DL", k), ch("P", k))
    n = TUNE["ends"]
    for k in range(V // n):
        ea, less = next_ex(n), next_ex(n)
        s_act(ea, ch("T2A", k, n), F.Exp, bias=math.log(3.0), scale=-0.125)
        s_act(ch("GD", k, n), ch("T2B", k, n), F.Exp, scale=-0.125)
        cp("*", less, ea, None, -1.0 / 3)
        summed_up(ea, k * n, True)
        dma("G", [(ap(ch("GD", k, n)), ap(less))], [less], [ch("GD", k, n)], 3.6 + n / 400, accum_op=A.add, max_dma_last_dim=2048)
    for rnd in range(2):
        f = 2 * rnd
        if rnd:
            v_tt(ch("DLT", 0, 128), ch("UW", 0, 128), ch("UW", 1, 128), A.subtract)
            open_window(["PN0", "DB"])
            for k in (3, 2, 1, 0):
                new_tolls(ch("Q", k % 2), k, ch("DLT", 0, 128), "E", "E")
                close_window(k, "E")
            tolls_and_edges()
            dma("Y", [(T.stN[:], T.E[:])], [("E", 0, V)], [("stN", 0, 4)], 3.0)
            exchange(7, "N", 4.4)
            dma("Y", [(T.lnN[q], T.stN[q])], [("stN", 0, 4)], [("lnN", q, q + 1)], 2.4)
            dma("Y", [(T.EN[:], T.lnN[:])], [("lnN", 0, 4)], [("EN", 0, V)], 3.0)
        else:
            open_window(["DB"])
            for k in (3, 2, 1, 0):
                pe(group(ch("P", k), [(ID, ch("E", k))], False, False), acc=True)
                close_window(k, "PN0")
            tolls_and_edges()
        cur[0] = 1 - cur[0]
        forest(f, None)
        send(5 + rnd, [((q - 1) % 4, ap(ch("UW", 4 + rnd, 128)), ap(ch("RU", rnd, 128)))], [ch("UW", 4 + rnd, 128)], [ch("RU", rnd, 128)], 0.6)
        open_window(["PN0", "ED"])
        for t in range(3):
            o = ("Q", 0, 128) if t == 0 else ("Q", 384 + 128 * t, 512 + 128 * t)
            pe(group(o, [(("M1", 32 * t, 32 * t + 128), ch("UW", f, 128)), (("M2", 32 * t, 32 * t + 128), ch("RU", rnd, 128))]))
        cp("*", ("ADW", 0, 128), ("Q", 0, 128))
        cp("*", ("ADW", 128, 384), ("Q", 512, 768))
        for k in (3, 2, 1, 0):
            close_window(k, None, ("ADW", 0, 128))
        cur[0] = 1 - cur[0]
        forest(f + 1, True)

    mine = ch("DLT", 1, 128)
    v_tt(mine, ch("UW", 2, 128), ch("UW", 3, 128), A.subtract)
    told = send(8, [(r, ap(mine), ap(ch("DH", q, 128))) for r in others], [mine], [ch("DH", r, 128) for r in others], 1.1)
    tiles = [mine if r == q else ch("DH", r, 128) for r in range(4)]
    add("T", lambda: [[g.tensor.matmul(T.Q[32 * r:32 * r + 32, 0:128], T.II[:, 32 * q:32 * q + 32], ap(tiles[r]), True, True)
                       for r in range(4)][-1]], tiles + [ID, ("GD", 0, V)], [("Q", 0, 128)], 0.06 + 512 * PCY)
    cp("*", ("DN", 0, 128), ("Q", 0, 128))
    for p, (lo, hi) in enumerate(GAIN):
        st, ln, w = "stG%d" % p, "lnG%d" % p, hi - lo
        staged = dma("Y", [(T[st][:], T.GD[:, lo:hi])], [("GD", lo, hi)], [(st, 0, 4)], 2.4 + 0.8 * w / 512)
        send(17 + p, [(r, T[st][r], T[ln][q]) for r in others], [(st, 0, 4)], [(ln, r, r + 1) for r in others], 2.7 * w / 512)
        ops[-3]["after"] = TUNE["behind"] and told if p == len(GAIN) - 1 else None
    for p, (lo, hi) in enumerate(GAIN):
        st, ln = "stG%d" % p, "lnG%d" % p
        ops[dma("Y", [(T.gain[32 * r:32 * r + 32, lo:hi], T[st if r == q else ln][r]) for r in range(4)],
                [(st, q, q + 1)] + [(ln, r, r + 1) for r in others], [], 2.4 + 0.8 * (hi - lo) / 512)]["after"] = staged
    for k in range(4):
        new_tolls(ch("P", k), k, ("DN", 0, 128), "EN", "W0")
        ops[dma("Y", [(T.tollout[:, 512 * k:512 * k + 512], ap(ch("W0", k)))], [ch("W0", k)], [], 2.5)]["after"] = staged
    return ops


def dependencies(ops):
    log = {}
    for n, o in enumerate(ops):
        deps, order = set(), set()
        touched = []
        for x, w in [(x, x[0] in PSUM) for x in o["rd"]] + [(x, True) for x in o["wr"]]:
            lo, hi = (x[1] // 512 * 512, (x[2] + 511) // 512 * 512) if x[0] in PSUM else (x[1], x[2])
            touched.append((x[0], lo, hi, w))
        for name, lo, hi, w in touched:
            for (a, b, m, mw) in log.get(name, []):
                if a < hi and lo < b and (w or mw) and m != n:
                    if name == "link" or o["acc"] and name in PSUM and ops[m]["eng"] == "T":
                        order.add(m)
                    else:
                        deps.add(m)
        for name, lo, hi, w in touched:
            old = log.get(name, [])
            if w:
                old = [e for e in old if not (lo <= e[0] and e[1] <= hi)]
            log[name] = old + [(lo, hi, n, w)]
        order.update(x for x in (o["after"], o.get("more")) if x is not None)
        o["deps"], o["order"] = deps, order - deps


def greedy(ops, level):
    n = len(ops)
    users = [[] for _ in range(n)]
    for k, o in enumerate(ops):
        for d in o["deps"] | o["order"]:
            users[d].append(k)
    missing = [len(o["deps"] | o["order"]) for o in ops]
    ready, start, where = [0.0] * n, [0.0] * n, [None] * n
    pool = {e: [] for e in QUEUES}
    free = {e: 0.0 for e in pool}

    def engines(k):
        return "VS" if "alt" in ops[k] else ops[k]["eng"]

    def span(k, e):
        return (ops[k]["alt"][e][1],) * 2 if "alt" in ops[k] else (ops[k]["issue"], ops[k]["dur"])

    def soon(k, depth):
        t = ready[k]
        if missing[k]:
            if not depth:
                return 1e9
            for d in ops[k]["deps"] | ops[k]["order"]:
                if where[d] is None:
                    t = max(t, max(soon(d, depth - 1), min(free[x] for x in engines(d))) + ops[d]["dur"] + LAT)
        return t

    for k in range(n):
        if not missing[k]:
            for e in engines(k):
                pool[e].append(k)
    left = n
    while left:
        t, e = min((max(free[e], min(ready[k] for k in pool[e])), e) for e in pool if pool[e])
        now = [k for k in pool[e] if ready[k] <= t + 1e-9]
        own = TUNE["own"]
        k = max(now, key=lambda j: (level[j] + (0.0 if "alt" in ops[j] else own), -j))
        bar = level[k] + TUNE["urgent"]
        near = set(j for j in pool[e] if level[j] > bar)
        rim = set(j for x in pool for j in pool[x] if level[j] > bar)
        for _ in range(TUNE["hops"]):
            rim = set(u for j in rim for u in users[j] if level[u] > bar)
            near |= rim
        due = [soon(j, TUNE["hops"]) for j in near if e in engines(j)]
        due = min([x for x in due if x > t] or [1e9])
        if due < t + span(k, e)[0] * TUNE["share"]:
            fit = [j for j in now if t + span(j, e)[0] * TUNE["share"] <= due]
            if not fit:
                free[e] = min(due, t + 0.1)
                continue
            k = max(fit, key=lambda j: (level[j], -j))
        for x in engines(k):
            pool[x].remove(k)
        issue, dur = span(k, e)
        start[k], where[k], free[e] = t, e, t + issue
        left -= 1
        for u in users[k]:
            ready[u] = max(ready[u], t + dur + (LAT if k in ops[u]["deps"] else 0.0))
            missing[u] -= 1
            if not missing[u]:
                for x in engines(u):
                    pool[x].append(u)
    return start, where


def pack(ops, before, rank, backward):
    n = len(ops)
    after = [[] for _ in range(n)]
    for k in range(n):
        for d in before[k]:
            after[d].append(k)
    missing = [len(b) for b in before]
    ready, start, where = [0.0] * n, [0.0] * n, [None] * n
    busy = {e: [] for e in QUEUES}
    line_up = sorted((rank[k], k) for k in range(n) if not missing[k])
    while line_up:
        k = line_up.pop(0)[1]
        o = ops[k]
        lead = o["dur"] - o["issue"] if backward else 0.0
        best = None
        for e in ("SV" if "alt" in o else o["eng"]):
            t, line = ready[k] + lead, busy[e]
            if "alt" in o:
                o["dur"] = o["issue"] = o["alt"][e][1]
            lo, hi = 0, len(line)
            while lo < hi:
                mid = (lo + hi) // 2
                if line[mid][1] <= t:
                    lo = mid + 1
                else:
                    hi = mid
            while lo < len(line) and line[lo][0] < t + o["issue"] - 1e-9:
                t = max(t, line[lo][1])
                lo += 1
            end = t + o["issue"] + (TUNE["lean"] if e == "V" else 0.0)
            if best is None or end < best[0]:
                best = (end, t, e, lo)
        _, t, e, lo = best
        if "alt" in o:
            o["dur"] = o["issue"] = o["alt"][e][1]
        busy[e].insert(lo, (t, t + o["issue"]))
        start[k], where[k] = t - lead, e
        for u in after[k]:
            gap = LAT if (k in ops[u]["deps"] or u in o["deps"]) else 0.0
            ready[u] = max(ready[u], start[k] + o["dur"] + gap)
            missing[u] -= 1
            if not missing[u]:
                x, lo, hi = (rank[u], u), 0, len(line_up)
                while lo < hi:
                    mid = (lo + hi) // 2
                    if line_up[mid] < x:
                        lo = mid + 1
                    else:
                        hi = mid
                line_up.insert(lo, x)
    return start, where


def refine(ops):
    n = len(ops)
    before = [o["deps"] | o["order"] for o in ops]
    after = [set() for _ in range(n)]
    for k in range(n):
        for d in before[k]:
            after[d].add(k)
    level = [0.0] * n
    for k in range(n - 1, -1, -1):
        level[k] = ops[k]["dur"] + max([level[u] + LAT for u in after[k]] or [0.0])
    rank = [-level[k] - ops[k]["bias"] for k in range(n)]
    state = [TUNE["seed"]]

    def draw():
        state[0] = (state[0] * 1103515245 + 12345) % 2147483648
        return state[0] / 2147483648.0

    start, where = greedy(ops, [-x for x in rank])
    order = [(k, where[k]) for k in sorted(range(n), key=lambda k: (start[k], k))]
    ends = [replay(ops, order, case) for case in CASES]
    best = (sum(ends), order)
    rank = start
    for _ in range(TUNE["passes"]):
        start, where = pack(ops, before, rank, False)
        order = [(k, where[k]) for k in sorted(range(n), key=lambda k: (start[k], k))]
        ends = [replay(ops, order, case) for case in CASES]
        if sum(ends) < best[0]:
            best = (sum(ends), order)
        back, _ = pack(ops, after, [-start[k] - ops[k]["dur"] for k in range(n)], True)
        rank = [-back[k] - ops[k]["dur"] for k in range(n)]
    return polish(ops, best[1], after, draw)


def polish(ops, order, after, draw):
    n = len(ops)
    deps, soft = [list(o["deps"]) for o in ops], [list(o["order"]) for o in ops]
    before, users = [deps[k] + soft[k] for k in range(n)], [list(u) for u in after]
    gaps = [[(u, LAT if k in ops[u]["deps"] else 0.0) for u in users[k]] for k in range(n)]
    factors = [[c[o["cls"]] for o in ops] for c in CASES]
    where, prv, nxt, last = [None] * n, [-1] * n, [-1] * n, {}

    def span(k, e):
        return (ops[k]["alt"][e][1],) * 2 if "alt" in ops[k] else (ops[k]["issue"], ops[k]["dur"])

    def link(p, k, u):
        prv[k], nxt[k] = p, u
        if p >= 0:
            nxt[p] = k
        if u >= 0:
            prv[u] = k

    for k, e in order:
        where[k] = e
        link(last.get(e, -1), k, -1)
        last[e] = k
    issue, dur = [span(k, where[k])[0] for k in range(n)], [span(k, where[k])[1] for k in range(n)]

    def sort(part, inside, waits, led):
        missing, seq = dict(waits), []
        for k in part:
            if prv[k] >= 0 and inside[prv[k]]:
                missing[k] += 1
            elif not missing[k]:
                seq.append(k)
        for k in seq:
            for u in led[k]:
                missing[u] -= 1
                if not missing[u]:
                    seq.append(u)
            u = nxt[k]
            if u >= 0 and inside[u]:
                missing[u] -= 1
                if not missing[u]:
                    seq.append(u)
        return seq

    def heads(seq, c, start, end):
        wake, f = LAT * CASES[c]["w"], factors[c]
        for k in seq:
            p = prv[k]
            t = start[p] + issue[p] * f[p] if p >= 0 else 0.0
            for d in deps[k]:
                if end[d] + wake > t:
                    t = end[d] + wake
            for d in soft[k]:
                if end[d] > t:
                    t = end[d]
            start[k], end[k] = t, t + dur[k] * f[k]

    def tails(seq, rest):
        for k in reversed(seq):
            t = 0.0
            for u, gap in gaps[k]:
                if rest[u] + gap > t:
                    t = rest[u] + gap
            t, u = t + dur[k], nxt[k]
            rest[k] = issue[k] + rest[u] if u >= 0 and issue[k] + rest[u] > t else t

    def value(seq):
        total = 0.0
        for c in range(TUNE["cases"] - 1, -1, -1):
            start, end = [0.0] * n, [0.0] * n
            heads(seq, c, start, end)
            total += CASES[c]["weight"] * (max(end) + TUNE["pull"] * sum(end) / n)
        return total, seq, start, end

    def insert(k, stretch, lines, start, end, rest, hold, wait, lean):
        part, seq = stretch[0], sort(*stretch)
        heads(seq, 0, start, end)
        tails(seq, rest)
        top, ready, tail, best = max(start[j] + rest[j] for j in part), start[k], rest[k] - dur[k], None
        for e in ("VS" if "alt" in ops[k] else ops[k]["eng"]):
            (s, d), (line, first, final) = span(k, e), lines[e]
            a, b = 0, len(line)
            while a < len(line) and start[line[a]] + issue[line[a]] <= ready + 1e-9:
                a += 1
            while b > 0 and rest[line[b - 1]] <= tail + 1e-9:
                b -= 1
            for j in range(min(a, b), max(a, b) + 1):
                p, u = line[j - 1] if j else first, line[j] if j < len(line) else final
                t = max(ready, start[p] + issue[p]) if p >= 0 else ready
                long, late = (max(t + d + tail, t + s + rest[u]), max(0.0, t + s - start[u])) if u >= 0 else (t + d + tail, 0.0)
                cost = 50.0 * max(0.0, long - top) + hold * late + wait * (t - ready) + 0.01 * draw() + lean * s * (e == "V")
                if best is None or cost < best[0]:
                    best = (cost, e, j, p, u)
        _, e, j, p, u = best
        lines[e][0].insert(j, k)
        where[k] = e
        issue[k], dur[k] = span(k, e)
        link(p, k, u)

    now, rest = value([k for k, _ in order]), [0.0] * n
    tails(now[1], rest)
    for _ in range(TUNE["moves"]):
        seq, start = now[1], now[2]
        t, wide = draw() * max(start), TUNE["span"] * (0.3 + draw())
        lo, hi, queues = t - 2.0, t + wide + TUNE["reach"], ("VS", "ST", "VST", "T", "S", "VSTGYD", "GYXD")[int(draw() * 7)]
        inside = [lo <= x < hi for x in start]
        part = [k for k in seq if inside[k]]
        pick = [k for k in part if t <= start[k] < t + wide and where[k] in queues]
        while len(pick) > TUNE["batch"]:
            pick.pop(int(draw() * len(pick)))
        lines = {e: [k for k in part if where[k] == e] for e in QUEUES}
        if not pick or not lines["V"] or not lines["S"]:
            continue
        lines = {e: (line, prv[line[0]], nxt[line[-1]]) for e, line in lines.items() if line}
        saved = (list(prv), list(nxt), list(where), list(issue), list(dur))
        for k in pick:
            lines[where[k]][0].remove(k)
            if prv[k] >= 0:
                nxt[prv[k]] = nxt[k]
            if nxt[k] >= 0:
                prv[nxt[k]] = prv[k]
            prv[k] = nxt[k] = -1
        weights = (3.0 * draw() ** 2, 0.3 * draw() ** 3 - 0.02, draw())
        key = start if draw() < 0.5 else [-x for x in rest]
        pick.sort(key=lambda k: key[k] + 2.0 * draw())
        work = (list(start), list(now[3]), list(rest))
        stretch = (part, inside, {k: sum(inside[d] for d in before[k]) for k in part},
                   {k: [u for u in users[k] if inside[u]] for k in part})
        for k in pick:
            insert(k, stretch, lines, *work, *weights)
        new = value([k for k in seq if start[k] < lo] + sort(*stretch) + [k for k in seq if start[k] >= hi])
        if new[0] <= now[0] and len(new[1]) == n:
            now = new
            tails(now[1], rest)
        else:
            prv[:], nxt[:], where[:], issue[:], dur[:] = saved
    return [(k, where[k]) for k in now[1]]


def replay(ops, order, case):
    free, end, wake, last = {}, [0.0] * len(ops), LAT * case["w"], 0.0
    for k, e in order:
        o = ops[k]
        t = free.get(e, 0.0)
        for d in o["deps"]:
            if end[d] + wake > t:
                t = end[d] + wake
        for d in o["order"]:
            if end[d] > t:
                t = end[d]
        f = case[o["cls"]]
        issue, dur = (o["alt"][e][1],) * 2 if "alt" in o else (o["issue"], o["dur"])
        free[e] = t + issue * f
        end[k] = t + dur * f
        if end[k] > last:
            last = end[k]
    return last * case["weight"]


def emit(g, T, ops, order):
    queue = {"V": g.vector, "S": g.scalar, "T": g.tensor, "G": g, "Y": g.sync}
    total, seen = {"sent": 0}, {}
    for k, e in order:
        o = ops[k]
        if o["kind"] == "x":
            o["done"] = (o["sem"], o["count"])
            total[o["sem"]] = o["count"]
            continue
        if "alt" in o:
            o["fn"] = o["alt"][e][0]
        need = {}
        for d in o["deps"]:
            s, c = ops[d]["done"]
            need[s] = max(need.get(s, 0), c)
        for s, c in need.items():
            if seen.get((e, s), 0) < c:
                queue[e].wait_ge(T.sem[s], c)
                seen[(e, s)] = c
        made = o["fn"]()
        if o["kind"] == "r":
            total["sent"] += o["count"]
            continue
        if o["kind"] == "d":
            s, step = o["sem"], 16
        else:
            s, step = "e" + e, 1
        for ins in made:
            ins.then_inc(T.sem[s], step)
            total[s] = total.get(s, 0) + step
        o["done"] = (s, total[s])
    for s, c in total.items():
        if seen.get(("G", s), 0) < c:
            g.wait_ge(T.sem[s], c)


def rank_program(g, core, T, topo):
    if T.rank_of(core) is None:
        return
    ops = build(g, core, T, topo)
    dependencies(ops)
    key = str(TUNE)
    if key not in ORDER:
        ORDER[key] = refine(ops)
    emit(g, T, ops, ORDER[key])
